import numpy as np, ml_dtypes
CORES = [3,11,19,27,35,43,51,59]
N = 8
BF = ml_dtypes.bfloat16
Q, B, H, L, CAP, TR, ST, LN = 4096, 2048, 2048, 256, 32, 4, 2, 3
def code(rng, r):
    m = rng.integers(0, 2, (r, 16)); m[0] = 1
    return (((np.arange(2 ** r)[:, None] >> np.arange(r)) & 1) @ m) & 1
def lay(rng, cb, n, noise, wild):
    v = 63 * cb[rng.integers(0, len(cb), n)].T
    v = np.abs(v - rng.integers(1, 4, (16, n)) * (rng.random((16, n)) < noise))
    return np.where(rng.random((1, n)) < wild, rng.integers(0, 64, (16, n)), v)
def coefs(rng):
    co = rng.integers(1, 256, (N, 8, 16, 3)); co[..., 2] = co[0, ..., 2].copy()
    return co
def home(v, c):
    s = np.add.reduce(c[:, None] * (v >> 2), axis=0)
    return s & (N - 1), (s >> LN) & (H - 1)
def store(p, g, v, words, at=None):
    d, h = home(v if at is None else at, p["co"][0, g, :, 2])
    for j in range(v.shape[1]):
        p["xst"][d[j], g, :, h[j]] = v[:, j]; p["vst"][d[j], g, h[j]] = words[j]
def fill(u):
    c = np.zeros(16, np.int64)
    for i in range(6):
        c[i] = min(255, u); u = u - int(c[i])
    return c
def parts(rng, co, noise, wild):
    p = dict(co=co, gen=np.zeros((N, 8, 16, Q), np.int64), hlp=rng.integers(0, Q, (N, 8, 16, B)), xl=np.zeros((N, 8, 16, L), np.int64), wl=rng.integers(0, Q, (N, 8, L)), vst=rng.integers(0, Q, (N, 8, H)), cb=[])
    p["xst"] = np.where(rng.random((N, 8, 1, H)) < 0.1, rng.integers(0, 256, (N, 8, 16, H)), 255)
    for g in range(8):
        cb = code(rng, int(rng.integers(5, 9))); p["cb"].append(cb)
        for a in range(N):
            p["gen"][a, g] = lay(rng, cb, Q, noise, wild); p["xl"][a, g] = lay(rng, cb, L, noise, 4 * wild)
        v = lay(rng, cb, len(cb), noise, 0.0); store(p, g, v, rng.integers(0, Q, len(cb)))
    return p
def pack(p):
    def b(a, n): return np.ascontiguousarray(a.reshape(N, 128, n)).astype(np.float32).astype(BF)
    return {"gen": b(p["gen"], Q), "hlp": np.ascontiguousarray(p["hlp"].reshape(N, 128, B)).astype(np.int32), "xl": b(p["xl"], L), "wl": p["wl"].astype(np.int32),
            "xst": b(p["xst"], H), "vst": p["vst"].astype(np.int32), "co": b(p["co"], 3)}
def setup_inputs(rng):
    return pack(parts(rng, coefs(rng), 0.008, 0.02))
def setup_inputs_spread(rng):
    co = coefs(rng); co[..., 0] = np.minimum(np.exp2(8 * rng.random((N, 8, 16))).astype(np.int64), 255)
    p = parts(rng, co, 0.02, 0.02)
    for g in range(1, 8, 2):
        p["gen"][:, g] = np.minimum((np.exp2(1 + 5 * rng.random((N, 1, Q))) * 2 * rng.random((N, 16, Q))).astype(np.int64), 63)
        p["xl"][:, g] = np.minimum((np.exp2(1 + 5 * rng.random((N, 1, L))) * 2 * rng.random((N, 16, L))).astype(np.int64), 63)
        p["xst"][:, g] = np.where(rng.random((N, 1, H)) < 0.5, (256 * rng.random((N, 16, H)) ** 3).astype(np.int64), p["xst"][:, g])
    p["hlp"][:, ::2] = (Q * rng.random((N, 4, 16, B)) ** 3).astype(np.int64)
    p["wl"] = (Q * rng.random((N, 8, L)) ** 2).astype(np.int64)
    return pack(p)
def setup_inputs_ends(rng):
    co = 255 * rng.integers(0, 2, (N, 8, 16, 3)); mid = rng.integers(1, 256, co.shape); half = rng.random(co.shape) < 0.5
    co[:, 0::4] = np.where(half, mid, co)[:, 0::4]; co[:, 3::4] = 255
    co[:, 2, :, 0] = 0; co[:, 2, 15, 0] = 255; co[:, 5, :, 0] = 0; co[:, 5, :, 2] = 255; co[..., 2] = co[0, ..., 2].copy()
    p = parts(rng, co, 0.0, 0.0)
    def e(hi, sh): return np.where(rng.random(sh) < 0.7, hi * rng.integers(0, 2, sh), rng.integers(0, hi + 1, sh))
    p["hlp"] = e(Q - 1, (N, 8, 16, B)); p["wl"] = e(Q - 1, (N, 8, L)); p["vst"] = e(Q - 1, (N, 8, H))
    xs = p["xst"]; p["xst"] = np.where((xs == 0) | (xs == 63) | (xs == 255), xs, 255 * rng.integers(0, 2, xs.shape))
    bb = (255 * 15 * 16) & (B - 1)
    for a in range(N):
        for g in range(8):
            G = p["gen"][a, g]
            if g % 4 == 3:
                G[:, 0] = 0; G[:, Q - 1] = 63; G[:, Q - 2] = 63; G[:, 1] = 0; G[15, 1] = 1; G[:, Q - 3] = G[:, 1]
                h = np.zeros(16, np.int64)
                if a % 2 == 1: h[9] = Q - 3; h[15] = 1
                else: h[6] = Q - 2; h[15] = Q - 1
                p["hlp"][a, g, :, bb] = h
                pick = rng.random(L) < 0.15; pick[0] = True; pick[3] = True; pick[L - 1] = True
                p["xl"][a, g][:, pick] = 63
            elif g % 4 == 0: G[:, 0] = 63; G[:, Q - 1] = 0
            else: G[:, 0] = 63 * p["cb"][g][int(rng.integers(1, len(p["cb"][g])))]; G[:, Q - 1] = G[:, 0]
    p["hlp"][:, 7, :, B - 1] = Q - 1; p["hlp"][:, 7, :, B - 2] = 0
    v = np.full(16, 63); v[15] = 0
    p["xl"][:, 5] = v[:, None]; store(p, 5, v[:, None], [Q - 1])
    p["wl"][:, 5, 0] = Q - 1; p["wl"][:, 5, 1] = 0
    return pack(p)
def setup_inputs_corners(rng):
    co = coefs(rng)
    for g in range(0, 8, 2):
        co[:, g, :, 0] = 0; co[:, g, :, 2] = N * rng.integers(1, 31, 16); co[:, g, 0, 2] = 1
        co[:, g + 1, :, 0] = 255 * rng.integers(0, 2, (N, 16))
    p = parts(rng, co, 0.008, 0.02)
    p["wl"] = np.where(rng.random((N, 8, L)) < 0.3, (Q - 1) * rng.integers(0, 2, (N, 8, L)), p["wl"])
    p["xst"][:, 3] = 255
    for a in range(N): p["xst"][a, 1] = lay(rng, p["cb"][1], H, 0.008, 0.02)
    for g in range(0, 8, 2):
        for a in range(N):
            if g == 2: to = [(a + 1) % N] * L
            elif g == 6: to = [N - 1] * L
            else: to = [(a + 1) % N] * CAP + [(a + 2) % N] * (CAP + 1) + [(a + 3) % N] * (CAP - 1) + [(a + 4) % N] + [a] * (L - 3 * CAP - 1)
            p["xl"][a, g, 0] = 4 * rng.permutation(np.array(to)) + rng.integers(0, 4, L)
            ls = rng.permutation(L)[:60]; its = p["xl"][a, g][:, ls]
            far = (its == 63) & (rng.random((1, 60)) < 0.3); far[0] = False
            store(p, g, np.where(far, 255, its), np.where(rng.random(60) < 0.5, p["wl"][a, g, ls], rng.integers(0, Q, 60)), its)
    return pack(p)
def setup_inputs_crowd(rng):
    co = coefs(rng); co[:, 3:, :, 0] = 0; co[:, 1, :, 0] = 0
    v = np.full(16, 21); v[:6] = 63; v[11] = 5; v[12] = 0; v[13] = 1
    u, rem = divmod(N * H - 1, 15); c = fill(u); c[13] = (-u) & (N - 1); c[15] = 1; v[15] = 4 * rem + 1; co[:, 3:, :, 2] = c
    u, rem = divmod(B - 1, 15); c = fill(u); c[11] = rem
    co[:, 4, :, 1] = c; co[:, 7, :, 1] = c
    gw = v.copy(); gw[12] = 63; aft = (63 - np.abs(v - gw))[:, None]
    p = parts(rng, co, 0.008, 0.02)
    for g, far in ((3, 0), (4, 1), (5, 7), (6, 7), (7, 5)):
        w0 = int(rng.integers(0, Q)); word = w0 ^ 1
        if g == 4: w0, word = Q - 9, Q - 7
        if g == 7: w0, word = Q - 7, Q - 9
        p["gen"][:, g, :, w0] = gw; p["xl"][:, g] = v[:, None]; p["wl"][:, g] = w0
        store(p, g, v[:, None], [word]); s = aft.copy(); s[3, 0] = 63 - far
        if g == 3: s[12, 0] = 255
        store(p, g, s, [int(rng.integers(0, Q))], aft)
        if g in (3, 5, 6): p["xl"][int(rng.integers(0, N)), g, 14, CAP - 1] = 22
    for g in (0, 1, 2):
        cb = p["cb"][g]; few = 63 * cb[rng.integers(1, len(cb), 4)].T
        if g == 0: p["xl"][:, g] = few[:, rng.integers(0, 4, (N, L))].transpose(1, 0, 2)
        else:
            p["xl"][:, g] = few[:, :1]
            if g == 2:
                for a in range(N): p["xl"][a, g, :, int(rng.integers(0, L))] = rng.integers(0, 64, 16)
            else: store(p, g, np.full((16, 1), 255), [0], few[:, :1])
    for a in range(N):
        it = rng.integers(1, 64, 16); bb = int(np.add.reduce(co[a, 0, :, 1] * (it >> 2))) & (B - 1)
        p["gen"][a, 0, :, Q - 9] = it; p["hlp"][a, 0, 0, bb] = Q - 9
        ls = np.array([0, 9, L - 1]); p["xl"][a, 0][:, ls] = it[:, None]; p["wl"][a, 0, ls] = Q - 7
    return pack(p)
def check_inputs(d):
    bad = []
    for k, lo, hi in (("gen", 0, 63), ("hlp", 0, Q - 1), ("xl", 0, 63), ("wl", 0, Q - 1), ("xst", 0, 255), ("vst", 0, Q - 1), ("co", 0, 255)):
        a = np.asarray(d[k]).astype(np.float64)
        if not (np.all(a >= lo) and np.all(a <= hi)): bad.append("range of " + k)
        elif np.any(a != np.floor(a)): bad.append("whole numbers in " + k)
    c = np.asarray(d["co"]).astype(np.float64)[..., 2]
    if np.any(c != c[:1]): bad.append("column 2 of co alike on all ranks")
    return bad
def reference(gen, hlp, xl, wl, xst, vst, co):
    G = gen.astype(np.float32).astype(np.int32).reshape(N, 8, 16, Q); S = hlp.astype(np.int32).reshape(N, 8, 16, B)
    x = xl.astype(np.float32).astype(np.int32).reshape(N, 8, 16, L); W = wl.astype(np.int32)
    X = xst.astype(np.float32).astype(np.int32).reshape(N, 8, 16, H); V = vst.astype(np.int32)
    cc = co.astype(np.float32).astype(np.int32).reshape(N, 8, 16, 3); cw, ca, cp = cc[..., 0:1], cc[..., 1:2], cc[..., 2:3]
    A = np.zeros((N, 8), np.int64)
    for t in range(TR):
        for step in range(ST):
            b = np.add.reduce(ca * (x >> 2), axis=2) & (B - 1)
            hs = np.take_along_axis(S, b[:, :, None, :], 3)
            y = np.take_along_axis(G, hs.reshape(N, 8, 1, 16 * L), 3).reshape(N, 8, 16, 16, L)
            y = np.abs(x[:, :, :, None, :] - y)
            sc = np.add.reduce(cw[..., None] * y, axis=2)
            k = np.argmin(sc, axis=2)
            go = np.min(sc, axis=2) < np.add.reduce(cw * x, axis=2)
            yk = np.take_along_axis(y, k[:, :, None, None, :], 3)[:, :, :, 0]
            s = np.take_along_axis(hs, k[:, :, None, :], 2)[:, :, 0]
            x = np.where(go[:, :, None], yk, x)
            W = np.where(go, ((W * s >> 5) + W + 37 * s) & (Q - 1), W)
        f = np.add.reduce(cp * (x >> 2), axis=2); to = f & (N - 1); pl = (f >> LN) & (H - 1)
        ret = np.full((N, 8, L), -1, np.int32)
        for d in range(N):
            m = to == d; sent = m & (np.add.accumulate(m.astype(np.int32), axis=2) <= CAP)
            dist = np.add.reduce(np.abs(np.take_along_axis(X[d][None], pl[:, :, None, :], 3) - x), axis=2)
            kn = sent & (dist <= (A[d] & 7)[None, :, None]); un = sent & ~kn
            ret = np.where(kn, np.take_along_axis(V[d][None], pl, 2), ret)
            A[d] = np.count_nonzero(kn, axis=(0, 2))
            for g in range(8):
                aa, ll = np.nonzero(un[:, g])
                u, first = np.unique(pl[aa, g, ll], return_index=True); aa, ll = aa[first], ll[first]
                X[d, g][:, u] = x[aa, g, :, ll].T; V[d, g, u] = W[aa, g, ll]
        up = (ret >= 0) & (ret != W); new = ((ret * W >> 5) + ret + W) & (Q - 1)
        for r in range(N):
            for g in range(8):
                ll = np.nonzero(up[r, g])[0]
                u, first = np.unique(b[r, g, ll], return_index=True); ll = ll[first]
                S[r, g, (ll + t) & 15, u] = new[r, g, ll]
        x = 63 - np.abs(x - np.take_along_axis(G, W[:, :, None, :], 3))
    sh = np.add.reduce(S * np.arange(1, 17, dtype=np.int32)[:, None], axis=2)
    return {"yx": x.reshape(N, 128, L).astype(np.float32).astype(BF), "yw": W.astype(np.float32), "ys": X.reshape(N, 128, H).astype(np.float32).astype(BF),
            "yv": V.astype(np.float32), "yh": sh.astype(np.float32)}

@@ -1,0 +1,692 @@
+from concourse.bass import DstId, RemoteDMATransfer
+from concourse.mybir import AluOpType as OP, ActivationFunctionType as AF
+
+N, Q, B, H, L, CAP, TR = 8, 4096, 2048, 2048, 256, 32, 4
+BIG = 1.0e8
+MAGIC = 1.5 * 2.0 ** 26
+PIECES = [(128, 32, "a"), (160, 32, "v"), (192, 32, "v"), (224, 32, "v"),
+          (0, 32, "v"), (32, 32, "v"), (64, 32, "v"), (96, 16, "v"), (112, 16, "v")]
+
+SCRATCH = {}
+PART = {}
+
+
+def _decl(where, dtype, spec):
+    for item in spec.split():
+        name, cols = item.split(":")
+        if int(cols) == 16:
+            pool = "POOL_" + dtype
+            used = SCRATCH[pool][1][1] if pool in SCRATCH else 0
+            SCRATCH[pool] = (where, [128, used + 16], dtype)
+            PART[name] = (pool, used, 16)
+        else:
+            SCRATCH[name] = (where, [128, int(cols)], dtype)
+            PART[name] = (name, 0, int(cols))
+
+
+_decl("sbuf", "bfloat16", "GN:4096 XT:2304 X0:256 X1:256 X2:256 QA:256 QB:256 QC:256 CO:8 AB:8192 DD:2048 GG:2048 NE:2048 XTR:128 "
+      "BM:144 LA:144 LC:144 LW:144 LD:144 BO:128 BC:128 BN:128 ID:128 THL:128 KP:256 DM:256 ONE:256 C192:2 OH:32 OH1:256 OH2:256 "
+      "OW:256 CN:256 VL:256 C33:256 SB:544 WS:544 AW:256 R2:2176 RQ:1024 QQ:256 DQ:256 AQ:256 KN:256 VD:256 EE:2176 DC:256 JD:256 HB:512 "
+      "VT:2304 VH:256 VG:256 HD:256 LO:256 WP:256 RG:256 RW:256 LR:144 L0:144 MX:768 MB:256")
+_decl("sbuf", "float32", "SF:2304 YV:2304 YH:2304 IO:2048 IN:272 NM:272 D0:256 ND:256 RS:256 TRI:1024 ROT:384 KW:128 BMF:144 BOF:128 "
+      "COL:32 COF:4 U16:16 BASE:16 U512:16 U2048:16 SC:256 OWN:16 F1:16 F2:16 F3:16 F4:16 F5:16 F6:16 F7:16 F8:16 F9:16 TF:256 SEL1:256 SEL2:256 "
+      "WB:32 WT:32 WC:256 CC:256 CDS:256 CDO:256 KY:16 KO:16 HM:256 ZD:256 EV:16 PA:16 YC:256")
+_decl("sbuf", "int32", "SI:2048 VI:128 VJ:256 WI:256 IP:8 I1:16 I2:16 I3:16 I4:16 I5:16 I6:16 AK1:16 AK2:16 BI:16 HI:16 ZI:16 WN:16 WH:16 WL:16")
+_decl("sbuf", "uint16", "HS:256 BOF1:16 BP1:16 BP2:16 BT:16 OFX:16 A1:16 A2:16 OFQ:16 HOF:16 OFS:16 OFH:16 WU:16 EXP:16 C16S:256 C16O:256")
+_decl("psum", "float32", "P0:512 P1:512 P2:512 P3:512 P4:512 P5:512 P6:512")
+_decl("psum", "bfloat16", "PT:1024")
+
+SEMAPHORES = (["sv", "sa", "st", "sg"] + ["d%d" % i for i in range(32)] + ["ls%d" % i for i in range(2 * TR)]
+              + ["ar%d" % i for i in range(2 * TR)] + ["ha%d" % i for i in range(2 * TR)])
+
+
+def _mask(engines):
+    m = 0
+    for e in engines:
+        m |= 1 << e
+    return m
+
+
+def share(engines, i, n):
+    return engines[i * len(engines) // n:(i + 1) * len(engines) // n]
+
+
+def routes(T, topo, r):
+    core = T.cores[r]
+    rest = [d for d in range(N) if d != r]
+    pairs = []
+    i = 0
+    while len(pairs) < 2:
+        if rest[i + 1] == rest[i] + 1:
+            pairs.append((rest[i], rest[i + 1]))
+            i += 2
+        else:
+            i += 1
+    direct = [d for d in rest if d not in pairs[0] and d not in pairs[1]]
+    cands = [c for c in topo.cores_of(core) if T.rank_of(c) is None]
+    cands.sort(key=lambda c: topo.die(c) != topo.die(core))
+    helpers = []
+    for p in pairs:
+        helpers.append([c for c in cands if c not in helpers and all(topo.may_write(c, T.cores[d]) for d in p)][0])
+    return pairs, helpers, direct
+
+
+def arrivals(T, topo, d):
+    n = 0
+    for r in range(N):
+        if r != d:
+            pairs, helpers, direct = routes(T, topo, r)
+            src = T.cores[r] if d in direct else helpers[0 if d in pairs[0] else 1]
+            e = len(topo.engines(src, T.cores[d]))
+            n += e if d == direct[2] else e // 2
+    return n
+
+
+def landing(T, x, src):
+    t = x // 2
+    if x % 2 == 0:
+        return T.RQ[:, 256 * t + 32 * src:256 * t + 32 * src + 32]
+    return T.R2[:, 544 * t + 32 * src:544 * t + 32 * src + 32]
+
+
+def transfer(topo, dst, engines, sem, src_ap, dst_ap):
+    rid, pid, _ = topo.addr(dst)
+    return RemoteDMATransfer(dst_ids=[DstId(rid=rid, pnc=pid)], dma_engine_mask=_mask(engines), remote_sem=sem, src=src_ap, dst=dst_ap)
+
+
+def helper_program(g, core, T, topo, r, pair):
+    got = len(topo.engines(T.cores[r], core)) // 2
+    n = 0
+    for x in range(2 * TR):
+        g.wait_ge(T.sem["ha%d" % x], got)
+        trs = []
+        for i, d in enumerate(pair):
+            es = share(topo.engines(core, T.cores[d]), i, 2)
+            n += len(es)
+            s = T.HB[:, 64 * x + 32 * i:64 * x + 32 * i + 32]
+            trs.append(transfer(topo, T.cores[d], es, T.sem["ar%d" % x], s, landing(T, x, r)))
+        g.remote_dma_fused(trs, local_sem=T.sem["ls0"])
+    g.wait_ge(T.sem["ls0"], n)
+
+
+def rank_program(g, core, T, topo):
+    rank = T.rank_of(core)
+    if rank is None:
+        for r in range(N):
+            if core in topo.cores_of(T.cores[r]):
+                pairs, helpers, direct = routes(T, topo, r)
+                if core in helpers:
+                    helper_program(g, core, T, topo, r, pairs[helpers.index(core)])
+        return
+
+    eng = {"v": g.vector, "a": g.scalar, "t": g.tensor, "g": g, "s": g.sync}
+    known = {e: {} for e in eng}
+    count = {"sv": 0, "sa": 0, "st": 0, "sg": 0}
+    recs = {}
+    ndma = [0]
+    nrep = [0]
+
+    def need(e, toks):
+        best = {}
+        for tk in toks:
+            if tk[0] not in best or best[tk[0]][1] < tk[1]:
+                best[tk[0]] = tk
+        for tk in sorted(best.values(), key=lambda k: -len(k[2])):
+            if known[e].get(tk[0], 0) < tk[1]:
+                eng[e].wait_ge(T.sem[tk[0]], tk[1])
+                known[e][tk[0]] = tk[1]
+                for s, val in tk[2].items():
+                    if known[e].get(s, 0) < val:
+                        known[e][s] = val
+
+    def deps(e, reads, writes, tag=None):
+        toks = []
+        for spans, w in ((reads, False), (writes, True)):
+            for (nm, lo, hi) in spans:
+                ps = SCRATCH[nm][0] == "psum"
+                for (l2, h2, w2, e2, tk, tg) in recs.get(nm, []):
+                    if tag is not None and tg == tag:
+                        continue
+                    if ps and e2 != e:
+                        toks.append(tk)
+                    elif e == "t" and e2 == "t":
+                        continue
+                    elif l2 < hi and lo < h2 and (w or w2):
+                        toks.append(tk)
+        return toks
+
+    def note(e, reads, writes, tk, tag=None):
+        for (nm, lo, hi) in writes:
+            recs[nm] = [x for x in recs.get(nm, []) if not (lo <= x[0] and x[1] <= hi) or (tag is not None and x[5] == tag)] + [(lo, hi, True, e, tk, tag)]
+        for (nm, lo, hi) in reads:
+            recs[nm] = [x for x in recs.get(nm, []) if not (x[3] == e and not x[2] and lo <= x[0] and x[1] <= hi)] + [(lo, hi, False, e, tk, None)]
+
+    def A(nm, lo=0, hi=None, st=1):
+        nm, base, cols = PART[nm]
+        lo, hi = base + lo, base + (cols if hi is None else hi)
+        return (T[nm][:, lo:hi:st] if st != 1 else T[nm][:, lo:hi], (nm, lo, hi), [])
+
+    def IX(win, off):
+        return (win[0].indirect(off[0]), win[1], [off[1]])
+
+    def col(j):
+        return A("COL", j, j + 1)
+
+    def emit(e, out, ins, fn, tag=None):
+        aps = [x for x in ins if isinstance(x, tuple)]
+        reads = [x[1] for x in aps] + [y for x in aps for y in x[2]] + out[2]
+        need(e, deps(e, reads, [out[1]], tag))
+        s = "s" + e
+        count[s] += 1
+        fn(*[x[0] if isinstance(x, tuple) else x for x in [out] + ins]).then_inc(T.sem[s], 1)
+        note(e, reads, [out[1]], (s, count[s], dict(known[e])), tag)
+
+    def cp(out, a):
+        emit("v", out, [a], g.vector.tensor_copy)
+
+    def tt(out, a, b, op):
+        emit("v", out, [a, b, op], g.vector.tensor_tensor)
+
+    def ts(out, a, s1, op0, s2=None, op1=None):
+        emit("v", out, [a, s1, s2, op0] + ([op1] if op1 is not None else []), g.vector.tensor_scalar)
+
+    def scan(out, d0, d1, init, op0, op1):
+        emit("v", out, [d0, d1, init, op0, op1], g.vector.tensor_tensor_scan)
+
+    def mset(out, c):
+        emit("v", out, [c], g.vector.memset)
+
+    def act(out, a, f=AF.Identity, scale=1.0, bias=0.0):
+        if scale == 1.0 and bias == 0.0:
+            emit("a", out, [a], lambda o, i: g.scalar.activation(o, i, f))
+        else:
+            emit("a", out, [a], lambda o, i: g.scalar.activation(o, i, f, bias=bias, scale=scale))
+
+    def iota(out, pat, base=0, cm=0):
+        if SCRATCH[out[1][0]][2] == "int32":
+            emit("g", out, [], lambda o: g.iota(o, pat, base, cm))
+        else:
+            emit("g", out, [], lambda o: g.iota(o, pat, base, cm, allow_small_or_imprecise_dtypes=True))
+
+    def mm(items, tr=False):
+        count["st"] += 1
+        done = []
+        for it in items:
+            reads = [it[1][1], it[2][1]]
+            need("t", deps("t", reads, [it[0][1]]))
+            if tr:
+                ins = g.tensor.transpose(it[0][0], it[1][0], it[2][0])
+            else:
+                ins = g.tensor.matmul(it[0][0], it[1][0], it[2][0], it[3], it[4])
+            done.append((reads, it[0][1]))
+        ins.then_inc(T.sem.st, 1)
+        tk = ("st", count["st"], dict(known["t"]))
+        for reads, w in done:
+            note("t", reads, [w], tk)
+
+    def dma(e, out_ap, in_ap, reads, writes):
+        need(e, deps("d", reads, writes))
+        s = "d%d" % ndma[0]
+        ndma[0] += 1
+        eng[e].dma_start(out_ap, in_ap).then_inc(T.sem[s], 16)
+        count[s] = 16
+        tk = (s, 16, dict(known[e]))
+        note("d", reads, writes, tk)
+        return tk
+
+    def conv(out, lw, src, strided, rot=0):
+        mm([(out, A(lw, 15 - (j + rot) % 16, 143 - (j + rot) % 16), A(src, j, 256, 16) if strided else A(src, 16 * j, 16 * j + 16), j == 0, j == 15)
+            for j in range(16)])
+
+    def xrep(x, e, k0, k1, new=False):
+        if new:
+            nrep[0] += 1
+        for k in range(k0, k1):
+            o, i = A("AB", Q + k, Q + 2048, 16), A(x, 0, 128)
+            if e == "v":
+                emit(e, o, [i], g.vector.tensor_copy, nrep[0])
+            elif e == "a":
+                emit(e, o, [i], lambda o, i: g.scalar.activation(o, i, AF.Copy), nrep[0])
+            else:
+                emit(e, o, [i], lambda o, i: g.affine_select(o, i, [[0, 128]], OP.is_ge, 0.0, 0, 0), nrep[0])
+
+    def fill(nm, lo, hi, c):
+        while lo < hi:
+            n = min(272, hi - lo)
+            act(A(nm, lo, lo + n), A("IN", 0, n), scale=0.0, bias=c)
+            lo += n
+
+    pairs, helpers, direct = routes(T, topo, rank)
+    narr = arrivals(T, topo, rank)
+
+    def exchange(x):
+        t = x // 2
+        nm, w = "SB" if x % 2 == 0 else "AW", 32
+        need("g", deps("r", [(nm, 0, 256)], []))
+        ls = T.sem["ls%d" % x]
+        trs = []
+        n = 0
+        for i, h in enumerate(helpers):
+            es = share(topo.engines(core, h), i, 2)
+            n += len(es)
+            d = pairs[i][0]
+            trs.append(transfer(topo, h, es, T.sem["ha%d" % x], T[nm][:, w * d:w * d + 2 * w], T.HB[:, 64 * x:64 * x + 64]))
+        g.remote_dma_fused(trs, local_sem=ls)
+        for part in (direct[:2], direct[2:]):
+            trs = []
+            for i, d in enumerate(part):
+                es = share(topo.engines(core, T.cores[d]), i, len(part))
+                n += len(es)
+                trs.append(transfer(topo, T.cores[d], es, T.sem["ar%d" % x], T[nm][:, w * d:w * d + w], landing(T, x, rank)))
+            g.remote_dma_fused(trs, local_sem=ls)
+        count["ls%d" % x] = n
+        count["ar%d" % x] = narr
+        note("r", [(nm, 0, 256)], [], ("ls%d" % x, n, dict(known["g"])))
+        ln, lw = ("RQ", 256) if x % 2 == 0 else ("R2", 544)
+        for s in range(N):
+            if s != rank:
+                note("r", [], [(ln, lw * t + w * s, lw * t + w * s + w)], ("ar%d" % x, narr, {}))
+
+    mset(A("WI"), 0)
+    dma("s", T.X0[:], T.xl[:], [], [("X0", 0, 256)])
+    dma("s", T.CO[:, 0:3], T.co[:], [], [("CO", 0, 8)])
+    dma("s", T.WI[0:128:16, :], T.wl[:], [], [("WI", 0, 256)])
+    dma("s", T.VI[:], T.vst[:], [], [("VI", 0, 128)])
+    dma("s", T.SI[:], T.hlp[:], [], [("SI", 0, B)])
+    dma("s", T.GN[:], T.gen[:], [], [("GN", 0, Q)])
+    dma("s", T.XT[:, 0:H], T.xst[:], [], [("XT", 0, H)])
+
+    iota(A("IP", 0, 1), [[0, 1]], 0, 1)
+    iota(A("IN"), [[1, 272]])
+    iota(A("BOF"), [[16, 8], [0, 16]])
+    iota(A("NM"), [[0, 17], [1, 16]])
+    iota(A("U16"), [[16, 16]])
+    iota(A("NE"), [[1, 128], [0, 16]], 0, -1)
+    cp(col(0), A("IP", 0, 1))
+    ts(A("IP", 1, 2), A("IP", 0, 1), 112, OP.bitwise_and)
+    ts(A("IP", 2, 3), A("IP", 0, 1), 15, OP.bitwise_and)
+    cp(A("COL", 1, 3), A("IP", 1, 3))
+    ts(col(3), col(1), 15.0, OP.add)
+    ts(col(4), col(2), 256.0, OP.mult)
+    ts(col(5), col(2), 32.0, OP.mult)
+    ts(col(20), col(2), 1.0, OP.add)
+    ts(col(16), col(2), 8.0, OP.is_ge, 0.5, OP.mult)
+    mset(A("C192"), 192.0)
+    ts(A("BM"), A("IN", 0, 144), col(3), OP.is_equal)
+    ts(A("ID"), A("IN", 0, 128), col(0), OP.is_equal)
+    ts(A("BOF"), A("BOF"), col(1), OP.is_equal)
+    fill("AB", Q + 2048, 2 * Q, 0.0)
+    cp(A("BO"), A("BOF"))
+    cp(A("COF", 0, 3), A("CO", 0, 3))
+    ts(A("QA"), A("X0"), 0.25, OP.mult, 191.625, OP.add)
+    ts(A("LA"), A("BM"), A("COF", 1, 2), OP.mult)
+    ts(A("BN"), A("BO"), A("COF", 1, 2), OP.mult)
+    ts(A("BC"), A("BO"), A("COF", 2, 3), OP.mult)
+    mm([(A("P6", 0, 2), A("BN"), A("C192"), True, True), (A("P6", 2, 4), A("BC"), A("C192"), True, True)])
+    ts(A("LW"), A("BM"), A("COF", 0, 1), OP.mult, 32.0, OP.mult)
+    ts(A("LC"), A("BM"), A("COF", 2, 3), OP.mult)
+    cp(A("COL", 6, 8), A("P6", 1, 3))
+
+    def constants_a():
+        ts(A("BASE"), A("U16"), col(4), OP.add)
+        cp(A("KP"), A("NM", 0, 256))
+        ts(A("RS"), A("NM", 0, 256), 0.0, OP.is_equal, BIG, OP.mult)
+        ts(A("OH"), A("IN", 0, 32), col(2), OP.is_equal)
+        cp(A("BMF"), A("BM"))
+        cp(A("TF"), A("WI"))
+        conv(A("P6", 0, 16), "BMF", "TF", True)
+        ts(A("D0"), A("NM", 0, 256), col(2), OP.is_equal)
+        ts(A("ND"), A("NM", 0, 256), col(2), OP.not_equal)
+        mset(A("VT"), 0.0)
+        ts(A("U512"), A("U16"), col(2), OP.add, 272.0, OP.add)
+        ts(A("U2048"), A("U16"), col(2), OP.add, 2048.0, OP.add)
+        cp(A("EXP"), A("IN", 0, 16))
+        ts(A("LD"), A("BM"), col(5), OP.mult)
+        fill("ONE", 0, 256, 1.0)
+        fill("C33", 0, 256, 33.0)
+        fill("SB", 0, 256, -8.0)
+        fill("WS", 0, 256, 0.0)
+        for t in range(TR):
+            fill("R2", 544 * t + 256, 544 * t + 528, -1.0)
+        iota(A("IO"), [[1, 2048]], 1)
+
+    def constants_c():
+        ts(A("VJ", 0, 128), A("VI"), 6, OP.arith_shift_right)
+        ts(A("VJ", 128, 256), A("VI"), 63, OP.bitwise_and)
+        cp(A("VH"), A("VJ"))
+        dma("s", T.VT[0:128:16, 0:H], T.VH[:, 0:128], [("VH", 0, 128)], [("VT", 0, H)])
+        dma("s", T.VT[1:128:16, 0:H], T.VH[:, 128:256], [("VH", 128, 256)], [("VT", 0, H)])
+        for j in (0, 2):
+            ts(col(23), col(2), float(j), OP.is_equal, 64.0, OP.mult)
+            ts(col(24), col(2), float(j + 1), OP.is_equal)
+            tt(col(21 + j // 2), col(23), col(24), OP.add)
+        ts(col(24), col(22), 0.0, OP.is_gt)
+        ts(col(25), col(0), -2.0, OP.add)
+        ts(col(26), col(2), 0.0, OP.is_equal)
+        ts(A("LR"), A("BM"), col(21), OP.mult)
+        ts(A("L0"), A("BM"), col(26), OP.mult)
+
+    def constants_d():
+        for j in (2, 3):
+            ts(A("DQ", 0, 128), A("NM", 0, 128), float(j), OP.is_equal)
+            tt(A("MX", 128 * j - 256, 128 * j - 128), A("DQ", 0, 128), A("BO"), OP.mult)
+        ts(A("MX", 256, 384), A("IN", 0, 128), col(25), OP.is_equal, col(24), OP.mult)
+
+    def constants_e():
+        ts(A("MX", 384, 512), A("BO"), col(21), OP.mult)
+        ts(A("MX", 512, 640), A("BO"), col(22), OP.mult)
+        ts(A("MX", 640, 768), A("BO"), 64.0, OP.mult)
+        ts(A("DQ", 0, 128), A("NM", 0, 128), 2.0, OP.is_lt, -8192.0, OP.mult)
+        tt(A("BN"), A("DQ", 0, 128), A("BO"), OP.mult)
+
+    def constants_b():
+        ts(A("NE"), A("NE"), 0.0, OP.is_equal, -1.0, OP.mult)
+        cp(A("SF", 0, B), A("SI"))
+        tt(col(17), col(16), col(2), OP.add)
+        ts(A("THL"), A("ID"), 4096.0, OP.mult)
+        ts(A("KW"), A("BOF"), col(20), OP.mult)
+        ts(A("DM"), A("ONE"), col(17), OP.mult, -1.0, OP.mult)
+        cp(A("WN"), A("P6", 0, 16))
+        constants_c()
+
+    def round_constants(t):
+        if t == 0:
+            ts(col(27), col(2), 16.0, OP.add)
+            ts(A("I2", 0, 4), A("IN", 0, 4), -1.0, OP.mult, col(27), OP.add)
+            ts(A("I2", 4, 8), A("IN", 0, 4), col(2), OP.add)
+            ts(A("I3", 0, 8), A("I2", 0, 8), 15, OP.bitwise_and)
+            cp(A("COL", 8, 12), A("I3", 0, 4))
+            ts(A("COL", 12, 16), A("I3", 4, 8), col(1), OP.add)
+            ts(A("MB"), A("ND"), BIG, OP.mult)
+        ts(A("TRI", 256 * t, 256 * t + 256), A("NM", 0, 256), col(8 + t), OP.is_le, BIG, OP.mult)
+        if t:
+            ts(A("ROT", 128 * t - 128, 128 * t), A("IN", 0, 128), col(12 + t), OP.is_equal)
+
+    def index(ps, c, bits, keep, out):
+        ts(A("I1"), ps, c, OP.subtract)
+        if bits == 0:
+            ts(A(keep), A("I1"), B - 1, OP.bitwise_and)
+        else:
+            ts(A(keep), A("I1"), bits, OP.arith_shift_right, H - 1, OP.bitwise_and)
+        cp(A(out), A(keep))
+
+    def prep_side(x):
+        mm([(A("PT", 0, 128), A(x, 128, 256), A("ID"))], tr=True)
+        act(A("XTR"), A("PT", 0, 128))
+        conv(A("P1", 0, 16), "LW", x, False)
+        act(A("AB", Q + 2048 + 15, 2 * Q, 16), A(x, 128, 256))
+        act(A("OWN"), A("P1", 0, 16), bias=-1.0)
+
+    def step(table, xn, qn, ak, head, tail):
+        cp(A("HS", 128, 192), IX(A(table, 0, B), A("BOF1", 8, 12)))
+        cp(A("HS", 192, 256), IX(A(table, 0, B), A("BOF1", 12, 16)))
+        cp(A("HS", 0, 128), IX(A(table, 0, B), A("BOF1", 0, 8)))
+        head()
+        mm([(A("P2", 0, 256), A("ID"), A("KP"), True, False)])
+
+        def score(l0, n, last):
+            js = list(range(l0 // 16, (l0 + n) // 16))
+            mm([(A("P2", 0, 256), A("LW", 15 - j, 143 - j), A("AB", 256 * j, 256 * j + 256), False, last and j == js[-1]) for j in js])
+
+        def gather(i):
+            l0, n, e = PIECES[i]
+            off = A("HS", l0, l0 + n)
+            if l0 >= 128:
+                gg = A("GG", 16 * (l0 - 128), 16 * (l0 - 128 + n))
+                (act if e == "a" else cp)(gg, IX(A("GN"), off))
+            else:
+                tt(A("DD", 16 * l0, 16 * (l0 + n)), IX(A("GN"), off), A("AB", Q + 16 * l0, Q + 16 * (l0 + n)), OP.subtract)
+        early = [i for i, p in enumerate(PIECES) if p[2] == "a"]
+        for i in early:
+            gather(i)
+        prev = None
+        for i, (l0, n, e) in enumerate(PIECES):
+            if e != "a":
+                gather(i)
+            if l0 >= 128:
+                src = A("P3" if i % 2 else "P4", 0, 16 * n)
+                lo = 16 * (l0 - 128)
+                mm([(src, A("XTR"), A("NE", lo, lo + 16 * n), True, False), (src, A("ID"), A("GG", lo, lo + 16 * n), False, True)])
+            else:
+                src = A("DD", 16 * l0, 16 * (l0 + n))
+            if i == len(PIECES) - 1:
+                tail()
+            if prev is not None:
+                score(prev[0], prev[1], False)
+            act(A("AB", 16 * l0, 16 * (l0 + n)), src, AF.Abs)
+            prev = (l0, n)
+        score(prev[0], prev[1], True)
+        scan(A("SC"), A("RS"), A("P2", 0, 256), 0.0, OP.add, OP.min)
+        tt(A("I2"), A("SC", 15, 256, 16), A("OWN"), OP.min)
+        ts(A(ak), A("I2"), 31, OP.bitwise_and)
+        ts(A("F1"), A(ak), 16.0, OP.is_ge, 4080.0, OP.mult)
+        tt(A("F2"), A(ak), A("BASE"), OP.add)
+        tt(A("F3"), A("F1"), A("F2"), OP.add)
+        cp(A("OFX"), A("F3"))
+        ts(A(qn, 0, 128), IX(A("AB"), A("OFX", 0, 8)), 0.25, OP.mult, 191.625, OP.add)
+        act(A(qn, 128, 256), IX(A("AB"), A("OFX", 8, 16)), scale=0.25, bias=191.625)
+        if xn == "X1":
+            cp(A(xn, 0, 128), IX(A("AB"), A("OFX", 0, 8)))
+            act(A(xn, 128, 256), IX(A("AB"), A("OFX", 8, 16)))
+        else:
+            act(A(xn), IX(A("AB"), A("OFX")))
+
+    def onehot(ak, a16, oh):
+        cp(A(a16), A(ak))
+        act(A(oh), IX(A("OH"), A(a16)))
+
+    def select(oh, bp, sel):
+        tt(A(sel), IX(A("SF", 0, B), A(bp)), A(oh), OP.mult)
+
+    def new_word(ps):
+        tt(A("I3"), ps, A("WN"), OP.mult)
+        ts(A("F5"), ps, 37.0, OP.mult)
+        ts(A("I4"), A("I3"), 5, OP.arith_shift_right)
+        tt(A("F6"), A("F5"), A("WN"), OP.add)
+        tt(A("I5"), A("F6"), A("I4"), OP.add)
+        ts(A("WN"), A("I5"), Q - 1, OP.bitwise_and)
+
+    def columns(c16, cd, t):
+        cp(A(c16), A("CC"))
+        tt(A(cd), A("CC"), A("TRI", 256 * t, 256 * t + 256), OP.add)
+
+    def first_of_key(key, c16, cd, rot, out, between):
+        tt(A("EE", 0, 256), IX(A(key), A("EXP")), A(cd), OP.is_equal)
+        mm([(A("P5", 0, 256), A("BO"), A("EE", 0, 256), True, False)])
+        pos = 256
+        for c in range(15):
+            lo = 16 * c + 16
+            e = A("EE", pos, pos + 256 - lo)
+            pos += 256 - lo
+            ts(e, A(c16, lo, 256), A(key, c, c + 1), OP.is_equal)
+            mm([(A("P5", lo, 256), A("BO"), e, False, c == 14)])
+        act(A("DC"), A("P5", 0, 256), scale=256.0)
+        conv(A("P0", 0, 16), "BM", "DC", True, rot)
+        ts(A("F7"), A(key), 0.0, OP.is_equal, 4096.0, OP.mult)
+        ts(A("F9"), A(key), -1.0, OP.add)
+        tt(A("F8"), A("F7"), A("F9"), OP.add)
+        between()
+        tt(A("F6"), A("F8"), A("P0", 0, 16), OP.add)
+        tt(A("F5"), A("F6"), A("U2048"), OP.min)
+        cp(A(out), A("F5"))
+
+    def nothing():
+        pass
+
+    def prep_first(x, q):
+        xrep(x, "g", 0, 8, True)
+        prep_side(x)
+        xrep(x, "a", 8, 16)
+        conv(A("P3", 0, 16), "LA", q, True)
+        conv(A("P4", 0, 16), "LA", q, False)
+
+    def prep_index():
+        index(A("P3", 0, 16), col(6), 0, "I6", "BOF1")
+        index(A("P4", 0, 16), col(6), 0, "I6", "BP1")
+
+    def sums(out, weights, table, i0, i1):
+        for i in range(i0, i1):
+            p = A("P3" if i % 2 else "P4")
+            mm([(p, weights, A(table, 512 * i, 512 * i + 512), True, True)])
+            act(A(out, 512 * i, 512 * i + 512), p)
+
+    def store_words(t):
+        cp(IX(A("VT"), A("OFS")), A("RW"))
+
+    def store_items(t):
+        cp(IX(A("XT"), A("OFS")), A("RQ", 256 * t, 256 * t + 256))
+
+    prep_first("X0", "QA")
+    prep_index()
+    constants_a()
+    round_constants(0)
+
+    for t in range(TR):
+        last = t == TR - 1
+        step("SF" if t else "SI", "X1", "QB", "AK1", nothing if t else constants_b, (lambda: store_items(t - 1)) if t else constants_d)
+        conv(A("P0", 0, 16), "LA", "QB", True)
+        xrep("X1", "g", 0, 8, True)
+        xrep("X1", "v", 8, 15)
+        prep_side("X1")
+        xrep("X1", "a", 15, 16)
+        conv(A("P1", 16, 32), "LA", "QB", False)
+        index(A("P0", 0, 16), col(6), 0, "I6", "BOF1")
+        step("SF", "X2", "QC", "AK2", nothing, (lambda: store_words(t - 1)) if t else constants_e)
+        mm([(A("P5", 0, 256), A("ID"), A("DM"), True, False), (A("P5", 0, 256), A("BC"), A("QC"), False, True)])
+        onehot("AK1", "A1", "OH1")
+        onehot("AK2", "A2", "OH2")
+        ts(A("TF"), A("P5", 0, 256), MAGIC, OP.add, MAGIC, OP.subtract)
+        tt(A("OW"), A("P5", 0, 256), A("TF"), OP.is_equal)
+        conv(A("P6", 0, 16), "LD", "OW", True)
+        scan(A("CN"), A("OW"), A("C33"), 0.0, OP.add, OP.min)
+        tt(A("VL"), A("OW"), A("CN"), OP.mult)
+        conv(A("P0", 0, 16), "BM", "VL", True)
+        act(A("PA"), A("P6", 0, 16), bias=-1.0)
+        select("OH1", "BP1", "SEL1")
+        ts(A("F1"), A("P0", 0, 16), 33.0, OP.is_ge)
+        tt(A("EV"), A("P0", 0, 16), A("PA"), OP.add)
+        tt(A("F2"), A("F1"), A("U512"), OP.mult)
+        tt(A("F3"), A("F2"), A("EV"), OP.max)
+        cp(A("OFQ"), A("F3"))
+        cp(IX(A("SB", 0, 528), A("OFQ")), A("X2"))
+        exchange(2 * t)
+        act(A("RQ", 256 * t + 32 * rank, 256 * t + 32 * rank + 32), A("SB", 32 * rank, 32 * rank + 32))
+        conv(A("P6", 0, 16), "BMF", "SEL1", False)
+        index(A("P1", 16, 32), col(6), 0, "BI", "BP2")
+        act(A("CC"), IX(A("IO"), A("BP2")))
+        select("OH2", "BP2", "SEL2")
+        mm([(A("P2", 0, 256), A("ID"), A("MB"), True, False), (A("P2", 0, 256), A("BOF"), A("SEL2"), False, True)])
+        columns("C16S", "CDS", t)
+        new_word(A("P6", 0, 16))
+        scan(A("SC"), A("RS"), A("P2", 0, 256), 0.0, OP.add, OP.min)
+        if last:
+            sums("YV", A("MX", 384, 512), "VT", 0, 4)
+        new_word(A("SC", 15, 256, 16))
+        ts(A("WH"), A("WN"), 6, OP.arith_shift_right)
+        ts(A("WL"), A("WN"), 63, OP.bitwise_and)
+        cp(A("WU"), A("WN"))
+        tt(A("HD"), IX(A("WH"), A("EXP")), A("D0"), OP.mult)
+        tt(A("LO"), IX(A("WL"), A("EXP")), A("D0"), OP.mult)
+        mm([(A("P6", 0, 256), A("MX", 0, 128), A("HD"), True, False), (A("P6", 0, 256), A("MX", 128, 256), A("LO"), False, True)])
+        act(A("WP"), A("P6", 0, 256))
+        tt(A("JD"), IX(A("GN"), A("WU")), A("X2"), OP.subtract)
+        act(A("JD"), A("JD"), AF.Abs)
+        act(A("X0"), A("JD"), scale=-1.0, bias=63.0)
+        cp(A("WB", 0, 16), A("WN"))
+        ts(A("WB", 16, 32), A("BI"), 1.0, OP.add)
+        cp(IX(A("WS", 0, 528), A("OFQ")), A("WP"))
+        if t:
+            mm([(A("P1", 0, 32), A("ROT", 128 * t - 128, 128 * t), A("WB"), True, True)])
+            act(A("WT"), A("P1", 0, 32))
+            wt = "WT"
+        else:
+            wt = "WB"
+        if not last:
+            act(A("QA"), A("X0"), scale=0.25, bias=191.625)
+            round_constants(t + 1)
+        if last:
+            dma("s", T.yx[:], T.X0[:], [("X0", 0, 256)], [])
+            mm([(A("P6", 0, 256), A("MX", 640, 768), A("HD"), True, False), (A("P6", 0, 256), A("BO"), A("LO"), False, True)])
+            act(A("WC"), A("P6", 0, 256))
+            dma("s", T.yw[:], T.WC[0:128:16, :], [("WC", 0, 256)], [])
+            sums("YH", A("KW"), "SF", 0, 2)
+        rq = A("RQ", 256 * t, 256 * t + 256)
+        mm([(A("P5", 0, 256), A("THL"), A("ONE"), True, False)])
+        ts(A("QQ"), rq, 0.25, OP.mult, 191.625, OP.add)
+        conv(A("P0", 0, 16), "LC", "QQ", True)
+        ts(A("VD"), rq, 0.0, OP.is_lt, -BIG, OP.mult)
+        index(A("P0", 0, 16), col(7), 3, "HI", "HOF")
+        act(A("CC"), IX(A("IO"), A("HOF")))
+        tt(A("DQ"), IX(A("XT", 0, H), A("HOF")), rq, OP.subtract)
+        act(A("AQ"), A("DQ"), AF.Abs)
+        mm([(A("P5", 0, 256), A("BN"), A("AQ"), False, True)])
+        tt(A("VG"), IX(A("VT", 0, H), A("HOF")), A("WS", 0, 256), OP.add)
+        tt(A("AW"), A("P5", 0, 256), A("VG"), OP.min)
+        exchange(2 * t + 1)
+        act(A("R2", 544 * t + 32 * rank, 544 * t + 32 * rank + 32), A("AW", 32 * rank, 32 * rank + 32))
+        tt(A("KN"), A("P5", 0, 256), A("VD"), OP.is_lt)
+        conv(A("P0", 0, 16), "L0", "KN", True)
+        if not last:
+            need("a", deps("a", [], [col(18)[1]]))
+            emit("a", A("AQ"), [A("P5", 0, 256), col(18)], lambda o, i, s: g.scalar.activation(o, i, AF.Sign, accum_out=s))
+            note("a", [], [col(18)[1]], ("sa", count["sa"], dict(known["a"])))
+            prep_first("X0", "QA")
+        ts(A("BT"), A(wt, 16, 32), -1.0, OP.add)
+        ts(A("F1"), A("HI"), 1.0, OP.add)
+        columns("C16O", "CDO", 0)
+        tt(A("KO"), A("F1"), A("P0", 0, 16), OP.mult)
+
+        def count_known():
+            tt(A("HM"), IX(A("SF", 0, B), A("BT")), A("ND"), OP.mult)
+            if not last:
+                ts(A("IP", 3, 4), col(18), 0.5, OP.mult, 128.0, OP.add)
+                ts(A("IP", 4, 5), A("IP", 3, 4), 7, OP.bitwise_and)
+                ts(col(19), A("IP", 4, 5), 8192.0, OP.mult, 4096.0, OP.add)
+                ts(A("THL"), A("ID"), col(19), OP.mult)
+        first_of_key("KO", "C16O", "CDO", 0, "OFS", count_known)
+        if last:
+            sums("YH", A("KW"), "SF", 2, 4)
+            mm([(A("P3", 0, 256), A("KW"), A("HM"), True, False)])
+            store_items(t)
+            dma("s", T.ys[:], T.XT[:, 0:H], [("XT", 0, H)], [])
+        else:
+            prep_index()
+            fill("SB", 0, 256, -8.0)
+        W, b1 = A(wt, 0, 16), A(wt, 16, 32)
+        mm([(A("P6", 0, 256), A("MX", 512, 640) if last else A("MX", 256, 384), A("R2", 544 * t, 544 * t + 256), True, True)])
+        cp(A("RG", 0, 128), IX(A("R2", 544 * t, 544 * t + 528), A("OFQ", 0, 8)))
+        act(A("RG", 128, 256), IX(A("R2", 544 * t, 544 * t + 528), A("OFQ", 8, 16)))
+        ret = A("P1", 0, 16)
+        conv(ret, "LR", "RG", True, t)
+        act(A("WC" if last else "RW"), A("P6", 0, 256))
+        tt(A("F1"), ret, W, OP.not_equal)
+        ts(A("F2"), ret, 0.0, OP.is_ge, 4096.0, OP.mult)
+        tt(A("F3"), A("F1"), b1, OP.mult)
+        tt(A("KY"), A("F3"), A("F2"), OP.min)
+
+        def new_column():
+            ts(A("F1"), ret, 0.0, OP.max)
+            tt(A("I3"), A("F1"), W, OP.mult)
+            tt(A("F2"), A("F1"), W, OP.add)
+            ts(A("I4"), A("I3"), 5, OP.arith_shift_right)
+            tt(A("I5"), A("F2"), A("I4"), OP.add)
+            ts(A("ZI"), A("I5"), Q - 1, OP.bitwise_and)
+            tt(A("ZD"), IX(A("ZI"), A("EXP")), A("D0"), OP.mult)
+            if last:
+                mm([(A("P3", 0, 256), A("KW"), A("ZD"), False, True)])
+                act(A("YC"), A("P3", 0, 256))
+
+        def last_words():
+            cp(IX(A("YV"), A("OFS")), A("WC"))
+            dma("a", T.yv[:], T.YV[0:128:16, 0:H], [("YV", 0, H)], [])
+        if last:
+            new_column()
+        first_of_key("KY", "C16S", "CDS", t, "OFH", last_words if last else new_column)
+        if last:
+            cp(IX(A("YH"), A("OFH")), A("YC"))
+            dma("s", T.yh[:], T.YH[0:128:16, 0:B], [("YH", 0, B)], [])
+        else:
+            tt(IX(A("SF"), A("OFH")), A("ZD"), A("HM"), OP.add)
+    for s, n in count.items():
+        if n:
+            g.wait_ge(T.sem[s], n)

@@ -7,6 +7,11 @@ MAGIC = 1.5 * 2.0 ** 26
 PIECES = [(128, 32, "a"), (160, 32, "v"), (192, 32, "v"), (224, 32, "v"),
           (0, 32, "v"), (32, 32, "v"), (64, 32, "v"), (96, 16, "v"), (112, 16, "v")]
 
+R0 = 128
+CY, LAT, WAY, HOLD = 0.83e-3, 0.2, 3.0, 1.0
+HELP = False
+SAME = True
+
 SCRATCH = {}
 PART = {}
 
@@ -24,7 +29,7 @@ def _decl(where, dtype, spec):
             PART[name] = (name, 0, int(cols))
 
 
-_decl("sbuf", "bfloat16", "GN:4096 XT:2304 X0:256 X1:256 X2:256 QA:256 QB:256 QC:256 CO:8 AB:8192 DD:2048 GG:2048 NE:2048 XTR:128 "
+_decl("sbuf", "bfloat16", "GN:4096 XT:2304 X0:256 X1:256 X2:256 QA:256 QB:256 QC:256 CO:8 AB:8192 DD:2048 GG:4096 NE:2048 XTR:256 "
       "BM:144 LA:144 LC:144 LW:144 LD:144 BO:128 BC:128 BN:128 ID:128 THL:128 KP:256 DM:256 ONE:256 C192:2 OH:32 OH1:256 OH2:256 "
       "OW:256 CN:256 VL:256 C33:256 SB:544 WS:544 AW:256 R2:2176 RQ:1024 QQ:256 DQ:256 AQ:256 KN:256 VD:256 EE:2176 DC:256 JD:256 HB:512 "
       "VT:2304 VH:256 VG:256 HD:256 LO:256 WP:256 RG:256 RW:256 LR:144 L0:144 MX:768 MB:256")
@@ -33,6 +38,12 @@ _decl("sbuf", "float32", "SF:2304 YV:2304 YH:2304 IO:2048 IN:272 NM:272 D0:256 N
       "WB:32 WT:32 WC:256 CC:256 CDS:256 CDO:256 KY:16 KO:16 HM:256 ZD:256 EV:16 PA:16 YC:256")
 _decl("sbuf", "int32", "SI:2048 VI:128 VJ:256 WI:256 IP:8 I1:16 I2:16 I3:16 I4:16 I5:16 I6:16 AK1:16 AK2:16 BI:16 HI:16 ZI:16 WN:16 WH:16 WL:16")
 _decl("sbuf", "uint16", "HS:256 BOF1:16 BP1:16 BP2:16 BT:16 OFX:16 A1:16 A2:16 OFQ:16 HOF:16 OFS:16 OFH:16 WU:16 EXP:16 C16S:256 C16O:256")
+TEMPS = "F1 F2 F3 F5 F6 F7 F8 F9 I1 I2 I3 I4 I5 I6".split()
+for _c in "abcdefgh":
+    _decl("sbuf", "float32", " ".join(n + _c + ":16" for n in TEMPS if n[0] == "F"))
+    _decl("sbuf", "int32", " ".join(n + _c + ":16" for n in TEMPS if n[0] == "I"))
+_decl("sbuf", "float32", "CC2:256 SD:256")
+_decl("sbuf", "bfloat16", "EF:2176 DC2:256 ORD:2")
 _decl("psum", "float32", "P0:512 P1:512 P2:512 P3:512 P4:512 P5:512 P6:512")
 _decl("psum", "bfloat16", "PT:1024")
 
@@ -54,6 +65,8 @@ def share(engines, i, n):
 def routes(T, topo, r):
     core = T.cores[r]
     rest = [d for d in range(N) if d != r]
+    if not HELP:
+        return [], [], rest
     pairs = []
     i = 0
     while len(pairs) < 2:
@@ -71,6 +84,10 @@ def routes(T, topo, r):
     return pairs, helpers, direct
 
 
+def calls(direct):
+    return [p for p in (direct[:-3], direct[-3:-1], direct[-1:]) if p]
+
+
 def arrivals(T, topo, d):
     n = 0
     for r in range(N):
@@ -78,7 +95,7 @@ def arrivals(T, topo, d):
             pairs, helpers, direct = routes(T, topo, r)
             src = T.cores[r] if d in direct else helpers[0 if d in pairs[0] else 1]
             e = len(topo.engines(src, T.cores[d]))
-            n += e if d == direct[2] else e // 2
+            n += e // ([len(p) for p in calls(direct) if d in p] + [2])[0]
     return n
 
 
@@ -125,6 +142,7 @@ def rank_program(g, core, T, topo):
     recs = {}
     ndma = [0]
     nrep = [0]
+    ctx = ["a"]
 
     def need(e, toks):
         best = {}
@@ -151,6 +169,8 @@ def rank_program(g, core, T, topo):
                         toks.append(tk)
                     elif e == "t" and e2 == "t":
                         continue
+                    elif not SAME and e == e2 and e in "va" and w:
+                        continue
                     elif l2 < hi and lo < h2 and (w or w2):
                         toks.append(tk)
         return toks
@@ -162,24 +182,101 @@ def rank_program(g, core, T, topo):
             recs[nm] = [x for x in recs.get(nm, []) if not (x[3] == e and not x[2] and lo <= x[0] and x[1] <= hi)] + [(lo, hi, False, e, tk, None)]
 
     def A(nm, lo=0, hi=None, st=1):
-        nm, base, cols = PART[nm]
+        nm, base, cols = PART[nm + ctx[0] if nm in TEMPS else nm]
         lo, hi = base + lo, base + (cols if hi is None else hi)
-        return (T[nm][:, lo:hi:st] if st != 1 else T[nm][:, lo:hi], (nm, lo, hi), [])
+        return (T[nm][:, lo:hi:st] if st != 1 else T[nm][:, lo:hi], (nm, lo, hi), [], (hi - lo + st - 1) // st)
 
     def IX(win, off):
-        return (win[0].indirect(off[0]), win[1], [off[1]])
+        return (win[0].indirect(off[0]), win[1], [off[1]], 16 * off[3])
+
+    ops = []
+
+    def later(e, reads, writes, dur, lag, fn, tag=None):
+        ops.append((e, reads, writes, dur, lag, fn, tag))
+
+    def issue():
+        last = {}
+        preds = []
+        for i, (e, reads, writes, dur, lag, fn, tag) in enumerate(ops):
+            p = set()
+            for spans, w in ((reads, False), (writes, True)):
+                for (nm, lo, hi) in spans:
+                    for (l2, h2, w2, j, tg) in last.get(nm, []):
+                        if l2 < hi and lo < h2 and (w or w2) and (tag is None or tg != tag):
+                            p.add(j)
+            for (nm, lo, hi) in writes:
+                last[nm] = [x for x in last.get(nm, []) if not (lo <= x[0] and x[1] <= hi) or (tag is not None and x[4] == tag)] + [(lo, hi, True, i, tag)]
+            for (nm, lo, hi) in reads:
+                last.setdefault(nm, []).append((lo, hi, False, i, None))
+            p.discard(i)
+            preds.append(p)
+        succ = [[] for _ in ops]
+        for i, p in enumerate(preds):
+            for j in p:
+                succ[j].append(i)
+        prio = [0.0] * len(ops)
+        for i in range(len(ops) - 1, -1, -1):
+            prio[i] = ops[i][3] + ops[i][4] + max([prio[j] + LAT for j in succ[i]] + [0.0])
+        left = [len(p) for p in preds]
+        at = [0.0] * len(ops)
+        free = {e: 0.0 for e in eng}
+        bank = {}
+        ready = [i for i in range(len(ops)) if not left[i]]
+        while ready:
+            def start(i):
+                s = max(at[i], free[ops[i][0]])
+                for (nm, lo, hi) in ops[i][1] + ops[i][2]:
+                    if nm in bank and bank[nm][0] != ops[i][0]:
+                        s = max(s, bank[nm][1])
+                return s
+            st = {i: start(i) for i in ready}
+            i = min(ready, key=lambda k: (st[k], -prio[k]))
+            rivals = [k for k in ready if ops[k][0] == ops[i][0] and st[k] < st[i] + HOLD * ops[i][3] and prio[k] > prio[i]]
+            if rivals:
+                i = max(rivals, key=lambda k: prio[k])
+            ready.remove(i)
+            e, reads, writes, dur, lag, fn, tag = ops[i]
+            free[e] = st[i] + dur
+            for (nm, lo, hi) in reads + writes:
+                if SCRATCH[nm][0] == "psum":
+                    bank[nm] = (e, st[i] + dur + LAT)
+            fn()
+            for j in succ[i]:
+                at[j] = max(at[j], st[i] + dur + lag + (0.0 if e == "t" and ops[j][0] == "t" else LAT))
+                left[j] -= 1
+                if not left[j]:
+                    ready.append(j)
 
     def col(j):
         return A("COL", j, j + 1)
 
-    def emit(e, out, ins, fn, tag=None):
+    def emit(e, out, ins, fn, tag=None, more=()):
         aps = [x for x in ins if isinstance(x, tuple)]
         reads = [x[1] for x in aps] + [y for x in aps for y in x[2]] + out[2]
-        need(e, deps(e, reads, [out[1]], tag))
-        s = "s" + e
-        count[s] += 1
-        fn(*[x[0] if isinstance(x, tuple) else x for x in [out] + ins]).then_inc(T.sem[s], 1)
-        note(e, reads, [out[1]], (s, count[s], dict(known[e])), tag)
+        writes = [out[1]] + [x[1] for x in more]
+        wide = [x for x in aps if x[3] > 1]
+        kinds = [SCRATCH[x[1][0]] for x in [out] + wide]
+        n = out[3]
+        if out[2]:
+            dur = 0.055 + 3.8 * CY * n
+        elif wide and wide[0][2]:
+            dur = 0.055 + 1.5 * CY * n
+        elif e == "g":
+            dur = 0.17 + 2 * CY * n
+        elif e == "a":
+            dur = 0.06 + max(64, n) * CY
+        elif len(wide) == 2 and len(ins) == 3:
+            dur = max(64, n * (1 if "psum" in [k[0] for k in kinds[1:]] else 2)) * CY
+        else:
+            dur = max(64, n * (0.5 if all(k[2] in ("bfloat16", "uint16") for k in kinds) else 1)) * CY
+
+        def go():
+            need(e, deps(e, reads, writes, tag))
+            s = "s" + e
+            count[s] += 1
+            fn(*[x[0] if isinstance(x, tuple) else x for x in [out] + ins]).then_inc(T.sem[s], 1)
+            note(e, reads, writes, (s, count[s], dict(known[e])), tag)
+        later(e, reads, writes, dur, 0.0, go, tag)
 
     def cp(out, a):
         emit("v", out, [a], g.vector.tensor_copy)
@@ -209,6 +306,12 @@ def rank_program(g, core, T, topo):
             emit("g", out, [], lambda o: g.iota(o, pat, base, cm, allow_small_or_imprecise_dtypes=True))
 
     def mm(items, tr=False):
+        whole = not tr and not (items[0][3] and items[-1][4])
+        dur = sum(max(64, it[2][3]) * (4 if SCRATCH[it[1][1][0]][2] == "float32" else 1) for it in items) * CY / 2
+        later("t", [x[1] for it in items for x in it[1:3]], [(it[0][1][0], 0, 512) if whole else it[0][1] for it in items], dur, 0.0,
+              lambda: mm_now(items, tr))
+
+    def mm_now(items, tr):
         count["st"] += 1
         done = []
         for it in items:
@@ -224,7 +327,10 @@ def rank_program(g, core, T, topo):
         for reads, w in done:
             note("t", reads, [w], tk)
 
-    def dma(e, out_ap, in_ap, reads, writes):
+    def dma(e, out_ap, in_ap, reads, writes, lag=2.5):
+        later(e, reads + [("ORD", 0, 1)], writes + ([("ORD", 0, 1)] if lag > 2.5 else []), 0.06, lag, lambda: dma_now(e, out_ap, in_ap, reads, writes))
+
+    def dma_now(e, out_ap, in_ap, reads, writes):
         need(e, deps("d", reads, writes))
         s = "d%d" % ndma[0]
         ndma[0] += 1
@@ -241,14 +347,14 @@ def rank_program(g, core, T, topo):
     def xrep(x, e, k0, k1, new=False):
         if new:
             nrep[0] += 1
-        for k in range(k0, k1):
-            o, i = A("AB", Q + k, Q + 2048, 16), A(x, 0, 128)
+        for k in range(k0, k1 if R0 else k0):
+            o, i = A("AB", Q + k, Q + 16 * R0, 16), A(x, 0, R0)
             if e == "v":
                 emit(e, o, [i], g.vector.tensor_copy, nrep[0])
             elif e == "a":
                 emit(e, o, [i], lambda o, i: g.scalar.activation(o, i, AF.Copy), nrep[0])
             else:
-                emit(e, o, [i], lambda o, i: g.affine_select(o, i, [[0, 128]], OP.is_ge, 0.0, 0, 0), nrep[0])
+                emit(e, o, [i], lambda o, i: g.affine_select(o, i, [[0, R0]], OP.is_ge, 0.0, 0, 0), nrep[0])
 
     def fill(nm, lo, hi, c):
         while lo < hi:
@@ -260,6 +366,11 @@ def rank_program(g, core, T, topo):
     narr = arrivals(T, topo, rank)
 
     def exchange(x):
+        ln, lw = ("RQ", 256) if x % 2 == 0 else ("R2", 544)
+        later("g", [("SB" if x % 2 == 0 else "AW", 0, 256)], [(ln, lw * (x // 2) + 32 * s, lw * (x // 2) + 32 * s + 32) for s in range(N) if s != rank],
+              1.0, WAY, lambda: exchange_now(x))
+
+    def exchange_now(x):
         t = x // 2
         nm, w = "SB" if x % 2 == 0 else "AW", 32
         need("g", deps("r", [(nm, 0, 256)], []))
@@ -271,8 +382,9 @@ def rank_program(g, core, T, topo):
             n += len(es)
             d = pairs[i][0]
             trs.append(transfer(topo, h, es, T.sem["ha%d" % x], T[nm][:, w * d:w * d + 2 * w], T.HB[:, 64 * x:64 * x + 64]))
-        g.remote_dma_fused(trs, local_sem=ls)
-        for part in (direct[:2], direct[2:]):
+        if trs:
+            g.remote_dma_fused(trs, local_sem=ls)
+        for part in calls(direct):
             trs = []
             for i, d in enumerate(part):
                 es = share(topo.engines(core, T.cores[d]), i, len(part))
@@ -292,9 +404,9 @@ def rank_program(g, core, T, topo):
     dma("s", T.CO[:, 0:3], T.co[:], [], [("CO", 0, 8)])
     dma("s", T.WI[0:128:16, :], T.wl[:], [], [("WI", 0, 256)])
     dma("s", T.VI[:], T.vst[:], [], [("VI", 0, 128)])
-    dma("s", T.SI[:], T.hlp[:], [], [("SI", 0, B)])
-    dma("s", T.GN[:], T.gen[:], [], [("GN", 0, Q)])
-    dma("s", T.XT[:, 0:H], T.xst[:], [], [("XT", 0, H)])
+    dma("s", T.SI[:], T.hlp[:], [], [("SI", 0, B)], 7.0)
+    dma("s", T.GN[:], T.gen[:], [], [("GN", 0, Q)], 4.5)
+    dma("s", T.XT[:, 0:H], T.xst[:], [], [("XT", 0, H)], 2.6)
 
     iota(A("IP", 0, 1), [[0, 1]], 0, 1)
     iota(A("IN"), [[1, 272]])
@@ -315,7 +427,8 @@ def rank_program(g, core, T, topo):
     ts(A("BM"), A("IN", 0, 144), col(3), OP.is_equal)
     ts(A("ID"), A("IN", 0, 128), col(0), OP.is_equal)
     ts(A("BOF"), A("BOF"), col(1), OP.is_equal)
-    fill("AB", Q + 2048, 2 * Q, 0.0)
+    fill("AB", Q + 16 * R0, Q + 2048, 0.0)
+    mset(A("AB", Q + 2048, 2 * Q), 0.0)
     cp(A("BO"), A("BOF"))
     cp(A("COF", 0, 3), A("CO", 0, 3))
     ts(A("QA"), A("X0"), 0.25, OP.mult, 191.625, OP.add)
@@ -411,10 +524,10 @@ def rank_program(g, core, T, topo):
         cp(A(out), A(keep))
 
     def prep_side(x):
-        mm([(A("PT", 0, 128), A(x, 128, 256), A("ID"))], tr=True)
-        act(A("XTR"), A("PT", 0, 128))
+        mm([(A("PT", 128, 256), A(x, 128, 256), A("ID"))], tr=True)
+        act(A("XTR", 128, 256), A("PT", 128, 256))
         conv(A("P1", 0, 16), "LW", x, False)
-        act(A("AB", Q + 2048 + 15, 2 * Q, 16), A(x, 128, 256))
+        act(A("AB", Q + 16 * R0 + 15, 2 * Q, 16), A(x, R0, 256))
         act(A("OWN"), A("P1", 0, 16), bias=-1.0)
 
     def step(table, xn, qn, ak, head, tail):
@@ -431,8 +544,8 @@ def rank_program(g, core, T, topo):
         def gather(i):
             l0, n, e = PIECES[i]
             off = A("HS", l0, l0 + n)
-            if l0 >= 128:
-                gg = A("GG", 16 * (l0 - 128), 16 * (l0 - 128 + n))
+            if l0 >= R0:
+                gg = A("GG", 16 * l0, 16 * (l0 + n))
                 (act if e == "a" else cp)(gg, IX(A("GN"), off))
             else:
                 tt(A("DD", 16 * l0, 16 * (l0 + n)), IX(A("GN"), off), A("AB", Q + 16 * l0, Q + 16 * (l0 + n)), OP.subtract)
@@ -443,10 +556,10 @@ def rank_program(g, core, T, topo):
         for i, (l0, n, e) in enumerate(PIECES):
             if e != "a":
                 gather(i)
-            if l0 >= 128:
-                src = A("P3" if i % 2 else "P4", 0, 16 * n)
-                lo = 16 * (l0 - 128)
-                mm([(src, A("XTR"), A("NE", lo, lo + 16 * n), True, False), (src, A("ID"), A("GG", lo, lo + 16 * n), False, True)])
+            if l0 >= R0:
+                src = A(("P3", "P4")[i % 2], 0, 16 * n)
+                lo, h = 16 * (l0 % 128), 128 * (l0 // 128)
+                mm([(src, A("XTR", h, h + 128), A("NE", lo, lo + 16 * n), True, False), (src, A("ID"), A("GG", 16 * l0, 16 * (l0 + n)), False, True)])
             else:
                 src = A("DD", 16 * l0, 16 * (l0 + n))
             if i == len(PIECES) - 1:
@@ -487,26 +600,28 @@ def rank_program(g, core, T, topo):
         ts(A("WN"), A("I5"), Q - 1, OP.bitwise_and)
 
     def columns(c16, cd, t):
-        cp(A(c16), A("CC"))
-        tt(A(cd), A("CC"), A("TRI", 256 * t, 256 * t + 256), OP.add)
+        cc = A("CC2" if cd == "CDO" else "CC")
+        cp(A(c16), cc)
+        tt(A(cd), cc, A("TRI", 256 * t, 256 * t + 256), OP.add)
 
     def first_of_key(key, c16, cd, rot, out, between):
-        tt(A("EE", 0, 256), IX(A(key), A("EXP")), A(cd), OP.is_equal)
-        mm([(A("P5", 0, 256), A("BO"), A("EE", 0, 256), True, False)])
+        ee, dc, pc, po = ("EF", "DC2", "P6", A("P0", 32, 48)) if key == "KO" else ("EE", "DC", "P5", A("P0", 0, 16))
+        tt(A(ee, 0, 256), IX(A(key), A("EXP")), A(cd), OP.is_equal)
+        mm([(A(pc, 0, 256), A("BO"), A(ee, 0, 256), True, False)])
         pos = 256
         for c in range(15):
             lo = 16 * c + 16
-            e = A("EE", pos, pos + 256 - lo)
+            e = A(ee, pos, pos + 256 - lo)
             pos += 256 - lo
             ts(e, A(c16, lo, 256), A(key, c, c + 1), OP.is_equal)
-            mm([(A("P5", lo, 256), A("BO"), e, False, c == 14)])
-        act(A("DC"), A("P5", 0, 256), scale=256.0)
-        conv(A("P0", 0, 16), "BM", "DC", True, rot)
+            mm([(A(pc, lo, 256), A("BO"), e, False, c == 14)])
+        act(A(dc), A(pc, 0, 256), scale=256.0)
+        conv(po, "BM", dc, True, rot)
         ts(A("F7"), A(key), 0.0, OP.is_equal, 4096.0, OP.mult)
         ts(A("F9"), A(key), -1.0, OP.add)
         tt(A("F8"), A("F7"), A("F9"), OP.add)
         between()
-        tt(A("F6"), A("F8"), A("P0", 0, 16), OP.add)
+        tt(A("F6"), A("F8"), po, OP.add)
         tt(A("F5"), A("F6"), A("U2048"), OP.min)
         cp(A(out), A("F5"))
 
@@ -521,7 +636,9 @@ def rank_program(g, core, T, topo):
         conv(A("P4", 0, 16), "LA", q, False)
 
     def prep_index():
+        ctx[0] = "g"
         index(A("P3", 0, 16), col(6), 0, "I6", "BOF1")
+        ctx[0] = "e"
         index(A("P4", 0, 16), col(6), 0, "I6", "BP1")
 
     def sums(out, weights, table, i0, i1):
@@ -543,6 +660,7 @@ def rank_program(g, core, T, topo):
 
     for t in range(TR):
         last = t == TR - 1
+        ctx[0] = "a"
         step("SF" if t else "SI", "X1", "QB", "AK1", nothing if t else constants_b, (lambda: store_items(t - 1)) if t else constants_d)
         conv(A("P0", 0, 16), "LA", "QB", True)
         xrep("X1", "g", 0, 8, True)
@@ -553,6 +671,7 @@ def rank_program(g, core, T, topo):
         index(A("P0", 0, 16), col(6), 0, "I6", "BOF1")
         step("SF", "X2", "QC", "AK2", nothing, (lambda: store_words(t - 1)) if t else constants_e)
         mm([(A("P5", 0, 256), A("ID"), A("DM"), True, False), (A("P5", 0, 256), A("BC"), A("QC"), False, True)])
+        ctx[0] = "b"
         onehot("AK1", "A1", "OH1")
         onehot("AK2", "A2", "OH2")
         ts(A("TF"), A("P5", 0, 256), MAGIC, OP.add, MAGIC, OP.subtract)
@@ -572,16 +691,18 @@ def rank_program(g, core, T, topo):
         exchange(2 * t)
         act(A("RQ", 256 * t + 32 * rank, 256 * t + 32 * rank + 32), A("SB", 32 * rank, 32 * rank + 32))
         conv(A("P6", 0, 16), "BMF", "SEL1", False)
+        ctx[0] = "c"
         index(A("P1", 16, 32), col(6), 0, "BI", "BP2")
         act(A("CC"), IX(A("IO"), A("BP2")))
         select("OH2", "BP2", "SEL2")
         mm([(A("P2", 0, 256), A("ID"), A("MB"), True, False), (A("P2", 0, 256), A("BOF"), A("SEL2"), False, True)])
         columns("C16S", "CDS", t)
         new_word(A("P6", 0, 16))
-        scan(A("SC"), A("RS"), A("P2", 0, 256), 0.0, OP.add, OP.min)
+        scan(A("SD"), A("RS"), A("P2", 0, 256), 0.0, OP.add, OP.min)
         if last:
             sums("YV", A("MX", 384, 512), "VT", 0, 4)
-        new_word(A("SC", 15, 256, 16))
+        ctx[0] = "d"
+        new_word(A("SD", 15, 256, 16))
         ts(A("WH"), A("WN"), 6, OP.arith_shift_right)
         ts(A("WL"), A("WN"), 63, OP.bitwise_and)
         cp(A("WU"), A("WN"))
@@ -596,8 +717,8 @@ def rank_program(g, core, T, topo):
         ts(A("WB", 16, 32), A("BI"), 1.0, OP.add)
         cp(IX(A("WS", 0, 528), A("OFQ")), A("WP"))
         if t:
-            mm([(A("P1", 0, 32), A("ROT", 128 * t - 128, 128 * t), A("WB"), True, True)])
-            act(A("WT"), A("P1", 0, 32))
+            mm([(A("P1", 64, 96), A("ROT", 128 * t - 128, 128 * t), A("WB"), True, True)])
+            act(A("WT"), A("P1", 64, 96))
             wt = "WT"
         else:
             wt = "WB"
@@ -611,12 +732,13 @@ def rank_program(g, core, T, topo):
             dma("s", T.yw[:], T.WC[0:128:16, :], [("WC", 0, 256)], [])
             sums("YH", A("KW"), "SF", 0, 2)
         rq = A("RQ", 256 * t, 256 * t + 256)
+        ctx[0] = "e"
         mm([(A("P5", 0, 256), A("THL"), A("ONE"), True, False)])
         ts(A("QQ"), rq, 0.25, OP.mult, 191.625, OP.add)
         conv(A("P0", 0, 16), "LC", "QQ", True)
         ts(A("VD"), rq, 0.0, OP.is_lt, -BIG, OP.mult)
         index(A("P0", 0, 16), col(7), 3, "HI", "HOF")
-        act(A("CC"), IX(A("IO"), A("HOF")))
+        act(A("CC2"), IX(A("IO"), A("HOF")))
         tt(A("DQ"), IX(A("XT", 0, H), A("HOF")), rq, OP.subtract)
         act(A("AQ"), A("DQ"), AF.Abs)
         mm([(A("P5", 0, 256), A("BN"), A("AQ"), False, True)])
@@ -625,16 +747,15 @@ def rank_program(g, core, T, topo):
         exchange(2 * t + 1)
         act(A("R2", 544 * t + 32 * rank, 544 * t + 32 * rank + 32), A("AW", 32 * rank, 32 * rank + 32))
         tt(A("KN"), A("P5", 0, 256), A("VD"), OP.is_lt)
-        conv(A("P0", 0, 16), "L0", "KN", True)
+        ctx[0] = "f"
+        conv(A("P0", 48, 64), "L0", "KN", True)
         if not last:
-            need("a", deps("a", [], [col(18)[1]]))
-            emit("a", A("AQ"), [A("P5", 0, 256), col(18)], lambda o, i, s: g.scalar.activation(o, i, AF.Sign, accum_out=s))
-            note("a", [], [col(18)[1]], ("sa", count["sa"], dict(known["a"])))
+            emit("a", A("AQ"), [A("P5", 0, 256), col(18)], lambda o, i, s: g.scalar.activation(o, i, AF.Sign, accum_out=s), None, [col(18)])
             prep_first("X0", "QA")
         ts(A("BT"), A(wt, 16, 32), -1.0, OP.add)
         ts(A("F1"), A("HI"), 1.0, OP.add)
         columns("C16O", "CDO", 0)
-        tt(A("KO"), A("F1"), A("P0", 0, 16), OP.mult)
+        tt(A("KO"), A("F1"), A("P0", 48, 64), OP.mult)
 
         def count_known():
             tt(A("HM"), IX(A("SF", 0, B), A("BT")), A("ND"), OP.mult)
@@ -656,7 +777,8 @@ def rank_program(g, core, T, topo):
         mm([(A("P6", 0, 256), A("MX", 512, 640) if last else A("MX", 256, 384), A("R2", 544 * t, 544 * t + 256), True, True)])
         cp(A("RG", 0, 128), IX(A("R2", 544 * t, 544 * t + 528), A("OFQ", 0, 8)))
         act(A("RG", 128, 256), IX(A("R2", 544 * t, 544 * t + 528), A("OFQ", 8, 16)))
-        ret = A("P1", 0, 16)
+        ret = A("P1", 32, 48)
+        ctx[0] = "h"
         conv(ret, "LR", "RG", True, t)
         act(A("WC" if last else "RW"), A("P6", 0, 256))
         tt(A("F1"), ret, W, OP.not_equal)
@@ -665,12 +787,14 @@ def rank_program(g, core, T, topo):
         tt(A("KY"), A("F3"), A("F2"), OP.min)
 
         def new_column():
+            ctx[0] = "d"
             ts(A("F1"), ret, 0.0, OP.max)
             tt(A("I3"), A("F1"), W, OP.mult)
             tt(A("F2"), A("F1"), W, OP.add)
             ts(A("I4"), A("I3"), 5, OP.arith_shift_right)
             tt(A("I5"), A("F2"), A("I4"), OP.add)
             ts(A("ZI"), A("I5"), Q - 1, OP.bitwise_and)
+            ctx[0] = "h"
             tt(A("ZD"), IX(A("ZI"), A("EXP")), A("D0"), OP.mult)
             if last:
                 mm([(A("P3", 0, 256), A("KW"), A("ZD"), False, True)])
@@ -687,6 +811,7 @@ def rank_program(g, core, T, topo):
             dma("s", T.yh[:], T.YH[0:128:16, 0:B], [("YH", 0, B)], [])
         else:
             tt(IX(A("SF"), A("OFH")), A("ZD"), A("HM"), OP.add)
+    issue()
     for s, n in count.items():
         if n:
             g.wait_ge(T.sem[s], n)

@@ -2,15 +2,21 @@ from concourse.bass import DstId, RemoteDMATransfer
 from concourse.mybir import AluOpType as OP, ActivationFunctionType as AF
 
 N, Q, B, H, L, CAP, TR = 8, 4096, 2048, 2048, 256, 32, 4
-BIG = 1.0e8
+BIG = 2.0 ** 22
 MAGIC = 1.5 * 2.0 ** 26
-PIECES = [(128, 32, "a"), (160, 32, "v"), (192, 32, "v"), (224, 32, "v"),
-          (0, 32, "v"), (32, 32, "v"), (64, 32, "v"), (96, 16, "v"), (112, 16, "v")]
+HL = L // 2
+PIECES = {0: ("vava", "xxxx"), 1: ("avav", "avav"), 2: ("vava", "xxxx")}
+REP = {0: "vvvvvvvvaaaaaaaa", 1: "g" * 16, 2: "gggggggvvvvvvvvv"}
+STAY = "g"
+TAKE = {"QB": "aa", "QC": "av"}
 
-R0 = 128
-CY, LAT, WAY, HOLD = 0.83e-3, 0.2, 3.0, 1.0
-HELP = False
-SAME = True
+CY, LAT, WAY, HOLD = 0.83e-3, 0.2, (2.3, 2.5, 2.5), 1.0
+LINE = (1, 0, 1)
+PASSES, LONG = 1, 4.0
+SOONER = {"columns": 12.0, "words": 6.0, "items": 6.0, "stored": 6.0, "v1": 6.0, "a1": 6.0, "summed": 14.0, "last items": 5.0}
+AFTER = {"select": "x2", "jump": "slots", "words": "jump", "items": "words", "stored": "items", "v1": "answered", "sum": "slots"}
+GAT, SCA = 1.56, 3.8
+LAGS = (7.0, 11.5, 14.0)
 
 SCRATCH = {}
 PART = {}
@@ -29,26 +35,27 @@ def _decl(where, dtype, spec):
             PART[name] = (name, 0, int(cols))
 
 
-_decl("sbuf", "bfloat16", "GN:4096 XT:2304 X0:256 X1:256 X2:256 QA:256 QB:256 QC:256 CO:8 AB:8192 DD:2048 GG:4096 NE:2048 XTR:256 "
-      "BM:144 LA:144 LC:144 LW:144 LD:144 BO:128 BC:128 BN:128 ID:128 THL:128 KP:256 DM:256 ONE:256 C192:2 OH:32 OH1:256 OH2:256 "
-      "OW:256 CN:256 VL:256 C33:256 SB:544 WS:544 AW:256 R2:2176 RQ:1024 QQ:256 DQ:256 AQ:256 KN:256 VD:256 EE:2176 DC:256 JD:256 HB:512 "
-      "VT:2304 VH:256 VG:256 HD:256 LO:256 WP:256 RG:256 RW:256 LR:144 L0:144 MX:768 MB:256")
-_decl("sbuf", "float32", "SF:2304 YV:2304 YH:2304 IO:2048 IN:272 NM:272 D0:256 ND:256 RS:256 TRI:1024 ROT:384 KW:128 BMF:144 BOF:128 "
-      "COL:32 COF:4 U16:16 BASE:16 U512:16 U2048:16 SC:256 OWN:16 F1:16 F2:16 F3:16 F4:16 F5:16 F6:16 F7:16 F8:16 F9:16 TF:256 SEL1:256 SEL2:256 "
-      "WB:32 WT:32 WC:256 CC:256 CDS:256 CDO:256 KY:16 KO:16 HM:256 ZD:256 EV:16 PA:16 YC:256")
-_decl("sbuf", "int32", "SI:2048 VI:128 VJ:256 WI:256 IP:8 I1:16 I2:16 I3:16 I4:16 I5:16 I6:16 AK1:16 AK2:16 BI:16 HI:16 ZI:16 WN:16 WH:16 WL:16")
-_decl("sbuf", "uint16", "HS:256 BOF1:16 BP1:16 BP2:16 BT:16 OFX:16 A1:16 A2:16 OFQ:16 HOF:16 OFS:16 OFH:16 WU:16 EXP:16 C16S:256 C16O:256")
-TEMPS = "F1 F2 F3 F5 F6 F7 F8 F9 I1 I2 I3 I4 I5 I6".split()
+_decl("sbuf", "float32", "HO:256 ZC:256 SZ:256 KT:16 KU:16 LT:16")
+_decl("sbuf", "bfloat16", "CH:256 DN:256 EK:256 LK:144")
+_decl("sbuf", "int32", "AKA:16")
+_decl("sbuf", "uint16", "ZO:16")
+_decl("sbuf", "bfloat16", "GN:4112 TW:4096 XT:2304 VT:2304 XL:256 X0:256 X1:256 X2:256 QA:256 QB:256 QC:256 CO:8 AB:8192 XR:2048 DD:2048 "
+      "GG:4096 NE:2048 XTR:256 BM:144 LA:144 LC:144 LW:144 LD:144 LR:144 LN:144 LU:144 BO:128 BC:128 BA:128 BN:384 BK:512 ID:128 "
+      "THL:128 KP:256 DM:128 ONE:128 C192:2 OH:32 OH1:256 OH2:256 OW:256 CN:256 VL:256 SB:2048 WS:2048 R2:2048 AW:256 RQ:1024 QQ:256 "
+      "XG:256 MQ:256 VG:256 NG:256 AQ:256 EE:2176 EF:2176 JD:256 JA:256 VH:256 TH:256 WP:256 RG:256 NQ:256 RW:256 MX:512 MB:512 ORD:32")
+_decl("sbuf", "float32", "SF:2304 YV:2304 YH:2304 IO:2048 IN:272 NM:272 D0:272 ND:272 RS:256 RU:256 KW:128 BMF:144 BOF:128 IDF:128 "
+      "COL:32 COF:4 BASE:16 SC:256 OWN:16 TF:256 HF:256 SEL1:256 SELP:256 SEL2:256 SD:512 SK:512 WT:16 B1:16 WC:256 CC:256 CC2:256 "
+      "KY:16 KO:16 HM:256 ZD:256 YC:256")
+_decl("sbuf", "int32", "SI:2048 VI:128 VJ:256 WI:256 IP:8 AK1:16 AK2:16 BI:16 HI:16 ZI:16 WN:16")
+_decl("sbuf", "uint16", "HS:256 BO1:16 BO2:16 BP2:16 OFX:16 A1:16 A2:16 OFQ:16 HOF:16 OFS:16 OFH:16 WU:16 EXP:16 PERM:16 C16S:256 C16O:256")
+TEMPS = "F1 F2 F3 F4 F5 I1 I2 I3 I4 I5 I6".split()
 for _c in "abcdefgh":
     _decl("sbuf", "float32", " ".join(n + _c + ":16" for n in TEMPS if n[0] == "F"))
     _decl("sbuf", "int32", " ".join(n + _c + ":16" for n in TEMPS if n[0] == "I"))
-_decl("sbuf", "float32", "CC2:256 SD:256")
-_decl("sbuf", "bfloat16", "EF:2176 DC2:256 ORD:2")
-_decl("psum", "float32", "P0:512 P1:512 P2:512 P3:512 P4:512 P5:512 P6:512")
-_decl("psum", "bfloat16", "PT:1024")
+_decl("psum", "float32", "P0:512 P1:512 P2:512 P3:512 P4:512 P5:512 P6:512 P7:512")
 
-SEMAPHORES = (["sv", "sa", "st", "sg"] + ["d%d" % i for i in range(32)] + ["ls%d" % i for i in range(2 * TR)]
-              + ["ar%d" % i for i in range(2 * TR)] + ["ha%d" % i for i in range(2 * TR)])
+SEMAPHORES = (["sv", "sa", "st", "sg"] + ["d%d" % i for i in range(32)] + ["ls%d" % i for i in range(6 * TR)]
+              + ["ar%d" % i for i in range(4 * TR)])
 
 
 def _mask(engines):
@@ -62,48 +69,20 @@ def share(engines, i, n):
     return engines[i * len(engines) // n:(i + 1) * len(engines) // n]
 
 
-def routes(T, topo, r):
-    core = T.cores[r]
-    rest = [d for d in range(N) if d != r]
-    if not HELP:
-        return [], [], rest
-    pairs = []
-    i = 0
-    while len(pairs) < 2:
-        if rest[i + 1] == rest[i] + 1:
-            pairs.append((rest[i], rest[i + 1]))
-            i += 2
-        else:
-            i += 1
-    direct = [d for d in rest if d not in pairs[0] and d not in pairs[1]]
-    cands = [c for c in topo.cores_of(core) if T.rank_of(c) is None]
-    cands.sort(key=lambda c: topo.die(c) != topo.die(core))
-    helpers = []
-    for p in pairs:
-        helpers.append([c for c in cands if c not in helpers and all(topo.may_write(c, T.cores[d]) for d in p)][0])
-    return pairs, helpers, direct
+def calls(r):
+    half = N // 2
+    lo = half * (r // half)
+    own = [lo + (r - lo + i) % half for i in range(1, half)]
+    return [[d for d in range(N) if not lo <= d < lo + half], own[:2], own[2:]]
 
 
-def calls(direct):
-    return [p for p in (direct[:-3], direct[-3:-1], direct[-1:]) if p]
-
-
-def arrivals(T, topo, d):
+def arrivals(T, topo, d, part):
     n = 0
     for r in range(N):
-        if r != d:
-            pairs, helpers, direct = routes(T, topo, r)
-            src = T.cores[r] if d in direct else helpers[0 if d in pairs[0] else 1]
-            e = len(topo.engines(src, T.cores[d]))
-            n += e // ([len(p) for p in calls(direct) if d in p] + [2])[0]
+        for i, p in enumerate(calls(r)):
+            if d in p and min(i, 1) == part:
+                n += len(topo.engines(T.cores[r], T.cores[d])) // len(p)
     return n
-
-
-def landing(T, x, src):
-    t = x // 2
-    if x % 2 == 0:
-        return T.RQ[:, 256 * t + 32 * src:256 * t + 32 * src + 32]
-    return T.R2[:, 544 * t + 32 * src:544 * t + 32 * src + 32]
 
 
 def transfer(topo, dst, engines, sem, src_ap, dst_ap):
@@ -111,29 +90,9 @@ def transfer(topo, dst, engines, sem, src_ap, dst_ap):
     return RemoteDMATransfer(dst_ids=[DstId(rid=rid, pnc=pid)], dma_engine_mask=_mask(engines), remote_sem=sem, src=src_ap, dst=dst_ap)
 
 
-def helper_program(g, core, T, topo, r, pair):
-    got = len(topo.engines(T.cores[r], core)) // 2
-    n = 0
-    for x in range(2 * TR):
-        g.wait_ge(T.sem["ha%d" % x], got)
-        trs = []
-        for i, d in enumerate(pair):
-            es = share(topo.engines(core, T.cores[d]), i, 2)
-            n += len(es)
-            s = T.HB[:, 64 * x + 32 * i:64 * x + 32 * i + 32]
-            trs.append(transfer(topo, T.cores[d], es, T.sem["ar%d" % x], s, landing(T, x, r)))
-        g.remote_dma_fused(trs, local_sem=T.sem["ls0"])
-    g.wait_ge(T.sem["ls0"], n)
-
-
 def rank_program(g, core, T, topo):
     rank = T.rank_of(core)
     if rank is None:
-        for r in range(N):
-            if core in topo.cores_of(T.cores[r]):
-                pairs, helpers, direct = routes(T, topo, r)
-                if core in helpers:
-                    helper_program(g, core, T, topo, r, pairs[helpers.index(core)])
         return
 
     eng = {"v": g.vector, "a": g.scalar, "t": g.tensor, "g": g, "s": g.sync}
@@ -141,7 +100,7 @@ def rank_program(g, core, T, topo):
     count = {"sv": 0, "sa": 0, "st": 0, "sg": 0}
     recs = {}
     ndma = [0]
-    nrep = [0]
+    ntag = [0]
     ctx = ["a"]
 
     def need(e, toks):
@@ -163,13 +122,11 @@ def rank_program(g, core, T, topo):
             for (nm, lo, hi) in spans:
                 ps = SCRATCH[nm][0] == "psum"
                 for (l2, h2, w2, e2, tk, tg) in recs.get(nm, []):
-                    if tag is not None and tg == tag:
+                    if w and tag is not None and tg == tag:
                         continue
                     if ps and e2 != e:
                         toks.append(tk)
                     elif e == "t" and e2 == "t":
-                        continue
-                    elif not SAME and e == e2 and e in "va" and w:
                         continue
                     elif l2 < hi and lo < h2 and (w or w2):
                         toks.append(tk)
@@ -191,61 +148,103 @@ def rank_program(g, core, T, topo):
 
     ops = []
 
+    line = [False]
+    chain = {}
+    order = {}
+
     def later(e, reads, writes, dur, lag, fn, tag=None):
+        if line[0]:
+            if e in chain:
+                order[len(ops)] = chain[e]
+            chain[e] = len(ops)
         ops.append((e, reads, writes, dur, lag, fn, tag))
+
+    early = {}
+    marks = {}
+
+    def name(nm):
+        i = len(ops) - 1
+        early[i] = SOONER.get(nm, 0.0)
+        if AFTER.get(nm) in marks:
+            order[i] = marks[AFTER[nm]]
+        marks[nm] = i
 
     def issue():
         last = {}
         preds = []
+        soft = set()
         for i, (e, reads, writes, dur, lag, fn, tag) in enumerate(ops):
             p = set()
             for spans, w in ((reads, False), (writes, True)):
                 for (nm, lo, hi) in spans:
                     for (l2, h2, w2, j, tg) in last.get(nm, []):
-                        if l2 < hi and lo < h2 and (w or w2) and (tag is None or tg != tag):
+                        if l2 < hi and lo < h2 and (w or w2) and (not w or tag is None or tg != tag):
                             p.add(j)
             for (nm, lo, hi) in writes:
                 last[nm] = [x for x in last.get(nm, []) if not (lo <= x[0] and x[1] <= hi) or (tag is not None and x[4] == tag)] + [(lo, hi, True, i, tag)]
             for (nm, lo, hi) in reads:
                 last.setdefault(nm, []).append((lo, hi, False, i, None))
             p.discard(i)
+            if i in order and order[i] not in p:
+                p.add(order[i])
+                soft.add((order[i], i))
             preds.append(p)
         succ = [[] for _ in ops]
         for i, p in enumerate(preds):
             for j in p:
                 succ[j].append(i)
-        prio = [0.0] * len(ops)
+        banks = [sorted(set(nm for (nm, lo, hi) in o[1] + o[2] if SCRATCH[nm][0] == "psum")) for o in ops]
+
+        def gap(i, j):
+            return 0.0 if ops[i][0] == "t" and ops[j][0] == "t" or (i, j) in soft else ops[i][4] + LAT
+
+        def place(key, before, after, back):
+            left = [len(p) for p in before]
+            at = [0.0] * len(ops)
+            busy = {}
+            ready = [i for i in range(len(ops)) if not left[i]]
+            while ready:
+                i = min(ready, key=lambda k: (key[k], k))
+                ready.remove(i)
+                e, dur, s = ops[i][0], ops[i][3], at[i]
+                lanes = [(busy.setdefault(nm, []), LAT) for nm in banks[i]] + ([(busy.setdefault(e, []), 0.0)] if e != "x" else [])
+                moved = True
+                while moved:
+                    moved = False
+                    for taken, pad in lanes:
+                        for (lo, hi, e2) in reversed(taken):
+                            if hi + LONG < s:
+                                break
+                            if (not pad or e2 != e) and lo < s + dur + pad and s < hi + pad:
+                                s, moved = hi + pad, True
+                at[i] = s
+                for taken, pad in lanes:
+                    k = len(taken)
+                    while k and taken[k - 1][0] > s:
+                        k -= 1
+                    taken.insert(k, (s, s + dur, e))
+                for j in after[i]:
+                    at[j] = max(at[j], s + dur + (gap(j, i) if back else gap(i, j)))
+                    left[j] -= 1
+                    if not left[j]:
+                        ready.append(j)
+            return at
+
+        key = [0.0] * len(ops)
         for i in range(len(ops) - 1, -1, -1):
-            prio[i] = ops[i][3] + ops[i][4] + max([prio[j] + LAT for j in succ[i]] + [0.0])
-        left = [len(p) for p in preds]
-        at = [0.0] * len(ops)
-        free = {e: 0.0 for e in eng}
-        bank = {}
-        ready = [i for i in range(len(ops)) if not left[i]]
-        while ready:
-            def start(i):
-                s = max(at[i], free[ops[i][0]])
-                for (nm, lo, hi) in ops[i][1] + ops[i][2]:
-                    if nm in bank and bank[nm][0] != ops[i][0]:
-                        s = max(s, bank[nm][1])
-                return s
-            st = {i: start(i) for i in ready}
-            i = min(ready, key=lambda k: (st[k], -prio[k]))
-            rivals = [k for k in ready if ops[k][0] == ops[i][0] and st[k] < st[i] + HOLD * ops[i][3] and prio[k] > prio[i]]
-            if rivals:
-                i = max(rivals, key=lambda k: prio[k])
-            ready.remove(i)
-            e, reads, writes, dur, lag, fn, tag = ops[i]
-            free[e] = st[i] + dur
-            for (nm, lo, hi) in reads + writes:
-                if SCRATCH[nm][0] == "psum":
-                    bank[nm] = (e, st[i] + dur + LAT)
-            fn()
-            for j in succ[i]:
-                at[j] = max(at[j], st[i] + dur + lag + (0.0 if e == "t" and ops[j][0] == "t" else LAT))
-                left[j] -= 1
-                if not left[j]:
-                    ready.append(j)
+            key[i] = min([key[j] - gap(i, j) for j in succ[i]] + [0.0]) - ops[i][3]
+        best = None
+        for _ in range(PASSES):
+            for i in range(len(ops) - 1, -1, -1):
+                key[i] = min([key[i] - early.get(i, 0.0)] + [key[j] - gap(i, j) - ops[i][3] for j in succ[i]])
+            at = place(key, preds, succ, False)
+            end = max(at[i] + ops[i][3] + ops[i][4] for i in range(len(ops)))
+            if best is None or end < best[0]:
+                best = (end, at)
+            back = place([-at[i] - ops[i][3] for i in range(len(ops))], succ, preds, True)
+            key = [-back[i] - ops[i][3] for i in range(len(ops))]
+        for i in sorted(range(len(ops)), key=lambda k: (best[1][k], k)):
+            ops[i][5]()
 
     def col(j):
         return A("COL", j, j + 1)
@@ -258,9 +257,9 @@ def rank_program(g, core, T, topo):
         kinds = [SCRATCH[x[1][0]] for x in [out] + wide]
         n = out[3]
         if out[2]:
-            dur = 0.055 + 3.8 * CY * n
+            dur = 0.05 + SCA * CY * n
         elif wide and wide[0][2]:
-            dur = 0.055 + 1.5 * CY * n
+            dur = 0.06 + GAT * CY * n
         elif e == "g":
             dur = 0.17 + 2 * CY * n
         elif e == "a":
@@ -290,14 +289,16 @@ def rank_program(g, core, T, topo):
     def scan(out, d0, d1, init, op0, op1):
         emit("v", out, [d0, d1, init, op0, op1], g.vector.tensor_tensor_scan)
 
-    def mset(out, c):
-        emit("v", out, [c], g.vector.memset)
+    def mset(out, c, tag=None):
+        emit("v", out, [c], g.vector.memset, tag)
 
-    def act(out, a, f=AF.Identity, scale=1.0, bias=0.0):
-        if scale == 1.0 and bias == 0.0:
-            emit("a", out, [a], lambda o, i: g.scalar.activation(o, i, f))
+    def act(out, a, f=AF.Identity, scale=1.0, bias=0.0, tag=None):
+        if isinstance(bias, tuple):
+            emit("a", out, [a, bias], lambda o, i, b: g.scalar.activation(o, i, f, bias=b, scale=scale), tag)
+        elif scale == 1.0 and bias == 0.0:
+            emit("a", out, [a], lambda o, i: g.scalar.activation(o, i, f), tag)
         else:
-            emit("a", out, [a], lambda o, i: g.scalar.activation(o, i, f, bias=bias, scale=scale))
+            emit("a", out, [a], lambda o, i: g.scalar.activation(o, i, f, bias=bias, scale=scale), tag)
 
     def iota(out, pat, base=0, cm=0):
         if SCRATCH[out[1][0]][2] == "int32":
@@ -305,22 +306,28 @@ def rank_program(g, core, T, topo):
         else:
             emit("g", out, [], lambda o: g.iota(o, pat, base, cm, allow_small_or_imprecise_dtypes=True))
 
-    def mm(items, tr=False):
-        whole = not tr and not (items[0][3] and items[-1][4])
+    def copy(e, o, i, tag=None):
+        if e == "v":
+            emit(e, o, [i], g.vector.tensor_copy, tag)
+        elif e == "a":
+            emit(e, o, [i], lambda o, i: g.scalar.activation(o, i, AF.Copy), tag)
+        else:
+            n = o[3]
+            emit(e, o, [i], lambda o, i: g.affine_select(o, i, [[0, n]], OP.is_ge, 0.0, 0, 0), tag)
+
+    def mm(items, whole=False):
+        whole = whole or not (items[0][3] and items[-1][4])
         dur = sum(max(64, it[2][3]) * (4 if SCRATCH[it[1][1][0]][2] == "float32" else 1) for it in items) * CY / 2
         later("t", [x[1] for it in items for x in it[1:3]], [(it[0][1][0], 0, 512) if whole else it[0][1] for it in items], dur, 0.0,
-              lambda: mm_now(items, tr))
+              lambda: mm_now(items))
 
-    def mm_now(items, tr):
+    def mm_now(items):
         count["st"] += 1
         done = []
         for it in items:
             reads = [it[1][1], it[2][1]]
             need("t", deps("t", reads, [it[0][1]]))
-            if tr:
-                ins = g.tensor.transpose(it[0][0], it[1][0], it[2][0])
-            else:
-                ins = g.tensor.matmul(it[0][0], it[1][0], it[2][0], it[3], it[4])
+            ins = g.tensor.matmul(it[0][0], it[1][0], it[2][0], it[3], it[4])
             done.append((reads, it[0][1]))
         ins.then_inc(T.sem.st, 1)
         tk = ("st", count["st"], dict(known["t"]))
@@ -328,7 +335,7 @@ def rank_program(g, core, T, topo):
             note("t", reads, [w], tk)
 
     def dma(e, out_ap, in_ap, reads, writes, lag=2.5):
-        later(e, reads + [("ORD", 0, 1)], writes + ([("ORD", 0, 1)] if lag > 2.5 else []), 0.06, lag, lambda: dma_now(e, out_ap, in_ap, reads, writes))
+        later(e, reads, writes, 0.06, lag, lambda: dma_now(e, out_ap, in_ap, reads, writes))
 
     def dma_now(e, out_ap, in_ap, reads, writes):
         need(e, deps("d", reads, writes))
@@ -336,83 +343,69 @@ def rank_program(g, core, T, topo):
         ndma[0] += 1
         eng[e].dma_start(out_ap, in_ap).then_inc(T.sem[s], 16)
         count[s] = 16
-        tk = (s, 16, dict(known[e]))
-        note("d", reads, writes, tk)
-        return tk
+        note("d", reads, writes, (s, 16, dict(known[e])))
 
-    def conv(out, lw, src, strided, rot=0):
-        mm([(out, A(lw, 15 - (j + rot) % 16, 143 - (j + rot) % 16), A(src, j, 256, 16) if strided else A(src, 16 * j, 16 * j + 16), j == 0, j == 15)
+    def conv(out, lw, src, lo, n, strided=True, rot=0, first=True, last=True):
+        mm([(out, A(lw, 15 - (j + rot) % 16, 143 - (j + rot) % 16),
+             A(src, lo + j, lo + 16 * n, 16) if strided else A(src, lo + n * j, lo + n * j + n), first and j == 0, last and j == 15)
             for j in range(16)])
 
-    def xrep(x, e, k0, k1, new=False):
-        if new:
-            nrep[0] += 1
-        for k in range(k0, k1 if R0 else k0):
-            o, i = A("AB", Q + k, Q + 16 * R0, 16), A(x, 0, R0)
-            if e == "v":
-                emit(e, o, [i], g.vector.tensor_copy, nrep[0])
-            elif e == "a":
-                emit(e, o, [i], lambda o, i: g.scalar.activation(o, i, AF.Copy), nrep[0])
-            else:
-                emit(e, o, [i], lambda o, i: g.affine_select(o, i, [[0, R0]], OP.is_ge, 0.0, 0, 0), nrep[0])
-
-    def fill(nm, lo, hi, c):
+    def fill(nm, lo, hi, c, st=1, tag=None):
         while lo < hi:
-            n = min(272, hi - lo)
-            act(A(nm, lo, lo + n), A("IN", 0, n), scale=0.0, bias=c)
-            lo += n
+            n = min(272, (hi - lo + st - 1) // st)
+            act(A(nm, lo, min(hi, lo + n * st), st), A("IN", 0, n), scale=0.0, bias=c, tag=tag)
+            lo += n * st
 
-    pairs, helpers, direct = routes(T, topo, rank)
-    narr = arrivals(T, topo, rank)
+    def pieces(nm, ranks):
+        return [(nm, L * d, L * d + CAP) for d in ranks]
 
-    def exchange(x):
-        ln, lw = ("RQ", 256) if x % 2 == 0 else ("R2", 544)
-        later("g", [("SB" if x % 2 == 0 else "AW", 0, 256)], [(ln, lw * (x // 2) + 32 * s, lw * (x // 2) + 32 * s + 32) for s in range(N) if s != rank],
-              1.0, WAY, lambda: exchange_now(x))
+    plan = calls(rank)
 
-    def exchange_now(x):
-        t = x // 2
-        nm, w = "SB" if x % 2 == 0 else "AW", 32
-        need("g", deps("r", [(nm, 0, 256)], []))
-        ls = T.sem["ls%d" % x]
+    def source(x, d):
+        return ("SB", L * d, L * d + CAP) if x % 2 == 0 else ("AW", CAP * d, CAP * d + CAP)
+
+    def landing(x, s):
+        return ("RQ", L * (x // 2) + CAP * s, L * (x // 2) + CAP * s + CAP) if x % 2 == 0 else ("R2", L * s, L * s + CAP)
+
+    def exchange(x, i):
+        guard = [("R2", 0, N * L)] if x % 2 == 0 and i == 0 else []
+        lands = [landing(x, s) for s in (plan[0] if i == 0 else plan[1] + plan[2] if i == 2 else [])]
+        tok = ("ORD", 2 + 3 * x + i, 3 + 3 * x + i)
+        line[0] = True
+        later("g", [source(x, d) for d in plan[i]], guard + [tok], 0.3, 0.0, lambda: exchange_now(x, i, guard))
+        line[0] = False
+        ar = "ar%d" % (2 * x + min(i, 1))
+        later("x", [tok], lands, 0.0, WAY[i], lambda: note("r", [], lands, (ar, count[ar], {})))
+
+    def exchange_now(x, i, guard):
+        reads = [source(x, d) for d in plan[i]]
+        need("g", deps("r", reads, guard))
+        ls, ar = "ls%d" % (3 * x + i), "ar%d" % (2 * x + min(i, 1))
         trs = []
-        n = 0
-        for i, h in enumerate(helpers):
-            es = share(topo.engines(core, h), i, 2)
-            n += len(es)
-            d = pairs[i][0]
-            trs.append(transfer(topo, h, es, T.sem["ha%d" % x], T[nm][:, w * d:w * d + 2 * w], T.HB[:, 64 * x:64 * x + 64]))
-        if trs:
-            g.remote_dma_fused(trs, local_sem=ls)
-        for part in calls(direct):
-            trs = []
-            for i, d in enumerate(part):
-                es = share(topo.engines(core, T.cores[d]), i, len(part))
-                n += len(es)
-                trs.append(transfer(topo, T.cores[d], es, T.sem["ar%d" % x], T[nm][:, w * d:w * d + w], landing(T, x, rank)))
-            g.remote_dma_fused(trs, local_sem=ls)
-        count["ls%d" % x] = n
-        count["ar%d" % x] = narr
-        note("r", [(nm, 0, 256)], [], ("ls%d" % x, n, dict(known["g"])))
-        ln, lw = ("RQ", 256) if x % 2 == 0 else ("R2", 544)
-        for s in range(N):
-            if s != rank:
-                note("r", [], [(ln, lw * t + w * s, lw * t + w * s + w)], ("ar%d" % x, narr, {}))
+        for k, d in enumerate(plan[i]):
+            es = share(topo.engines(core, T.cores[d]), k, len(plan[i]))
+            count[ls] = count.get(ls, 0) + len(es)
+            (sn, sl, sh), (dn, dl, dh) = source(x, d), landing(x, rank)
+            trs.append(transfer(topo, T.cores[d], es, T.sem[ar], T[sn][:, sl:sh], T[dn][:, dl:dh]))
+        g.remote_dma_fused(trs, local_sem=T.sem[ls])
+        note("r", reads, [], (ls, count[ls], dict(known["g"])))
+        count[ar] = arrivals(T, topo, rank, min(i, 1))
 
     mset(A("WI"), 0)
-    dma("s", T.X0[:], T.xl[:], [], [("X0", 0, 256)])
+    line[0] = True
+    dma("s", T.XL[:], T.xl[:], [], [("XL", 0, 256)])
     dma("s", T.CO[:, 0:3], T.co[:], [], [("CO", 0, 8)])
-    dma("s", T.WI[0:128:16, :], T.wl[:], [], [("WI", 0, 256)])
-    dma("s", T.VI[:], T.vst[:], [], [("VI", 0, 128)])
-    dma("s", T.SI[:], T.hlp[:], [], [("SI", 0, B)], 7.0)
-    dma("s", T.GN[:], T.gen[:], [], [("GN", 0, Q)], 4.5)
-    dma("s", T.XT[:, 0:H], T.xst[:], [], [("XT", 0, H)], 2.6)
+    dma("s", T.SI[:], T.hlp[:], [], [("SI", 0, B)], LAGS[0])
+    dma("s", T.GN[:, 0:Q], T.gen[:], [], [("GN", 0, Q)], LAGS[1])
+    dma("s", T.WI[0:128:16, :], T.wl[:], [], [("WI", 0, 256)], LAGS[1])
+    dma("s", T.VI[:], T.vst[:], [], [("VI", 0, 128)], LAGS[1])
+    dma("s", T.XT[:, 0:H], T.xst[:], [], [("XT", 0, H)], LAGS[2])
+    line[0] = False
 
     iota(A("IP", 0, 1), [[0, 1]], 0, 1)
     iota(A("IN"), [[1, 272]])
     iota(A("BOF"), [[16, 8], [0, 16]])
     iota(A("NM"), [[0, 17], [1, 16]])
-    iota(A("U16"), [[16, 16]])
     iota(A("NE"), [[1, 128], [0, 16]], 0, -1)
     cp(col(0), A("IP", 0, 1))
     ts(A("IP", 1, 2), A("IP", 0, 1), 112, OP.bitwise_and)
@@ -420,397 +413,435 @@ def rank_program(g, core, T, topo):
     cp(A("COL", 1, 3), A("IP", 1, 3))
     ts(col(3), col(1), 15.0, OP.add)
     ts(col(4), col(2), 256.0, OP.mult)
-    ts(col(5), col(2), 32.0, OP.mult)
-    ts(col(20), col(2), 1.0, OP.add)
-    ts(col(16), col(2), 8.0, OP.is_ge, 0.5, OP.mult)
+    ts(col(5), col(2), 2.0, OP.mult)
     mset(A("C192"), 192.0)
     ts(A("BM"), A("IN", 0, 144), col(3), OP.is_equal)
     ts(A("ID"), A("IN", 0, 128), col(0), OP.is_equal)
     ts(A("BOF"), A("BOF"), col(1), OP.is_equal)
-    fill("AB", Q + 16 * R0, Q + 2048, 0.0)
-    mset(A("AB", Q + 2048, 2 * Q), 0.0)
     cp(A("BO"), A("BOF"))
     cp(A("COF", 0, 3), A("CO", 0, 3))
-    ts(A("QA"), A("X0"), 0.25, OP.mult, 191.625, OP.add)
+
+    def turn(out, src, f, scale, bias):
+        for lo in range(0, L, HL):
+            for e in range(2):
+                act(A(out, lo + 64 * e, lo + 64 * e + 64), A(src, lo + e, lo + HL, 2), f, scale, bias)
+    turn("X0", "XL", AF.Identity, 1.0, 0.0)
+    act(A("QA"), A("X0"), scale=0.25, bias=191.625)
     ts(A("LA"), A("BM"), A("COF", 1, 2), OP.mult)
-    ts(A("BN"), A("BO"), A("COF", 1, 2), OP.mult)
+    ts(A("BA"), A("BO"), A("COF", 1, 2), OP.mult)
     ts(A("BC"), A("BO"), A("COF", 2, 3), OP.mult)
-    mm([(A("P6", 0, 2), A("BN"), A("C192"), True, True), (A("P6", 2, 4), A("BC"), A("C192"), True, True)])
+    mm([(A("P6", 0, 2), A("BA"), A("C192"), True, True), (A("P6", 2, 4), A("BC"), A("C192"), True, True)])
     ts(A("LW"), A("BM"), A("COF", 0, 1), OP.mult, 32.0, OP.mult)
     ts(A("LC"), A("BM"), A("COF", 2, 3), OP.mult)
     cp(A("COL", 6, 8), A("P6", 1, 3))
+    ntag[0] += 1
+    fill("AB", 1, Q, 0.0, 2, ntag[0])
+    mset(A("AB", Q + 1, 2 * Q, 2), 0.0)
 
-    def constants_a():
-        ts(A("BASE"), A("U16"), col(4), OP.add)
-        cp(A("KP"), A("NM", 0, 256))
-        ts(A("RS"), A("NM", 0, 256), 0.0, OP.is_equal, BIG, OP.mult)
-        ts(A("OH"), A("IN", 0, 32), col(2), OP.is_equal)
+    def weights(out, base, spec):
+        for i, (k, w) in enumerate(spec):
+            ts(col(30 + min(i, 1)), col(2), float(k), OP.is_equal, float(w), OP.mult)
+            if i:
+                tt(col(30), col(30), col(31), OP.add)
+        ts(out, base, col(30), OP.mult)
+
+    def constants():
+        ts(A("NE"), A("NE"), 0.0, OP.is_equal, -1.0, OP.mult)
+        ts(A("KP", 0, 128), A("NM", 0, 128), 2.0, OP.mult)
+        ts(A("KP", 128, 256), A("NM", 0, 128), 2.0, OP.mult, 1.0, OP.add)
+        ts(col(21), col(5), 1.0, OP.add)
+        ts(A("LK"), A("BM"), col(21), OP.mult)
+        ts(A("BK", 256, 384), A("BO"), -4096.0, OP.mult)
+        ts(A("BK", 384, 512), A("ID"), 4 * BIG, OP.mult)
+        mset(A("GN", Q, Q + 16), 192.0)
+        iota(A("F1"), [[0, 2], [32, 8]])
+        ts(A("BASE"), A("F1"), col(4), OP.add)
+        ts(A("RS"), A("NM", 0, 256), 0.0, OP.is_equal, 4 * BIG, OP.mult)
+        ts(A("OH"), A("IN", 0, 32), col(5), OP.is_equal)
+        ts(col(16), col(2), 8.0, OP.is_ge, 0.5, OP.mult)
+        tt(col(17), col(16), col(2), OP.add)
+        fill("ONE", 0, 128, 1.0)
+        ts(A("DM"), A("ONE"), col(17), OP.mult, -1.0, OP.mult)
+        ts(A("LD"), A("BM"), col(4), OP.mult)
+        iota(A("F2"), [[128, 2], [1, 8]])
+        ts(col(8), col(2), 8.0, OP.mult)
+        ts(A("PERM"), A("F2"), col(8), OP.add)
+        cp(A("EXP"), A("IN", 0, 16))
         cp(A("BMF"), A("BM"))
         cp(A("TF"), A("WI"))
-        conv(A("P6", 0, 16), "BMF", "TF", True)
-        ts(A("D0"), A("NM", 0, 256), col(2), OP.is_equal)
-        ts(A("ND"), A("NM", 0, 256), col(2), OP.not_equal)
-        mset(A("VT"), 0.0)
-        ts(A("U512"), A("U16"), col(2), OP.add, 272.0, OP.add)
-        ts(A("U2048"), A("U16"), col(2), OP.add, 2048.0, OP.add)
-        cp(A("EXP"), A("IN", 0, 16))
-        ts(A("LD"), A("BM"), col(5), OP.mult)
-        fill("ONE", 0, 256, 1.0)
-        fill("C33", 0, 256, 33.0)
-        fill("SB", 0, 256, -8.0)
-        fill("WS", 0, 256, 0.0)
-        for t in range(TR):
-            fill("R2", 544 * t + 256, 544 * t + 528, -1.0)
+        conv(A("P7", 0, 16), "BMF", "TF", 0, 16)
+        cp(A("WN"), A("P7", 0, 16))
+        ts(A("D0"), A("NM"), col(2), OP.is_equal)
+        ts(A("ND"), A("NM"), col(2), OP.not_equal)
+        ts(A("MB", 0, 256), A("ND", 0, 256), BIG, OP.mult)
+        ts(A("MB", 256, 512), A("ND", 0, 256), BIG, OP.mult, 4096.0, OP.add)
+        cp(A("IDF"), A("ID"))
+        iota(A("RU"), [[16, 16], [0, 16]], B + 1)
+        ts(A("TF"), A("NM", 0, 256), 0.0, OP.not_equal, -BIG, OP.mult)
+        ts(A("RU"), A("RU"), col(2), OP.add)
+        tt(A("RU"), A("RU"), A("TF"), OP.add)
+        ts(A("BK", 0, 128), A("BO"), 4096.0, OP.mult)
+        ts(A("NG", 0, 128), A("IN", 0, 128), col(0), OP.is_gt)
+        tt(A("NG", 128, 256), A("NG", 0, 128), A("ID"), OP.subtract)
+        tt(A("BK", 128, 256), A("NG", 128, 256), A("BK", 0, 128), OP.mult)
+        for d in range(N):
+            iota(A("SB", L * d, L * d + CAP), [[0, CAP]], -8)
+            iota(A("WS", L * d, L * d + CAP), [[0, CAP]], 0)
         iota(A("IO"), [[1, 2048]], 1)
-
-    def constants_c():
+        iota(A("R2"), [[0, N * L]], -1)
+        mset(A("TW"), 0.0)
+        iota(A("TH"), [[1, 4], [0, 64]])
+        iota(A("AQ"), [[0, 4], [1, 64]])
+        ts(col(9), col(2), 4.0, OP.mult)
+        ts(A("TH"), A("TH"), col(9), OP.add)
+        dma("s", T.TW[0:128:16, :], T.TH[:], [("TH", 0, 256)], [("TW", 0, Q)])
+        dma("s", T.TW[1:128:16, :], T.AQ[:], [("AQ", 0, 256)], [("TW", 0, Q)])
+        weights(col(10), col(2), [(2, 127.5), (3, 85.0)])
+        ts(A("VT", 0, H), A("NE"), 0.0, OP.mult, col(10), OP.add)
         ts(A("VJ", 0, 128), A("VI"), 6, OP.arith_shift_right)
         ts(A("VJ", 128, 256), A("VI"), 63, OP.bitwise_and)
         cp(A("VH"), A("VJ"))
         dma("s", T.VT[0:128:16, 0:H], T.VH[:, 0:128], [("VH", 0, 128)], [("VT", 0, H)])
         dma("s", T.VT[1:128:16, 0:H], T.VH[:, 128:256], [("VH", 128, 256)], [("VT", 0, H)])
-        for j in (0, 2):
-            ts(col(23), col(2), float(j), OP.is_equal, 64.0, OP.mult)
-            ts(col(24), col(2), float(j + 1), OP.is_equal)
-            tt(col(21 + j // 2), col(23), col(24), OP.add)
-        ts(col(24), col(22), 0.0, OP.is_gt)
-        ts(col(25), col(0), -2.0, OP.add)
-        ts(col(26), col(2), 0.0, OP.is_equal)
-        ts(A("LR"), A("BM"), col(21), OP.mult)
-        ts(A("L0"), A("BM"), col(26), OP.mult)
-
-    def constants_d():
-        for j in (2, 3):
-            ts(A("DQ", 0, 128), A("NM", 0, 128), float(j), OP.is_equal)
-            tt(A("MX", 128 * j - 256, 128 * j - 128), A("DQ", 0, 128), A("BO"), OP.mult)
-        ts(A("MX", 256, 384), A("IN", 0, 128), col(25), OP.is_equal, col(24), OP.mult)
-
-    def constants_e():
-        ts(A("MX", 384, 512), A("BO"), col(21), OP.mult)
-        ts(A("MX", 512, 640), A("BO"), col(22), OP.mult)
-        ts(A("MX", 640, 768), A("BO"), 64.0, OP.mult)
-        ts(A("DQ", 0, 128), A("NM", 0, 128), 2.0, OP.is_lt, -8192.0, OP.mult)
-        tt(A("BN"), A("DQ", 0, 128), A("BO"), OP.mult)
-
-    def constants_b():
-        ts(A("NE"), A("NE"), 0.0, OP.is_equal, -1.0, OP.mult)
-        cp(A("SF", 0, B), A("SI"))
-        tt(col(17), col(16), col(2), OP.add)
-        ts(A("THL"), A("ID"), 4096.0, OP.mult)
+        weights(A("LR"), A("BM"), [(0, 64), (1, 1)])
+        ts(A("MX", 256, 384), A("BO"), col(30), OP.mult)
+        weights(A("MX", 384, 512), A("BO"), [(2, 64), (3, 1)])
+        weights(A("LN"), A("BM"), [(0, 4096), (1, 4096), (4, -8192)])
+        weights(A("LU"), A("BM"), [(4, -1)])
+        ts(col(11), col(0), 2.0, OP.add)
+        ts(col(12), col(2), 2.0, OP.is_lt)
+        ts(A("MX", 0, 128), A("IN", 0, 128), col(11), OP.is_equal, col(12), OP.mult)
+        ts(col(13), col(0), -2.0, OP.add)
+        ts(col(14), col(10), 0.0, OP.is_gt)
+        ts(A("MX", 128, 256), A("IN", 0, 128), col(13), OP.is_equal, col(14), OP.mult)
+        ts(col(15), col(2), 0.0, OP.is_equal, 1.0 / 8192, OP.mult)
+        ts(A("XG", 0, 128), A("NM", 0, 128), 2.5, OP.subtract)
+        tt(A("XG", 128, 256), A("XG", 0, 128), A("XG", 0, 128), OP.mult)
+        ts(A("XG", 0, 128), A("XG", 128, 256), 1.0, OP.is_gt, 8192.0, OP.mult)
+        tt(A("BN", 0, 128), A("XG", 0, 128), A("BO"), OP.mult)
+        ts(A("BN", 128, 256), A("BN", 0, 128), -2.0, OP.mult)
+        ts(A("THL"), A("BN", 0, 128), col(15), OP.mult, 4096.0, OP.mult)
+        ts(A("XG", 0, 128), A("NM", 0, 128), 4.0, OP.is_equal, BIG, OP.mult)
+        tt(A("BN", 256, 384), A("XG", 0, 128), A("BO"), OP.mult)
+        ts(col(20), col(2), 1.0, OP.add)
         ts(A("KW"), A("BOF"), col(20), OP.mult)
-        ts(A("DM"), A("ONE"), col(17), OP.mult, -1.0, OP.mult)
-        cp(A("WN"), A("P6", 0, 16))
-        constants_c()
 
-    def round_constants(t):
-        if t == 0:
-            ts(col(27), col(2), 16.0, OP.add)
-            ts(A("I2", 0, 4), A("IN", 0, 4), -1.0, OP.mult, col(27), OP.add)
-            ts(A("I2", 4, 8), A("IN", 0, 4), col(2), OP.add)
-            ts(A("I3", 0, 8), A("I2", 0, 8), 15, OP.bitwise_and)
-            cp(A("COL", 8, 12), A("I3", 0, 4))
-            ts(A("COL", 12, 16), A("I3", 4, 8), col(1), OP.add)
-            ts(A("MB"), A("ND"), BIG, OP.mult)
-        ts(A("TRI", 256 * t, 256 * t + 256), A("NM", 0, 256), col(8 + t), OP.is_le, BIG, OP.mult)
-        if t:
-            ts(A("ROT", 128 * t - 128, 128 * t), A("IN", 0, 128), col(12 + t), OP.is_equal)
-
-    def index(ps, c, bits, keep, out):
-        ts(A("I1"), ps, c, OP.subtract)
+    def index(ps, c, bits, keep, out, lo, hi):
+        ts(A("I1", lo, hi), ps, c, OP.subtract)
         if bits == 0:
-            ts(A(keep), A("I1"), B - 1, OP.bitwise_and)
+            ts(A(keep, lo, hi), A("I1", lo, hi), B - 1, OP.bitwise_and)
         else:
-            ts(A(keep), A("I1"), bits, OP.arith_shift_right, H - 1, OP.bitwise_and)
-        cp(A(out), A(keep))
+            ts(A(keep, lo, hi), A("I1", lo, hi), bits, OP.arith_shift_right, H - 1, OP.bitwise_and)
+        cp(A(out, lo, hi), A(keep, lo, hi))
 
-    def prep_side(x):
-        mm([(A("PT", 128, 256), A(x, 128, 256), A("ID"))], tr=True)
-        act(A("XTR", 128, 256), A("PT", 128, 256))
-        conv(A("P1", 0, 16), "LW", x, False)
-        act(A("AB", Q + 16 * R0 + 15, 2 * Q, 16), A(x, R0, 256))
-        act(A("OWN"), A("P1", 0, 16), bias=-1.0)
+    tags = {}
 
-    def step(table, xn, qn, ak, head, tail):
-        cp(A("HS", 128, 192), IX(A(table, 0, B), A("BOF1", 8, 12)))
-        cp(A("HS", 192, 256), IX(A(table, 0, B), A("BOF1", 12, 16)))
-        cp(A("HS", 0, 128), IX(A(table, 0, B), A("BOF1", 0, 8)))
-        head()
-        mm([(A("P2", 0, 256), A("ID"), A("KP"), True, False)])
+    nsub = [0]
 
-        def score(l0, n, last):
-            js = list(range(l0 // 16, (l0 + n) // 16))
-            mm([(A("P2", 0, 256), A("LW", 15 - j, 143 - j), A("AB", 256 * j, 256 * j + 256), False, last and j == js[-1]) for j in js])
+    def prep(h, x, q, bo, kind):
+        pb, lo = "P%d" % (4 + h), HL * h
+        if kind == 2:
+            conv(A(pb, 0, 8), "LA", q, lo, 8)
+            index(A(pb, 0, 8), col(6), 0, "I6", bo, 8 * h, 8 * h + 8)
+        elif h == 0:
+            conv(A(pb, 96, 112), "LA", q, 0, 16)
+            index(A(pb, 96, 112), col(6), 0, "I6", bo, 0, 16)
+            name("columns")
+        ntag[0] += 1
+        tags[h] = ntag[0]
+        if "x" in PIECES[kind][h]:
+            for k in range(16):
+                copy(REP[kind][k], A("XR", k, 16 * HL, 16), A(x, lo, lo + HL), tags[h])
+        else:
+            mm([(A(pb, 128, 256), A(x, lo, lo + HL), A("ID"), True, True)])
+            act(A("XTR", lo, lo + HL), A(pb, 128, 256))
+        conv(A(pb, 8, 16), "LW", x, lo, 8, False)
+        act(A("OWN", 8 * h, 8 * h + 8), A(pb, 8, 16), bias=-1.0)
+        copy(STAY, A("AB", Q * h + 31, Q * h + Q, 32), A(x, lo, lo + HL), tags[h])
 
-        def gather(i):
-            l0, n, e = PIECES[i]
-            off = A("HS", l0, l0 + n)
-            if l0 >= R0:
-                gg = A("GG", 16 * l0, 16 * (l0 + n))
-                (act if e == "a" else cp)(gg, IX(A("GN"), off))
-            else:
-                tt(A("DD", 16 * l0, 16 * (l0 + n)), IX(A("GN"), off), A("AB", Q + 16 * l0, Q + 16 * (l0 + n)), OP.subtract)
-        early = [i for i, p in enumerate(PIECES) if p[2] == "a"]
-        for i in early:
-            gather(i)
-        prev = None
-        for i, (l0, n, e) in enumerate(PIECES):
-            if e != "a":
-                gather(i)
-            if l0 >= R0:
-                src = A(("P3", "P4")[i % 2], 0, 16 * n)
-                lo, h = 16 * (l0 % 128), 128 * (l0 // 128)
-                mm([(src, A("XTR", h, h + 128), A("NE", lo, lo + 16 * n), True, False), (src, A("ID"), A("GG", 16 * l0, 16 * (l0 + n)), False, True)])
-            else:
+    def scores(h, table, bo, kind, close):
+        ps, lo, c0, c1 = "P%d" % h, HL * h, 8 * h, 8 * h + 8
+        cp(A("HS", lo, lo + 64), IX(A(table, 0, B), A(bo, c0, c0 + 4)))
+        cp(A("HS", lo + 64, lo + HL), IX(A(table, 0, B), A(bo, c0 + 4, c1)))
+        mm([(A(ps, 0, HL), A("ID"), A("KP", 0, HL), True, False)])
+        parts = PIECES[kind][h]
+        n = HL // len(parts)
+        for i, e in enumerate(parts):
+            l0 = n * i
+            off = A("HS", lo + l0, lo + l0 + n)
+            line[0] = LINE[kind] and e != "a"
+            if e == "x":
                 src = A("DD", 16 * l0, 16 * (l0 + n))
-            if i == len(PIECES) - 1:
-                tail()
-            if prev is not None:
-                score(prev[0], prev[1], False)
-            act(A("AB", 16 * l0, 16 * (l0 + n)), src, AF.Abs)
-            prev = (l0, n)
-        score(prev[0], prev[1], True)
-        scan(A("SC"), A("RS"), A("P2", 0, 256), 0.0, OP.add, OP.min)
-        tt(A("I2"), A("SC", 15, 256, 16), A("OWN"), OP.min)
-        ts(A(ak), A("I2"), 31, OP.bitwise_and)
-        ts(A("F1"), A(ak), 16.0, OP.is_ge, 4080.0, OP.mult)
-        tt(A("F2"), A(ak), A("BASE"), OP.add)
-        tt(A("F3"), A("F1"), A("F2"), OP.add)
-        cp(A("OFX"), A("F3"))
-        ts(A(qn, 0, 128), IX(A("AB"), A("OFX", 0, 8)), 0.25, OP.mult, 191.625, OP.add)
-        act(A(qn, 128, 256), IX(A("AB"), A("OFX", 8, 16)), scale=0.25, bias=191.625)
-        if xn == "X1":
-            cp(A(xn, 0, 128), IX(A("AB"), A("OFX", 0, 8)))
-            act(A(xn, 128, 256), IX(A("AB"), A("OFX", 8, 16)))
+                tt(src, IX(A("GN", 0, Q), off), A("XR", 16 * l0, 16 * (l0 + n)), OP.subtract)
+                name("x%d" % kind)
+            else:
+                gg = A("GG", 16 * (lo + l0), 16 * (lo + l0 + n))
+                (act if e == "a" else cp)(gg, IX(A("GN", 0, Q), off))
+                name("%s%d" % (e, kind))
+                line[0] = False
+                nsub[0] += 1
+                src = A(("P2", "P3")[nsub[0] % 2], 0, 16 * n)
+                mm([(src, A("XTR", lo, lo + HL), A("NE", 16 * l0, 16 * (l0 + n)), True, False), (src, A("ID"), gg, False, True)])
+            line[0] = LINE[kind] > 1
+            act(A("AB", Q * h + 32 * l0, Q * h + 32 * (l0 + n), 2), src, AF.Abs, tag=tags[h])
+            line[0] = False
+            js = range(l0 // 8, (l0 + n) // 8)
+            mm([(A(ps, 0, HL), A("LW", 15 - j, 143 - j), A("AB", Q * h + 256 * j, Q * h + 256 * j + 256, 2), False, close and j == 15) for j in js], True)
+
+    def least(h, ak):
+        ps, lo, c0, c1 = "P%d" % h, HL * h, 8 * h, 8 * h + 8
+        scan(A("SC", lo, lo + HL), A("RS", 0, HL), A(ps, 0, HL), 0.0, OP.add, OP.min)
+        tt(A("I2", c0, c1), A("SC", lo + 15, lo + HL, 16), A("OWN", c0, c1), OP.min)
+        ts(A(ak, c0, c1), A("I2", c0, c1), 31, OP.bitwise_and)
+        tt(A("F1", c0, c1), A(ak, c0, c1), A("BASE", c0, c1), OP.add)
+
+    def take(h, place, xn, qn):
+        lo, c0, c1 = HL * h, 8 * h, 8 * h + 8
+        cp(A("OFX", c0, c1), A(place, c0, c1))
+        win = IX(A("AB", Q * h, Q * h + Q), A("OFX", c0, c1))
+        if TAKE[qn][h] == "v":
+            ts(A(qn, lo, lo + HL), win, 0.25, OP.mult, 191.625, OP.add)
         else:
-            act(A(xn), IX(A("AB"), A("OFX")))
+            act(A(qn, lo, lo + HL), win, scale=0.25, bias=191.625)
+        act(A(xn, lo, lo + HL), win)
 
-    def onehot(ak, a16, oh):
-        cp(A(a16), A(ak))
-        act(A(oh), IX(A("OH"), A(a16)))
+    def mend(h):
+        ps, pz, pb, lo, c0, c1 = "P%d" % h, ("P6", "P3")[h], "P%d" % (4 + h), HL * h, 8 * h, 8 * h + 8
+        new = IX(A("SF", 0, B), A("BO1", c0, c1))
+        mm([(A(pz, 0, HL), A("ID"), A("MB", 256, 256 + HL), True, False)])
+        tt(A("CH", lo, lo + HL), new, A("HO", lo, lo + HL), OP.not_equal)
+        tt(A("ZC", lo, lo + HL), new, A("CH", lo, lo + HL), OP.mult)
+        mm([(A(pz, 0, HL), A("BK", 256, 384), A("CH", lo, lo + HL), False, False)])
+        conv(A(pb, 48, 56), "LK", "CH", lo, 8, False)
+        mm([(A(pz, 0, HL), A("BOF"), A("ZC", lo, lo + HL), False, True)])
+        act(A("KT", c0, c1), A(pb, 48, 56))
+        act(A("KU", c0, c1), A(pb, 48, 56), bias=-1.0)
+        scan(A("SZ", lo, lo + HL), A("RS", 0, HL), A(pz, 0, HL), 0.0, OP.add, OP.min)
+        cp(A("ZO", c0, c1), A("SZ", lo + 15, lo + HL, 16))
+        tt(A("DN", lo, lo + HL), IX(A("GN"), A("ZO", c0, c1)), A("X0", lo, lo + HL), OP.subtract)
+        act(A("AB", Q * h + 29, Q * h + Q, 32), A("DN", lo, lo + HL), AF.Abs, tag=tags[h])
+        mm([(A(pb, 56, 64), A("LW", 15 - j, 143 - j), A("AB", Q * h + 256 * j + 29, Q * h + 256 * j + 256, 32), j == 0, j == 15) for j in range(16)])
+        tt(A("EK", lo, lo + HL), IX(A("KT", c0, c1), A("EXP", 0, 8)), A("KP", HL, 2 * HL), OP.is_equal)
+        mm([(A(ps, 0, HL), A("BK", 384, 512), A("EK", lo, lo + HL), False, True)])
+        least(h, "AKA")
+        tt(A("F2", c0, c1), A("I2", c0, c1), A("KT", c0, c1), OP.subtract)
+        ts(A("F3", c0, c1), A("AKA", c0, c1), -1.0, OP.mult, 29.0, OP.add)
+        tt(A("LT", c0, c1), A(pb, 56, 64), A("F2", c0, c1), OP.is_le)
+        tt(A("F4", c0, c1), A("LT", c0, c1), A("F3", c0, c1), OP.mult)
+        tt(A("F5", c0, c1), A("F4", c0, c1), A("F1", c0, c1), OP.add)
+        take(h, "F5", "X1", "QB")
 
-    def select(oh, bp, sel):
-        tt(A(sel), IX(A("SF", 0, B), A(bp)), A(oh), OP.mult)
+    def query(h):
+        ps, lo = "P%d" % h, HL * h
+        f = A(ps, 128, 256)
+        mm([(f, A("ID"), A("DM"), True, False), (f, A("BC"), A("QC", lo, lo + HL), False, True)])
+        ts(A("TF", lo, lo + HL), f, MAGIC, OP.add, MAGIC, OP.subtract)
+        tt(A("OW", lo, lo + HL), f, A("TF", lo, lo + HL), OP.is_equal)
+        conv(A(ps, 256, 264), "LD", "OW", lo, 8, last=False)
+        scan(A("CN", lo, lo + HL), A("ONE"), A("OW", lo, lo + HL), A("CN", lo - 1, lo) if h else -1.0, OP.mult, OP.add)
+        tt(A("VL", lo, lo + HL), A("OW", lo, lo + HL), A("CN", lo, lo + HL), OP.mult)
+        conv(A(ps, 256, 264), "BM", "VL", lo, 8, first=False)
+        cp(A("OFQ", 8 * h, 8 * h + 8), A(ps, 256, 264))
+        cp(IX(A("SB"), A("OFQ", 8 * h, 8 * h + 8)), A("X2", lo, lo + HL))
+        name("slots")
 
-    def new_word(ps):
-        tt(A("I3"), ps, A("WN"), OP.mult)
-        ts(A("F5"), ps, 37.0, OP.mult)
+    def diagonal(out, ps, src):
+        mm([(A(ps, 0, 256), A("ID"), A("MB", 0, 256), True, False), (A(ps, 0, 256), A("BOF"), A(src), False, True)])
+        scan(out, A("RS"), A(ps, 0, 256), 0.0, OP.add, OP.min)
+
+    def new_word(s):
+        tt(A("I3"), s, A("WN"), OP.mult)
+        act(A("F1"), s, scale=37.0)
         ts(A("I4"), A("I3"), 5, OP.arith_shift_right)
-        tt(A("F6"), A("F5"), A("WN"), OP.add)
-        tt(A("I5"), A("F6"), A("I4"), OP.add)
+        tt(A("F2"), A("F1"), A("WN"), OP.add)
+        tt(A("I5"), A("F2"), A("I4"), OP.add)
         ts(A("WN"), A("I5"), Q - 1, OP.bitwise_and)
 
-    def columns(c16, cd, t):
-        cc = A("CC2" if cd == "CDO" else "CC")
-        cp(A(c16), cc)
-        tt(A(cd), cc, A("TRI", 256 * t, 256 * t + 256), OP.add)
+    def key_columns(ps, off, cc, c16):
+        act(A(cc), IX(A("IO"), A(off)))
+        cp(A(c16), A(cc))
+        mm([(A(ps, 0, 256), A("ID"), A("MB", 256, 512), True, False), (A(ps, 0, 256), A("IDF"), A(cc), False, False)])
 
-    def first_of_key(key, c16, cd, rot, out, between):
-        ee, dc, pc, po = ("EF", "DC2", "P6", A("P0", 32, 48)) if key == "KO" else ("EE", "DC", "P5", A("P0", 0, 16))
-        tt(A(ee, 0, 256), IX(A(key), A("EXP")), A(cd), OP.is_equal)
-        mm([(A(pc, 0, 256), A("BO"), A(ee, 0, 256), True, False)])
-        pos = 256
-        for c in range(15):
-            lo = 16 * c + 16
-            e = A(ee, pos, pos + 256 - lo)
+    def first_of_key(ps, key, c16, ee, sk, out):
+        pos = 0
+        for c in range(16):
+            lo = 16 * c
+            ts(A(ee, pos, pos + 256 - lo), A(c16, lo, 256), A(key, c, c + 1), OP.is_equal)
+            mm([(A(ps, lo, lo + 16), A("BK", 128, 256), A(ee, pos, pos + 16), False, c == 15)]
+               + ([(A(ps, lo + 16, 256), A("BK", 0, 128), A(ee, pos + 16, pos + 256 - lo), False, False)] if c < 15 else []), True)
             pos += 256 - lo
-            ts(e, A(c16, lo, 256), A(key, c, c + 1), OP.is_equal)
-            mm([(A(pc, lo, 256), A("BO"), e, False, c == 14)])
-        act(A(dc), A(pc, 0, 256), scale=256.0)
-        conv(po, "BM", dc, True, rot)
-        ts(A("F7"), A(key), 0.0, OP.is_equal, 4096.0, OP.mult)
-        ts(A("F9"), A(key), -1.0, OP.add)
-        tt(A("F8"), A("F7"), A("F9"), OP.add)
-        between()
-        tt(A("F6"), A("F8"), po, OP.add)
-        tt(A("F5"), A("F6"), A("U2048"), OP.min)
-        cp(A(out), A("F5"))
+        scan(A("SK", sk, sk + 256), A("RU"), A(ps, 0, 256), 0.0, OP.max, OP.min)
+        ts(A(out), A("SK", sk + 15, sk + 256, 16), -1.0, OP.add)
 
-    def nothing():
-        pass
-
-    def prep_first(x, q):
-        xrep(x, "g", 0, 8, True)
-        prep_side(x)
-        xrep(x, "a", 8, 16)
-        conv(A("P3", 0, 16), "LA", q, True)
-        conv(A("P4", 0, 16), "LA", q, False)
-
-    def prep_index():
-        ctx[0] = "g"
-        index(A("P3", 0, 16), col(6), 0, "I6", "BOF1")
-        ctx[0] = "e"
-        index(A("P4", 0, 16), col(6), 0, "I6", "BP1")
-
-    def sums(out, weights, table, i0, i1):
-        for i in range(i0, i1):
-            p = A("P3" if i % 2 else "P4")
-            mm([(p, weights, A(table, 512 * i, 512 * i + 512), True, True)])
+    def sums(out, weight, table):
+        for i in range(4):
+            p = A("P2" if i % 2 else "P0")
+            mm([(p, weight, A(table, 512 * i, 512 * i + 512), True, True)])
+            name("sum")
             act(A(out, 512 * i, 512 * i + 512), p)
+            name("summed")
 
-    def store_words(t):
-        cp(IX(A("VT"), A("OFS")), A("RW"))
+    def owner(t, u):
+        hu = plan[0][0] // (N // 2) if u == 0 else rank // (N // 2)
+        lo, c0, c1 = HL * hu, 8 * hu, 8 * hu + 8
+        rq, pk, pi = A("RQ", L * t + lo, L * t + lo + HL), "P%d" % (6 + u), A("P%d" % (4 + u), 32, 40)
+        mm([(A(pk, 0, HL), A("THL"), A("ONE"), True, False)])
+        act(A("QQ", lo, lo + HL), rq, scale=0.25, bias=191.625)
+        conv(pi, "LC", "QQ", lo, 8)
+        act(A("NG", lo, lo + HL), rq, AF.Relu, scale=-1.0)
+        mm([(A(pk, 0, HL), A("BN", 0, 128), rq, False, False), (A(pk, 0, HL), A("BN", 256, 384), A("NG", lo, lo + HL), False, False)])
+        mm([(A(pk, CAP * i, CAP * i + CAP), A("MX", 0, 128), A("WS", L * (4 * hu + i), L * (4 * hu + i) + CAP), False, False) for i in range(4)])
+        index(pi, col(7), 3, "HI", "HOF", c0, c1)
+        off = A("HOF", c0, c1)
+        tt(A("MQ", lo, lo + HL), IX(A("XT", 0, H), off), rq, OP.max)
+        act(A("XG", lo, lo + HL), IX(A("XT", 0, H), off))
+        act(A("VG", lo, lo + HL), IX(A("VT", 0, H), off))
+        mm([(A(pk, 0, HL), A("BN", 128, 256), A("MQ", lo, lo + HL), False, False), (A(pk, 0, HL), A("BN", 0, 128), A("XG", lo, lo + HL), False, True)])
+        tt(A("AW", lo, lo + HL), A(pk, 0, HL), A("VG", lo, lo + HL), OP.min)
 
-    def store_items(t):
-        cp(IX(A("XT"), A("OFS")), A("RQ", 256 * t, 256 * t + 256))
-
-    prep_first("X0", "QA")
-    prep_index()
-    constants_a()
-    round_constants(0)
+    constants()
+    ctx[0] = "a"
+    for h in range(2):
+        prep(h, "X0", "QA", "BO1", 0)
 
     for t in range(TR):
         last = t == TR - 1
+        table = "SF" if t else "SI"
         ctx[0] = "a"
-        step("SF" if t else "SI", "X1", "QB", "AK1", nothing if t else constants_b, (lambda: store_items(t - 1)) if t else constants_d)
-        conv(A("P0", 0, 16), "LA", "QB", True)
-        xrep("X1", "g", 0, 8, True)
-        xrep("X1", "v", 8, 15)
-        prep_side("X1")
-        xrep("X1", "a", 15, 16)
-        conv(A("P1", 16, 32), "LA", "QB", False)
-        index(A("P0", 0, 16), col(6), 0, "I6", "BOF1")
-        step("SF", "X2", "QC", "AK2", nothing, (lambda: store_words(t - 1)) if t else constants_e)
-        mm([(A("P5", 0, 256), A("ID"), A("DM"), True, False), (A("P5", 0, 256), A("BC"), A("QC"), False, True)])
-        ctx[0] = "b"
-        onehot("AK1", "A1", "OH1")
-        onehot("AK2", "A2", "OH2")
-        ts(A("TF"), A("P5", 0, 256), MAGIC, OP.add, MAGIC, OP.subtract)
-        tt(A("OW"), A("P5", 0, 256), A("TF"), OP.is_equal)
-        conv(A("P6", 0, 16), "LD", "OW", True)
-        scan(A("CN"), A("OW"), A("C33"), 0.0, OP.add, OP.min)
-        tt(A("VL"), A("OW"), A("CN"), OP.mult)
-        conv(A("P0", 0, 16), "BM", "VL", True)
-        act(A("PA"), A("P6", 0, 16), bias=-1.0)
-        select("OH1", "BP1", "SEL1")
-        ts(A("F1"), A("P0", 0, 16), 33.0, OP.is_ge)
-        tt(A("EV"), A("P0", 0, 16), A("PA"), OP.add)
-        tt(A("F2"), A("F1"), A("U512"), OP.mult)
-        tt(A("F3"), A("F2"), A("EV"), OP.max)
-        cp(A("OFQ"), A("F3"))
-        cp(IX(A("SB", 0, 528), A("OFQ")), A("X2"))
-        exchange(2 * t)
-        act(A("RQ", 256 * t + 32 * rank, 256 * t + 32 * rank + 32), A("SB", 32 * rank, 32 * rank + 32))
-        conv(A("P6", 0, 16), "BMF", "SEL1", False)
-        ctx[0] = "c"
-        index(A("P1", 16, 32), col(6), 0, "BI", "BP2")
-        act(A("CC"), IX(A("IO"), A("BP2")))
-        select("OH2", "BP2", "SEL2")
-        mm([(A("P2", 0, 256), A("ID"), A("MB"), True, False), (A("P2", 0, 256), A("BOF"), A("SEL2"), False, True)])
-        columns("C16S", "CDS", t)
-        new_word(A("P6", 0, 16))
-        scan(A("SD"), A("RS"), A("P2", 0, 256), 0.0, OP.add, OP.min)
-        if last:
-            sums("YV", A("MX", 384, 512), "VT", 0, 4)
-        ctx[0] = "d"
-        new_word(A("SD", 15, 256, 16))
-        ts(A("WH"), A("WN"), 6, OP.arith_shift_right)
-        ts(A("WL"), A("WN"), 63, OP.bitwise_and)
-        cp(A("WU"), A("WN"))
-        tt(A("HD"), IX(A("WH"), A("EXP")), A("D0"), OP.mult)
-        tt(A("LO"), IX(A("WL"), A("EXP")), A("D0"), OP.mult)
-        mm([(A("P6", 0, 256), A("MX", 0, 128), A("HD"), True, False), (A("P6", 0, 256), A("MX", 128, 256), A("LO"), False, True)])
-        act(A("WP"), A("P6", 0, 256))
-        tt(A("JD"), IX(A("GN"), A("WU")), A("X2"), OP.subtract)
-        act(A("JD"), A("JD"), AF.Abs)
-        act(A("X0"), A("JD"), scale=-1.0, bias=63.0)
-        cp(A("WB", 0, 16), A("WN"))
-        ts(A("WB", 16, 32), A("BI"), 1.0, OP.add)
-        cp(IX(A("WS", 0, 528), A("OFQ")), A("WP"))
+        for h in range(2):
+            if t:
+                mend(h)
+            else:
+                scores(h, table, "BO1", 0, True)
+                least(h, "AK1")
+                take(h, "F1", "X1", "QB")
+            prep(h, "X1", "QB", "BO2", 2)
         if t:
-            mm([(A("P1", 64, 96), A("ROT", 128 * t - 128, 128 * t), A("WB"), True, True)])
-            act(A("WT"), A("P1", 64, 96))
-            wt = "WT"
-        else:
-            wt = "WB"
-        if not last:
-            act(A("QA"), A("X0"), scale=0.25, bias=191.625)
-            round_constants(t + 1)
+            tt(A("F2"), A("KU"), A("AKA"), OP.subtract)
+            tt(A("F3"), A("F2"), A("LT"), OP.mult)
+            tt(A("AK1"), A("F3"), A("AKA"), OP.add)
+        (act if t else cp)(A("HF"), IX(A(table, 0, B), A("BO1")))
+        ctx[0] = "d"
+        for h in range(2):
+            scores(h, table, "BO2", 2, True)
+            least(h, "AK2")
+            take(h, "F1", "X2", "QC")
+            query(h)
+        for i in range(3):
+            exchange(2 * t, i)
+        act(A("RQ", L * t + CAP * rank, L * t + CAP * rank + CAP), A("SB", L * rank, L * rank + CAP))
+        ctx[0] = "b"
+        cp(A("A1"), A("AK1"))
+        act(A("OH1"), IX(A("OH"), A("A1")))
+        tt(A("SEL1"), IX(A("HF"), A("PERM")), A("OH1"), OP.mult)
+        name("select")
+        act(A("SELP"), IX(A("SEL1"), A("PERM")))
+        diagonal(A("SD", 0, 256), "P6", "SELP")
+        new_word(A("SD", 15, 256, 16))
+        name("word")
+        ctx[0] = "c"
+        for h in range(2):
+            conv(A("P4", 16 + 8 * h, 24 + 8 * h), "LA", "QB", HL * h, 8, False)
+        index(A("P4", 16, 32), col(6), 0, "BI", "BP2", 0, 16)
+        cp(A("A2"), A("AK2"))
+        act(A("OH2"), IX(A("OH"), A("A2")))
+        tt(A("SEL2"), IX(A(table, 0, B), A("BP2")), A("OH2"), OP.mult)
+        diagonal(A("SD", 256, 512), "P7", "SEL2")
+        new_word(A("SD", 256 + 15, 512, 16))
+        cp(A("WU"), A("WN"))
+        act(A("WP"), IX(A("TW"), A("WU")))
+        tt(A("JD"), IX(A("GN", 0, Q), A("WU")), A("X2"), OP.subtract)
+        name("jump")
+        cp(IX(A("WS"), A("OFQ")), A("WP"))
+        name("words")
+        if t:
+            cp(IX(A("XT"), A("OFS")), A("RQ", L * t - L, L * t))
+            name("items")
+            cp(IX(A("VT"), A("OFS")), A("RW"))
+            name("stored")
+        ts(A("B1"), A("BI"), 1.0, OP.add)
+        if t == 0:
+            cp(A("SF", 0, B), A("SI"))
+        tt(A("HM"), IX(A("SF", 0, B), A("BP2")), A("ND", t, t + 256), OP.mult)
+        if t:
+            conv(A("P4", 64, 80), "LR", "WP", 0, 16, rot=t)
+            act(A("WT"), A("P4", 64, 80))
         if last:
+            act(A("JA"), A("JD"), AF.Abs)
+            act(A("X0"), A("JA"), scale=-1.0, bias=63.0)
             dma("s", T.yx[:], T.X0[:], [("X0", 0, 256)], [])
-            mm([(A("P6", 0, 256), A("MX", 640, 768), A("HD"), True, False), (A("P6", 0, 256), A("BO"), A("LO"), False, True)])
-            act(A("WC"), A("P6", 0, 256))
+            mm([(A("P1", 0, 256), A("MX", 256, 384), A("WP"), True, True)])
+            act(A("WC"), A("P1", 0, 256))
             dma("s", T.yw[:], T.WC[0:128:16, :], [("WC", 0, 256)], [])
-            sums("YH", A("KW"), "SF", 0, 2)
-        rq = A("RQ", 256 * t, 256 * t + 256)
-        ctx[0] = "e"
-        mm([(A("P5", 0, 256), A("THL"), A("ONE"), True, False)])
-        ts(A("QQ"), rq, 0.25, OP.mult, 191.625, OP.add)
-        conv(A("P0", 0, 16), "LC", "QQ", True)
-        ts(A("VD"), rq, 0.0, OP.is_lt, -BIG, OP.mult)
-        index(A("P0", 0, 16), col(7), 3, "HI", "HOF")
-        act(A("CC2"), IX(A("IO"), A("HOF")))
-        tt(A("DQ"), IX(A("XT", 0, H), A("HOF")), rq, OP.subtract)
-        act(A("AQ"), A("DQ"), AF.Abs)
-        mm([(A("P5", 0, 256), A("BN"), A("AQ"), False, True)])
-        tt(A("VG"), IX(A("VT", 0, H), A("HOF")), A("WS", 0, 256), OP.add)
-        tt(A("AW"), A("P5", 0, 256), A("VG"), OP.min)
-        exchange(2 * t + 1)
-        act(A("R2", 544 * t + 32 * rank, 544 * t + 32 * rank + 32), A("AW", 32 * rank, 32 * rank + 32))
-        tt(A("KN"), A("P5", 0, 256), A("VD"), OP.is_lt)
-        ctx[0] = "f"
-        conv(A("P0", 48, 64), "L0", "KN", True)
-        if not last:
-            emit("a", A("AQ"), [A("P5", 0, 256), col(18)], lambda o, i, s: g.scalar.activation(o, i, AF.Sign, accum_out=s), None, [col(18)])
-            prep_first("X0", "QA")
-        ts(A("BT"), A(wt, 16, 32), -1.0, OP.add)
-        ts(A("F1"), A("HI"), 1.0, OP.add)
-        columns("C16O", "CDO", 0)
-        tt(A("KO"), A("F1"), A("P0", 48, 64), OP.mult)
-
-        def count_known():
-            tt(A("HM"), IX(A("SF", 0, B), A("BT")), A("ND"), OP.mult)
-            if not last:
-                ts(A("IP", 3, 4), col(18), 0.5, OP.mult, 128.0, OP.add)
-                ts(A("IP", 4, 5), A("IP", 3, 4), 7, OP.bitwise_and)
-                ts(col(19), A("IP", 4, 5), 8192.0, OP.mult, 4096.0, OP.add)
-                ts(A("THL"), A("ID"), col(19), OP.mult)
-        first_of_key("KO", "C16O", "CDO", 0, "OFS", count_known)
-        if last:
-            sums("YH", A("KW"), "SF", 2, 4)
-            mm([(A("P3", 0, 256), A("KW"), A("HM"), True, False)])
-            store_items(t)
-            dma("s", T.ys[:], T.XT[:, 0:H], [("XT", 0, H)], [])
         else:
-            prep_index()
-            fill("SB", 0, 256, -8.0)
-        W, b1 = A(wt, 0, 16), A(wt, 16, 32)
-        mm([(A("P6", 0, 256), A("MX", 512, 640) if last else A("MX", 256, 384), A("R2", 544 * t, 544 * t + 256), True, True)])
-        cp(A("RG", 0, 128), IX(A("R2", 544 * t, 544 * t + 528), A("OFQ", 0, 8)))
-        act(A("RG", 128, 256), IX(A("R2", 544 * t, 544 * t + 528), A("OFQ", 8, 16)))
-        ret = A("P1", 32, 48)
+            turn("JA", "JD", AF.Abs, 1.0, 0.0)
+            act(A("QA"), A("JA"), scale=-0.25, bias=207.375)
+            act(A("X0"), A("JA"), scale=-1.0, bias=63.0)
+            ctx[0] = "g"
+            for h in range(2):
+                prep(h, "X0", "QA", "BO1", 1)
+            act(A("HO"), IX(A("SF", 0, B), A("BO1")))
+        ctx[0] = "e"
+        owner(t, 0)
+        exchange(2 * t + 1, 0)
+        owner(t, 1)
+        name("answered")
+        exchange(2 * t + 1, 1)
+        exchange(2 * t + 1, 2)
+        if not last:
+            for h in range(2):
+                scores(h, table, "BO1", 1, False)
+        act(A("R2", L * rank, L * rank + CAP), A("AW", CAP * rank, CAP * rank + CAP))
+        ctx[0] = "f"
+        rq = A("RQ", L * t, L * t + L)
+        key_columns("P6", "BP2", "CC", "C16S")
+        conv(A("P7", 256, 272), "LU", "AW", 0, 16)
+        ts(A("F1"), A("HI"), 1.0, OP.add)
+        tt(A("KO"), A("F1"), A("P7", 256, 272), OP.min)
+        key_columns("P7", "HOF", "CC2", "C16O")
+        first_of_key("P7", "KO", "C16O", "EF", 256, "OFS")
+        if last:
+            cp(IX(A("XT"), A("OFS")), rq)
+            name("last items")
+            dma("s", T.ys[:], T.XT[:, 0:H], [("XT", 0, H)], [])
+            sums("YH", A("KW"), "SF")
+            sums("YV", A("MX", 256, 384), "VT")
+            mm([(A("P3", 0, 256), A("KW"), A("HM"), True, False)])
+        else:
+            emit("a", A("AQ"), [A("AW"), col(18)], lambda o, i, s: g.scalar.activation(o, i, AF.Sign, bias=0.5, accum_out=s), None, [col(18)])
+            ts(A("IP", 3, 4), col(18), 0.5, OP.mult, 128.0, OP.add)
+            ts(A("IP", 4, 5), A("IP", 3, 4), 7, OP.bitwise_and)
+            ts(col(19), A("IP", 4, 5), 8192.0, OP.mult, 4096.0, OP.add)
+            ts(A("THL"), A("BN", 0, 128), col(19), OP.mult, col(15), OP.mult)
+            for d in range(N):
+                iota(A("SB", L * d, L * d + CAP), [[0, CAP]], -8)
         ctx[0] = "h"
-        conv(ret, "LR", "RG", True, t)
-        act(A("WC" if last else "RW"), A("P6", 0, 256))
-        tt(A("F1"), ret, W, OP.not_equal)
-        ts(A("F2"), ret, 0.0, OP.is_ge, 4096.0, OP.mult)
-        tt(A("F3"), A("F1"), b1, OP.mult)
-        tt(A("KY"), A("F3"), A("F2"), OP.min)
-
-        def new_column():
-            ctx[0] = "d"
-            ts(A("F1"), ret, 0.0, OP.max)
-            tt(A("I3"), A("F1"), W, OP.mult)
-            tt(A("F2"), A("F1"), W, OP.add)
-            ts(A("I4"), A("I3"), 5, OP.arith_shift_right)
-            tt(A("I5"), A("F2"), A("I4"), OP.add)
-            ts(A("ZI"), A("I5"), Q - 1, OP.bitwise_and)
-            ctx[0] = "h"
-            tt(A("ZD"), IX(A("ZI"), A("EXP")), A("D0"), OP.mult)
-            if last:
-                mm([(A("P3", 0, 256), A("KW"), A("ZD"), False, True)])
-                act(A("YC"), A("P3", 0, 256))
-
-        def last_words():
-            cp(IX(A("YV"), A("OFS")), A("WC"))
-            dma("a", T.yv[:], T.YV[0:128:16, 0:H], [("YV", 0, H)], [])
+        tt(A("NQ"), IX(A("R2"), A("OFQ")), A("WP"), OP.not_equal)
+        act(A("RG"), IX(A("R2"), A("OFQ")))
+        conv(A("P4", 80, 96), "LN", "NQ", 0, 16)
+        conv(A("P5", 80, 96), "LR", "RG", 0, 16, rot=t)
+        tt(A("KY"), A("B1"), A("P4", 80, 96), OP.min)
+        W = A("WT" if t else "WN")
+        act(A("F1"), A("P5", 80, 96), AF.Relu)
+        tt(A("I3"), A("F1"), W, OP.mult)
+        tt(A("F2"), A("F1"), W, OP.add)
+        ts(A("I4"), A("I3"), 5, OP.arith_shift_right)
+        tt(A("I5"), A("F2"), A("I4"), OP.add)
+        ts(A("ZI"), A("I5"), Q - 1, OP.bitwise_and)
+        tt(A("ZD"), IX(A("ZI"), A("EXP")), A("D0", t, t + 256), OP.mult)
+        first_of_key("P6", "KY", "C16S", "EE", 0, "OFH")
+        mm([(A("P7", L + CAP * s, L + CAP * s + CAP), A("MX", 384, 512) if last else A("MX", 128, 256), A("R2", L * s, L * s + CAP), True, True) for s in range(N)])
         if last:
-            new_column()
-        first_of_key("KY", "C16S", "CDS", t, "OFH", last_words if last else new_column)
-        if last:
+            mm([(A("P3", 0, 256), A("KW"), A("ZD"), False, True)])
+            act(A("YC"), A("P3", 0, 256))
+            act(A("WC"), A("P7", L, 2 * L))
             cp(IX(A("YH"), A("OFH")), A("YC"))
             dma("s", T.yh[:], T.YH[0:128:16, 0:B], [("YH", 0, B)], [])
+            cp(IX(A("YV"), A("OFS")), A("WC"))
+            dma("a", T.yv[:], T.YV[0:128:16, 0:H], [("YV", 0, H)], [])
         else:
             tt(IX(A("SF"), A("OFH")), A("ZD"), A("HM"), OP.add)
+            act(A("RW"), A("P7", L, 2 * L), bias=col(10))
     issue()
     for s, n in count.items():
         if n:

@@ -5,16 +5,23 @@ N, Q, B, H, L, CAP, TR = 8, 4096, 2048, 2048, 256, 32, 4
 BIG = 2.0 ** 22
 MAGIC = 1.5 * 2.0 ** 26
 HL = L // 2
-PIECES = {0: ("vava", "xxxx"), 1: ("avav", "avav"), 2: ("vava", "xxxx")}
-REP = {0: "vvvvvvvvaaaaaaaa", 1: "g" * 16, 2: "gggggggvvvvvvvvv"}
+PIECES = {0: ("vava", "xxxx"), 1: ("aava", "avav"), 2: ("vava", "xxxXX")}
+REP = {0: "vvvvvvvvaaaaaaaa", 1: "g" * 16, 2: "ggggvvvvvvvvvvva"}
 STAY = "g"
-TAKE = {"QB": "aa", "QC": "av"}
+TAKE = {"QB": "aa", "QC": "aa"}
 
 CY, LAT, WAY, HOLD = 0.83e-3, 0.2, (2.3, 2.5, 2.5), 1.0
 LINE = (1, 0, 1)
-PASSES, LONG = 1, 4.0
-SOONER = {"columns": 12.0, "words": 6.0, "items": 6.0, "stored": 6.0, "v1": 6.0, "a1": 6.0, "summed": 14.0, "last items": 5.0}
-AFTER = {"select": "x2", "jump": "slots", "words": "jump", "items": "words", "stored": "items", "v1": "answered", "sum": "slots"}
+PASSES, LONG, REACH, TIDY, PACE = 4000, 4.0, 8.0, 0.5, (1.0, 1.3)
+KEPT = {}
+EASE, TRIES, STEP = 0.02, 60, 4.0
+SQUEEZE = 0.0
+JOINT = False
+VIA = False
+WB = True
+JUMP = "a"
+SOONER = {"columns": 19.0, "words": 10.0, "items": 12.0, "stored": 12.0, "v1": 3.0, "a1": 3.0, "summed": 10.0, "last items": 5.0, "word": 4.0, "kept": 14.0, "z": 1.0, "yv": 2.0}
+AFTER = {"words": "slots", "v1": "answered"}
 GAT, SCA = 1.56, 3.8
 LAGS = (7.0, 11.5, 14.0)
 
@@ -35,12 +42,12 @@ def _decl(where, dtype, spec):
             PART[name] = (name, 0, int(cols))
 
 
-_decl("sbuf", "float32", "HO:256 ZC:256 SZ:256 KT:16 KU:16 LT:16")
-_decl("sbuf", "bfloat16", "CH:256 DN:256 EK:256 LK:144")
+_decl("sbuf", "float32", "HG:256 H2:256 HO:256 ZC:256 SZ:256 KT:16 KU:16 LT:16")
+_decl("sbuf", "bfloat16", "CH:256 DN:256 EK:256 LK:144 LOW:128 M1:8")
 _decl("sbuf", "int32", "AKA:16")
 _decl("sbuf", "uint16", "ZO:16")
 _decl("sbuf", "bfloat16", "GN:4112 TW:4096 XT:2304 VT:2304 XL:256 X0:256 X1:256 X2:256 QA:256 QB:256 QC:256 CO:8 AB:8192 XR:2048 DD:2048 "
-      "GG:4096 NE:2048 XTR:256 BM:144 LA:144 LC:144 LW:144 LD:144 LR:144 LN:144 LU:144 BO:128 BC:128 BA:128 BN:384 BK:512 ID:128 "
+      "GG:4096 NE:2048 XTR:256 BM:144 LA:144 LC:144 LW:144 LD:144 LR:144 LN:144 LU:144 BO:128 BC:128 BA:128 BN:384 BK:640 ID:128 "
       "THL:128 KP:256 DM:128 ONE:128 C192:2 OH:32 OH1:256 OH2:256 OW:256 CN:256 VL:256 SB:2048 WS:2048 R2:2048 AW:256 RQ:1024 QQ:256 "
       "XG:256 MQ:256 VG:256 NG:256 AQ:256 EE:2176 EF:2176 JD:256 JA:256 VH:256 TH:256 WP:256 RG:256 NQ:256 RW:256 MX:512 MB:512 ORD:32")
 _decl("sbuf", "float32", "SF:2304 YV:2304 YH:2304 IO:2048 IN:272 NM:272 D0:272 ND:272 RS:256 RU:256 KW:128 BMF:144 BOF:128 IDF:128 "
@@ -88,6 +95,90 @@ def arrivals(T, topo, d, part):
 def transfer(topo, dst, engines, sem, src_ap, dst_ap):
     rid, pid, _ = topo.addr(dst)
     return RemoteDMATransfer(dst_ids=[DstId(rid=rid, pnc=pid)], dma_engine_mask=_mask(engines), remote_sem=sem, src=src_ap, dst=dst_ap)
+
+
+def close_up(seq, eng, banks, kin, preds, paces, lag):
+    n = len(seq)
+    succ = [[] for _ in seq]
+    for i in range(n):
+        for j, _ in preds[i]:
+            succ[j].append(i)
+
+    def times(seq, dur):
+        fin, ready, why, free, last = [0.0] * n, [0.0] * n, [None] * n, {}, {}
+        for i in seq:
+            e = eng[i]
+            s, w = 0.0, None
+            for j, gp in preds[i]:
+                if fin[j] + gp >= s:
+                    s, w = fin[j] + gp, j
+            ready[i] = s
+            if e in free and free[e][0] > s:
+                s, w = free[e]
+            for b in banks[i]:
+                for e2, tj in last.setdefault(b, {}).items():
+                    if e2 != e and tj[0] > s:
+                        s, w = tj
+            fin[i] = s = s + dur[i]
+            why[i] = w
+            if e != "x":
+                free[e] = (s, i)
+            for b in banks[i]:
+                last[b][e] = (s + LAT, i)
+        i = max(range(n), key=lambda k: fin[k] + lag[k])
+        end, held = fin[i] + lag[i], []
+        while why[i] is not None:
+            if fin[i] - dur[i] > ready[i] + 0.02:
+                held.append((i, why[i]))
+            i = why[i]
+        return end + TIDY * sum(fin) / n, held, fin, ready
+
+    def worth(seq):
+        r = [times(seq, dur) for dur in paces]
+        return sum(x[0] / w for x, w in zip(r, PACE)), [p for x in r for p in x[1]], r[0][2], r[0][3]
+
+    def move(seq, i, j, ahead):
+        a, b = seq.index(j), seq.index(i)
+        if a >= b:
+            return seq
+        part = seq[a:b + 1]
+        took = {i if ahead else j}
+        for k in (reversed(part) if ahead else part):
+            if k in took:
+                took.update([x for x, _ in preds[k]] if ahead else succ[k])
+        if (j if ahead else i) in took:
+            return seq
+        one, two = [k for k in part if k in took], [k for k in part if k not in took]
+        return seq[:a] + (one + two if ahead else two + one) + seq[b + 1:]
+
+    dur = paces[0]
+    best, held, fin, ready = worth(seq)
+    r = 12345
+    for turn in range(PASSES):
+        r = (r * 6364136223846793005 + 1442695040888963407) % 2 ** 64
+        i, j = held[(r >> 40) % len(held)]
+        how = (r >> 33) % 5
+        if how == 0:
+            new = move(seq, i, j, True)
+        elif how == 1:
+            new = move(seq, i, j, False)
+        elif how == 2:
+            new = move(seq, i, [k for k in seq if eng[k] == eng[i] and fin[k] > ready[i]][0], True)
+        else:
+            if how == 4:
+                j = (r >> 20) % n
+            mine = [k for k in seq if eng[k] == eng[j] and ready[j] - 0.1 < fin[k] < fin[j] + REACH]
+            idle = [(a, b) for a, b in zip(mine, mine[1:]) if j not in (a, b) and fin[b] - dur[b] - max(fin[a], ready[j]) > 0.5 * dur[j]]
+            if not idle:
+                continue
+            a, b = idle[(r >> 12) % len(idle)]
+            new = move(seq, j, b, True) if fin[b] < fin[j] else move(seq, a, j, False)
+        if new is not seq:
+            value, h2, f2, r2 = worth(new)
+            if value <= best + EASE * (1.0 - turn / PASSES):
+                best, held, fin, ready = value, h2, f2, r2
+                seq = [k for _, _, k in sorted((fin[k] - dur[k], p, k) for p, k in enumerate(new))]
+    return seq
 
 
 def rank_program(g, core, T, topo):
@@ -155,18 +246,22 @@ def rank_program(g, core, T, topo):
     def later(e, reads, writes, dur, lag, fn, tag=None):
         if line[0]:
             if e in chain:
-                order[len(ops)] = chain[e]
+                order[len(ops)] = [chain[e]]
             chain[e] = len(ops)
         ops.append((e, reads, writes, dur, lag, fn, tag))
+        k = (e, ctx[0]) + tuple(x[0] if x[0][0] != "P" else x[:2] for x in writes[:1] + reads[:1])
+        seen[k] = seen.get(k, 0) + 1
+        kin.append(k + (seen[k],))
 
+    seen = {}
+    kin = []
     early = {}
     marks = {}
 
     def name(nm):
         i = len(ops) - 1
         early[i] = SOONER.get(nm, 0.0)
-        if AFTER.get(nm) in marks:
-            order[i] = marks[AFTER[nm]]
+        order[i] = order.get(i, []) + [marks[x] for x in AFTER.get(nm, "").split() if x in marks]
         marks[nm] = i
 
     def issue():
@@ -185,9 +280,10 @@ def rank_program(g, core, T, topo):
             for (nm, lo, hi) in reads:
                 last.setdefault(nm, []).append((lo, hi, False, i, None))
             p.discard(i)
-            if i in order and order[i] not in p:
-                p.add(order[i])
-                soft.add((order[i], i))
+            for j in order.get(i, []):
+                if j not in p:
+                    p.add(j)
+                    soft.add((j, i))
             preds.append(p)
         succ = [[] for _ in ops]
         for i, p in enumerate(preds):
@@ -215,7 +311,7 @@ def rank_program(g, core, T, topo):
                         for (lo, hi, e2) in reversed(taken):
                             if hi + LONG < s:
                                 break
-                            if (not pad or e2 != e) and lo < s + dur + pad and s < hi + pad:
+                            if (not pad or e2 != e) and lo < s + max(dur - SQUEEZE, min(dur, 0.02)) + pad and s < hi + pad:
                                 s, moved = hi + pad, True
                 at[i] = s
                 for taken, pad in lanes:
@@ -228,23 +324,66 @@ def rank_program(g, core, T, topo):
                     left[j] -= 1
                     if not left[j]:
                         ready.append(j)
+            free = {}
+            for i in sorted(range(len(ops)), key=lambda k: (at[k], k)):
+                e = ops[i][0]
+                at[i] = max([free.get(e, 0.0)] + [at[j] + ops[j][3] + gap(j, i) for j in before[i]]
+                            + [s for nm in banks[i] for e2, s in free.get(nm, {}).items() if e2 != e])
+                if e != "x":
+                    free[e] = at[i] + ops[i][3]
+                for nm in banks[i]:
+                    free.setdefault(nm, {})[e] = at[i] + ops[i][3] + LAT
             return at
 
         key = [0.0] * len(ops)
         for i in range(len(ops) - 1, -1, -1):
             key[i] = min([key[j] - gap(i, j) for j in succ[i]] + [0.0]) - ops[i][3]
-        best = None
-        for _ in range(PASSES):
-            for i in range(len(ops) - 1, -1, -1):
-                key[i] = min([key[i] - early.get(i, 0.0)] + [key[j] - gap(i, j) - ops[i][3] for j in succ[i]])
-            at = place(key, preds, succ, False)
-            end = max(at[i] + ops[i][3] + ops[i][4] for i in range(len(ops)))
-            if best is None or end < best[0]:
-                best = (end, at)
-            back = place([-at[i] - ops[i][3] for i in range(len(ops))], succ, preds, True)
-            key = [-back[i] - ops[i][3] for i in range(len(ops))]
-        for i in sorted(range(len(ops)), key=lambda k: (best[1][k], k)):
+        if not KEPT:
+            base, best, more = key, None, {}
+            for n in range(TRIES):
+                key = list(base)
+                for i in range(len(ops) - 1, -1, -1):
+                    key[i] = min([key[i] - early.get(i, 0.0) - max(0.0, more.get(kin[i], 0.0))] + [key[j] - gap(i, j) - ops[i][3] for j in succ[i]])
+                key = [key[i] - min(0.0, more.get(kin[i], 0.0)) for i in range(len(ops))]
+                at = place(key, preds, succ, False)
+                i = max(range(len(ops)), key=lambda k: at[k] + ops[k][3] + ops[k][4])
+                end = at[i] + ops[i][3] + ops[i][4]
+                if best is None or end <= best[0]:
+                    ends = {}
+                    for j in range(len(ops)):
+                        for nm, pad in [(ops[j][0], 0.0)] + [(b, LAT) for b in banks[j]]:
+                            ends[(nm, round(at[j] + ops[j][3] + pad, 4))] = j
+                    held = []
+                    while at[i] > 0:
+                        p = [j for j in preds[i] if at[j] + ops[j][3] + gap(j, i) > at[i] - 1e-4]
+                        if not p:
+                            p = [ends[(nm, round(at[i], 4))] for nm in [ops[i][0]] + banks[i] if ends.get((nm, round(at[i], 4)), i) != i]
+                            held.append((i, p[0]))
+                        i = p[0]
+                    best = (end, at, more, held, key)
+                i, j = best[3][n * 7919 // 3 % len(best[3])]
+                more = dict(best[2])
+                if n % 3 == 0:
+                    more[kin[i]] = more.get(kin[i], 0.0) + max(0.0, best[4][i] - best[4][j]) + 0.1
+                elif n % 3 == 1:
+                    more[kin[j]] = more.get(kin[j], 0.0) + STEP
+                else:
+                    more[kin[j]] = min(0.0, more.get(kin[j], 0.0)) - max(0.0, best[4][i] - best[4][j]) - 0.1
+            at = best[1]
+            seq = close_up(sorted(range(len(ops)), key=lambda k: (at[k], k)), [o[0] for o in ops], banks, kin,
+                           [[(j, gap(j, i)) for j in preds[i]] for i in range(len(ops))],
+                           [[o[3] * (1.0 if o[0] in "xs" or o[3] == 0.3 else f) for o in ops] for f in PACE], [o[4] for o in ops])
+            KEPT.update({i: n for n, i in enumerate(seq)})
+        left = [len(p) for p in preds]
+        ready = [i for i in range(len(ops)) if not left[i]]
+        while ready:
+            i = min(ready, key=lambda k: KEPT[k])
+            ready.remove(i)
             ops[i][5]()
+            for j in succ[i]:
+                left[j] -= 1
+                if not left[j]:
+                    ready.append(j)
 
     def col(j):
         return A("COL", j, j + 1)
@@ -396,17 +535,19 @@ def rank_program(g, core, T, topo):
     dma("s", T.XL[:], T.xl[:], [], [("XL", 0, 256)])
     dma("s", T.CO[:, 0:3], T.co[:], [], [("CO", 0, 8)])
     dma("s", T.SI[:], T.hlp[:], [], [("SI", 0, B)], LAGS[0])
+    dma("s", T.WI[0:128:16, :], T.wl[:], [], [("WI", 0, 256)], LAGS[0])
     dma("s", T.GN[:, 0:Q], T.gen[:], [], [("GN", 0, Q)], LAGS[1])
-    dma("s", T.WI[0:128:16, :], T.wl[:], [], [("WI", 0, 256)], LAGS[1])
     dma("s", T.VI[:], T.vst[:], [], [("VI", 0, 128)], LAGS[1])
     dma("s", T.XT[:, 0:H], T.xst[:], [], [("XT", 0, H)], LAGS[2])
-    line[0] = False
 
     iota(A("IP", 0, 1), [[0, 1]], 0, 1)
     iota(A("IN"), [[1, 272]])
-    iota(A("BOF"), [[16, 8], [0, 16]])
     iota(A("NM"), [[0, 17], [1, 16]])
+    iota(A("BOF"), [[16, 8], [0, 16]])
+    iota(A("F1"), [[0, 2], [32, 8]])
+    iota(A("F2"), [[128, 2], [1, 8]])
     iota(A("NE"), [[1, 128], [0, 16]], 0, -1)
+    line[0] = False
     cp(col(0), A("IP", 0, 1))
     ts(A("IP", 1, 2), A("IP", 0, 1), 112, OP.bitwise_and)
     ts(A("IP", 2, 3), A("IP", 0, 1), 15, OP.bitwise_and)
@@ -453,17 +594,18 @@ def rank_program(g, core, T, topo):
         ts(A("LK"), A("BM"), col(21), OP.mult)
         ts(A("BK", 256, 384), A("BO"), -4096.0, OP.mult)
         ts(A("BK", 384, 512), A("ID"), 4 * BIG, OP.mult)
+        ts(A("BK", 512, 640), A("ID"), -1.0, OP.mult)
         mset(A("GN", Q, Q + 16), 192.0)
-        iota(A("F1"), [[0, 2], [32, 8]])
         ts(A("BASE"), A("F1"), col(4), OP.add)
         ts(A("RS"), A("NM", 0, 256), 0.0, OP.is_equal, 4 * BIG, OP.mult)
         ts(A("OH"), A("IN", 0, 32), col(5), OP.is_equal)
-        ts(col(16), col(2), 8.0, OP.is_ge, 0.5, OP.mult)
-        tt(col(17), col(16), col(2), OP.add)
         fill("ONE", 0, 128, 1.0)
-        ts(A("DM"), A("ONE"), col(17), OP.mult, -1.0, OP.mult)
-        ts(A("LD"), A("BM"), col(4), OP.mult)
-        iota(A("F2"), [[128, 2], [1, 8]])
+        ts(A("DM"), A("ONE"), col(2), OP.mult, -1.0, OP.mult)
+        ts(col(16), col(2), 8.0, OP.is_lt)
+        ts(A("LOW"), A("ONE"), col(16), OP.mult)
+        ts(col(17), col(4), -2048.0, OP.add, col(16), OP.max)
+        ts(A("LD"), A("BM"), col(17), OP.mult)
+        mset(A("M1"), -1.0)
         ts(col(8), col(2), 8.0, OP.mult)
         ts(A("PERM"), A("F2"), col(8), OP.add)
         cp(A("EXP"), A("IN", 0, 16))
@@ -540,34 +682,44 @@ def rank_program(g, core, T, topo):
 
     def prep(h, x, q, bo, kind):
         pb, lo = "P%d" % (4 + h), HL * h
-        if kind == 2:
+        if kind == 2 and not JOINT:
             conv(A(pb, 0, 8), "LA", q, lo, 8)
             index(A(pb, 0, 8), col(6), 0, "I6", bo, 8 * h, 8 * h + 8)
+        elif kind == 2:
+            if h:
+                conv(A(pb, 96, 112), "LA", q, 0, 16)
+                index(A(pb, 96, 112), col(6), 0, "I6", bo, 0, 16)
         elif h == 0:
             conv(A(pb, 96, 112), "LA", q, 0, 16)
             index(A(pb, 96, 112), col(6), 0, "I6", bo, 0, 16)
             name("columns")
         ntag[0] += 1
         tags[h] = ntag[0]
-        if "x" in PIECES[kind][h]:
+        if "x" in PIECES[kind][h].lower():
             for k in range(16):
                 copy(REP[kind][k], A("XR", k, 16 * HL, 16), A(x, lo, lo + HL), tags[h])
         else:
             mm([(A(pb, 128, 256), A(x, lo, lo + HL), A("ID"), True, True)])
             act(A("XTR", lo, lo + HL), A(pb, 128, 256))
-        conv(A(pb, 8, 16), "LW", x, lo, 8, False)
-        act(A("OWN", 8 * h, 8 * h + 8), A(pb, 8, 16), bias=-1.0)
+        own = A("P%d" % h, 272, 280)
+        mm([(own, A("ID"), A("M1"), True, False)] + [(own, A("LW", 15 - j, 143 - j), A(x, lo + 8 * j, lo + 8 * j + 8), False, j == 15) for j in range(16)])
         copy(STAY, A("AB", Q * h + 31, Q * h + Q, 32), A(x, lo, lo + HL), tags[h])
 
     def scores(h, table, bo, kind, close):
         ps, lo, c0, c1 = "P%d" % h, HL * h, 8 * h, 8 * h + 8
-        cp(A("HS", lo, lo + 64), IX(A(table, 0, B), A(bo, c0, c0 + 4)))
-        cp(A("HS", lo + 64, lo + HL), IX(A(table, 0, B), A(bo, c0 + 4, c1)))
+        if kind == 2 and h == 0:
+            cp(A("HS", lo, lo + 64), IX(A(table, 0, B), A(bo, c0, c0 + 4)))
+            name("helpers")
+            cp(A("HS", lo + 64, lo + HL), IX(A(table, 0, B), A(bo, c0 + 4, c1)))
+        elif kind == 1:
+            act(A("HO", lo, lo + HL), IX(A("SF", 0, B), A(bo, c0, c1)))
+            cp(A("HS", lo, lo + HL), A("HO", lo, lo + HL) if table == "SF" and VIA else IX(A(table, 0, B), A(bo, c0, c1)))
+        else:
+            cp(A("HS", lo, lo + HL), IX(A(table, 0, B), A(bo, c0, c1)))
         mm([(A(ps, 0, HL), A("ID"), A("KP", 0, HL), True, False)])
-        parts = PIECES[kind][h]
-        n = HL // len(parts)
-        for i, e in enumerate(parts):
-            l0 = n * i
+        l0 = n = 0
+        for e in PIECES[kind][h]:
+            l0, n, e = l0 + n, 32 if e.islower() else 16, e.lower()
             off = A("HS", lo + l0, lo + l0 + n)
             line[0] = LINE[kind] and e != "a"
             if e == "x":
@@ -591,13 +743,14 @@ def rank_program(g, core, T, topo):
     def least(h, ak):
         ps, lo, c0, c1 = "P%d" % h, HL * h, 8 * h, 8 * h + 8
         scan(A("SC", lo, lo + HL), A("RS", 0, HL), A(ps, 0, HL), 0.0, OP.add, OP.min)
-        tt(A("I2", c0, c1), A("SC", lo + 15, lo + HL, 16), A("OWN", c0, c1), OP.min)
+        tt(A("I2", c0, c1), A("SC", lo + 15, lo + HL, 16), A(ps, 272, 280), OP.min)
         ts(A(ak, c0, c1), A("I2", c0, c1), 31, OP.bitwise_and)
         tt(A("F1", c0, c1), A(ak, c0, c1), A("BASE", c0, c1), OP.add)
 
     def take(h, place, xn, qn):
         lo, c0, c1 = HL * h, 8 * h, 8 * h + 8
         cp(A("OFX", c0, c1), A(place, c0, c1))
+        name("%s%d" % (xn, h))
         win = IX(A("AB", Q * h, Q * h + Q), A("OFX", c0, c1))
         if TAKE[qn][h] == "v":
             ts(A(qn, lo, lo + HL), win, 0.25, OP.mult, 191.625, OP.add)
@@ -612,8 +765,10 @@ def rank_program(g, core, T, topo):
         tt(A("CH", lo, lo + HL), new, A("HO", lo, lo + HL), OP.not_equal)
         tt(A("ZC", lo, lo + HL), new, A("CH", lo, lo + HL), OP.mult)
         mm([(A(pz, 0, HL), A("BK", 256, 384), A("CH", lo, lo + HL), False, False)])
-        conv(A(pb, 48, 56), "LK", "CH", lo, 8, False)
         mm([(A(pz, 0, HL), A("BOF"), A("ZC", lo, lo + HL), False, True)])
+        name("new z")
+        conv(A(pb, 48, 56), "LK", "CH", lo, 8, False)
+        name("new k")
         act(A("KT", c0, c1), A(pb, 48, 56))
         act(A("KU", c0, c1), A(pb, 48, 56), bias=-1.0)
         scan(A("SZ", lo, lo + HL), A("RS", 0, HL), A(pz, 0, HL), 0.0, OP.add, OP.min)
@@ -637,10 +792,9 @@ def rank_program(g, core, T, topo):
         mm([(f, A("ID"), A("DM"), True, False), (f, A("BC"), A("QC", lo, lo + HL), False, True)])
         ts(A("TF", lo, lo + HL), f, MAGIC, OP.add, MAGIC, OP.subtract)
         tt(A("OW", lo, lo + HL), f, A("TF", lo, lo + HL), OP.is_equal)
-        conv(A(ps, 256, 264), "LD", "OW", lo, 8, last=False)
-        scan(A("CN", lo, lo + HL), A("ONE"), A("OW", lo, lo + HL), A("CN", lo - 1, lo) if h else -1.0, OP.mult, OP.add)
+        scan(A("CN", lo, lo + HL), A("LOW"), A("OW", lo, lo + HL), A("CN", lo - 1, lo) if h else -1.0, OP.mult, OP.add)
         tt(A("VL", lo, lo + HL), A("OW", lo, lo + HL), A("CN", lo, lo + HL), OP.mult)
-        conv(A(ps, 256, 264), "BM", "VL", lo, 8, first=False)
+        conv(A(ps, 256, 264), "LD", "VL", lo, 8)
         cp(A("OFQ", 8 * h, 8 * h + 8), A(ps, 256, 264))
         cp(IX(A("SB"), A("OFQ", 8 * h, 8 * h + 8)), A("X2", lo, lo + HL))
         name("slots")
@@ -686,7 +840,8 @@ def rank_program(g, core, T, topo):
         lo, c0, c1 = HL * hu, 8 * hu, 8 * hu + 8
         rq, pk, pi = A("RQ", L * t + lo, L * t + lo + HL), "P%d" % (6 + u), A("P%d" % (4 + u), 32, 40)
         mm([(A(pk, 0, HL), A("THL"), A("ONE"), True, False)])
-        act(A("QQ", lo, lo + HL), rq, scale=0.25, bias=191.625)
+        ts(A("QQ", lo, lo + HL), rq, 0.25, OP.mult, 191.625, OP.add)
+        name("arrived%d" % u)
         conv(pi, "LC", "QQ", lo, 8)
         act(A("NG", lo, lo + HL), rq, AF.Relu, scale=-1.0)
         mm([(A(pk, 0, HL), A("BN", 0, 128), rq, False, False), (A(pk, 0, HL), A("BN", 256, 384), A("NG", lo, lo + HL), False, False)])
@@ -707,10 +862,15 @@ def rank_program(g, core, T, topo):
     for t in range(TR):
         last = t == TR - 1
         table = "SF" if t else "SI"
+        seen.clear()
         ctx[0] = "a"
         for h in range(2):
             if t:
                 mend(h)
+                name("mended%d" % h)
+                if h:
+                    cp(IX(A("XT"), A("OFS")), A("RQ", L * t - L, L * t))
+                    name("items")
             else:
                 scores(h, table, "BO1", 0, True)
                 least(h, "AK1")
@@ -732,11 +892,11 @@ def rank_program(g, core, T, topo):
         act(A("RQ", L * t + CAP * rank, L * t + CAP * rank + CAP), A("SB", L * rank, L * rank + CAP))
         ctx[0] = "b"
         cp(A("A1"), A("AK1"))
-        act(A("OH1"), IX(A("OH"), A("A1")))
-        tt(A("SEL1"), IX(A("HF"), A("PERM")), A("OH1"), OP.mult)
+        act(A("HG"), IX(A("HF"), A("PERM")))
+        tt(A("SEL1"), IX(A("OH"), A("A1")), A("HG"), OP.mult)
         name("select")
         act(A("SELP"), IX(A("SEL1"), A("PERM")))
-        diagonal(A("SD", 0, 256), "P6", "SELP")
+        diagonal(A("SD", 0, 256), "P6" if WB else "P2", "SELP")
         new_word(A("SD", 15, 256, 16))
         name("word")
         ctx[0] = "c"
@@ -744,19 +904,23 @@ def rank_program(g, core, T, topo):
             conv(A("P4", 16 + 8 * h, 24 + 8 * h), "LA", "QB", HL * h, 8, False)
         index(A("P4", 16, 32), col(6), 0, "BI", "BP2", 0, 16)
         cp(A("A2"), A("AK2"))
-        act(A("OH2"), IX(A("OH"), A("A2")))
-        tt(A("SEL2"), IX(A(table, 0, B), A("BP2")), A("OH2"), OP.mult)
-        diagonal(A("SD", 256, 512), "P7", "SEL2")
+        (act if t else cp)(A("H2"), IX(A(table, 0, B), A("BP2")))
+        tt(A("SEL2"), IX(A("OH"), A("A2")), A("H2"), OP.mult)
+        diagonal(A("SD", 256, 512), "P3", "SEL2")
         new_word(A("SD", 256 + 15, 512, 16))
         cp(A("WU"), A("WN"))
         act(A("WP"), IX(A("TW"), A("WU")))
-        tt(A("JD"), IX(A("GN", 0, Q), A("WU")), A("X2"), OP.subtract)
-        name("jump")
+        if JUMP == "v":
+            jd = "JD"
+            tt(A("JD"), IX(A("GN", 0, Q), A("WU")), A("X2"), OP.subtract)
+            name("jump")
+        else:
+            jd = "P2"
+            act(A("JD"), IX(A("GN", 0, Q), A("WU")))
+            mm([(A("P2", 0, L), A("BK", 512, 640), A("X2"), True, False), (A("P2", 0, L), A("ID"), A("JD"), False, True)])
         cp(IX(A("WS"), A("OFQ")), A("WP"))
         name("words")
         if t:
-            cp(IX(A("XT"), A("OFS")), A("RQ", L * t - L, L * t))
-            name("items")
             cp(IX(A("VT"), A("OFS")), A("RW"))
             name("stored")
         ts(A("B1"), A("BI"), 1.0, OP.add)
@@ -767,20 +931,19 @@ def rank_program(g, core, T, topo):
             conv(A("P4", 64, 80), "LR", "WP", 0, 16, rot=t)
             act(A("WT"), A("P4", 64, 80))
         if last:
-            act(A("JA"), A("JD"), AF.Abs)
+            act(A("JA"), A(jd, 0, L), AF.Abs)
             act(A("X0"), A("JA"), scale=-1.0, bias=63.0)
             dma("s", T.yx[:], T.X0[:], [("X0", 0, 256)], [])
             mm([(A("P1", 0, 256), A("MX", 256, 384), A("WP"), True, True)])
             act(A("WC"), A("P1", 0, 256))
             dma("s", T.yw[:], T.WC[0:128:16, :], [("WC", 0, 256)], [])
         else:
-            turn("JA", "JD", AF.Abs, 1.0, 0.0)
+            turn("JA", jd, AF.Abs, 1.0, 0.0)
             act(A("QA"), A("JA"), scale=-0.25, bias=207.375)
             act(A("X0"), A("JA"), scale=-1.0, bias=63.0)
             ctx[0] = "g"
             for h in range(2):
                 prep(h, "X0", "QA", "BO1", 1)
-            act(A("HO"), IX(A("SF", 0, B), A("BO1")))
         ctx[0] = "e"
         owner(t, 0)
         exchange(2 * t + 1, 0)
@@ -800,6 +963,7 @@ def rank_program(g, core, T, topo):
         tt(A("KO"), A("F1"), A("P7", 256, 272), OP.min)
         key_columns("P7", "HOF", "CC2", "C16O")
         first_of_key("P7", "KO", "C16O", "EF", 256, "OFS")
+        name("kept")
         if last:
             cp(IX(A("XT"), A("OFS")), rq)
             name("last items")
@@ -817,18 +981,19 @@ def rank_program(g, core, T, topo):
                 iota(A("SB", L * d, L * d + CAP), [[0, CAP]], -8)
         ctx[0] = "h"
         tt(A("NQ"), IX(A("R2"), A("OFQ")), A("WP"), OP.not_equal)
-        act(A("RG"), IX(A("R2"), A("OFQ")))
+        name("differs")
+        act(A("RG"), IX(A("R2"), A("OFQ")), AF.Relu)
         conv(A("P4", 80, 96), "LN", "NQ", 0, 16)
         conv(A("P5", 80, 96), "LR", "RG", 0, 16, rot=t)
         tt(A("KY"), A("B1"), A("P4", 80, 96), OP.min)
         W = A("WT" if t else "WN")
-        act(A("F1"), A("P5", 80, 96), AF.Relu)
-        tt(A("I3"), A("F1"), W, OP.mult)
-        tt(A("F2"), A("F1"), W, OP.add)
+        tt(A("I3"), A("P5", 80, 96), W, OP.mult)
+        tt(A("F2"), A("P5", 80, 96), W, OP.add)
         ts(A("I4"), A("I3"), 5, OP.arith_shift_right)
         tt(A("I5"), A("F2"), A("I4"), OP.add)
         ts(A("ZI"), A("I5"), Q - 1, OP.bitwise_and)
         tt(A("ZD"), IX(A("ZI"), A("EXP")), A("D0", t, t + 256), OP.mult)
+        name("z")
         first_of_key("P6", "KY", "C16S", "EE", 0, "OFH")
         mm([(A("P7", L + CAP * s, L + CAP * s + CAP), A("MX", 384, 512) if last else A("MX", 128, 256), A("R2", L * s, L * s + CAP), True, True) for s in range(N)])
         if last:
@@ -836,8 +1001,10 @@ def rank_program(g, core, T, topo):
             act(A("YC"), A("P3", 0, 256))
             act(A("WC"), A("P7", L, 2 * L))
             cp(IX(A("YH"), A("OFH")), A("YC"))
+            name("yh")
             dma("s", T.yh[:], T.YH[0:128:16, 0:B], [("YH", 0, B)], [])
             cp(IX(A("YV"), A("OFS")), A("WC"))
+            name("yv")
             dma("a", T.yv[:], T.YV[0:128:16, 0:H], [("YV", 0, H)], [])
         else:
             tt(IX(A("SF"), A("OFH")), A("ZD"), A("HM"), OP.add)

from concourse.bass import DstId, RemoteDMATransfer
from concourse.mybir import AluOpType as OP, ActivationFunctionType as AF

N, Q, B, H, L, CAP, TR = 8, 4096, 2048, 2048, 256, 32, 4
BIG = 2.0 ** 22
MAGIC = 1.5 * 2.0 ** 26
HL = L // 2
PIECES = {0: ("vava", "xxxx"), 1: ("aava", "avav"), 2: ("vava", "xxxXX")}
REP = {0: "vvvvvvvvaaaaaaaa", 1: "g" * 16, 2: "ggggvvvvvvvvvvva"}
STAY = "g"
TAKE = {"QB": "aa", "QC": "aa"}

CY, LAT, WAY, HOLD = 0.83e-3, 0.2, (2.3, 2.5, 2.5), 1.0
LINE = (1, 0, 1)
PASSES, LONG, REACH, TIDY, PACE = 4000, 4.0, 8.0, 0.5, (1.0, 1.3)
KEPT = {}
EASE, TRIES, STEP = 0.02, 60, 4.0
SQUEEZE = 0.0
JOINT = False
VIA = False
WB = True
JUMP = "a"
SOONER = {"columns": 19.0, "words": 10.0, "items": 12.0, "stored": 12.0, "v1": 3.0, "a1": 3.0, "summed": 10.0, "last items": 5.0, "word": 4.0, "kept": 14.0, "z": 1.0, "yv": 2.0}
AFTER = {"words": "slots", "v1": "answered"}
GAT, SCA = 1.56, 3.8
LAGS = (7.0, 11.5, 14.0)

SCRATCH = {}
PART = {}


def _decl(where, dtype, spec):
    for item in spec.split():
        name, cols = item.split(":")
        if int(cols) == 16:
            pool = "POOL_" + dtype
            used = SCRATCH[pool][1][1] if pool in SCRATCH else 0
            SCRATCH[pool] = (where, [128, used + 16], dtype)
            PART[name] = (pool, used, 16)
        else:
            SCRATCH[name] = (where, [128, int(cols)], dtype)
            PART[name] = (name, 0, int(cols))


_decl("sbuf", "float32", "HG:256 H2:256 HO:256 ZC:256 SZ:256 KT:16 KU:16 LT:16")
_decl("sbuf", "bfloat16", "CH:256 DN:256 EK:256 LK:144 LOW:128 M1:8")
_decl("sbuf", "int32", "AKA:16")
_decl("sbuf", "uint16", "ZO:16")
_decl("sbuf", "bfloat16", "GN:4112 TW:4096 XT:2304 VT:2304 XL:256 X0:256 X1:256 X2:256 QA:256 QB:256 QC:256 CO:8 AB:8192 XR:2048 DD:2048 "
      "GG:4096 NE:2048 XTR:256 BM:144 LA:144 LC:144 LW:144 LD:144 LR:144 LN:144 LU:144 BO:128 BC:128 BA:128 BN:384 BK:640 ID:128 "
      "THL:128 KP:256 DM:128 ONE:128 C192:2 OH:32 OH1:256 OH2:256 OW:256 CN:256 VL:256 SB:2048 WS:2048 R2:2048 AW:256 RQ:1024 QQ:256 "
      "XG:256 MQ:256 VG:256 NG:256 AQ:256 EE:2176 EF:2176 JD:256 JA:256 VH:256 TH:256 WP:256 RG:256 NQ:256 RW:256 MX:512 MB:512 ORD:32")
_decl("sbuf", "float32", "SF:2304 YV:2304 YH:2304 IO:2048 IN:272 NM:272 D0:272 ND:272 RS:256 RU:256 KW:128 BMF:144 BOF:128 IDF:128 "
      "COL:32 COF:4 BASE:16 SC:256 OWN:16 TF:256 HF:256 SEL1:256 SELP:256 SEL2:256 SD:512 SK:512 WT:16 B1:16 WC:256 CC:256 CC2:256 "
      "KY:16 KO:16 HM:256 ZD:256 YC:256")
_decl("sbuf", "int32", "SI:2048 VI:128 VJ:256 WI:256 IP:8 AK1:16 AK2:16 BI:16 HI:16 ZI:16 WN:16")
_decl("sbuf", "uint16", "HS:256 BO1:16 BO2:16 BP2:16 OFX:16 A1:16 A2:16 OFQ:16 HOF:16 OFS:16 OFH:16 WU:16 EXP:16 PERM:16 C16S:256 C16O:256")
TEMPS = "F1 F2 F3 F4 F5 I1 I2 I3 I4 I5 I6".split()
for _c in "abcdefgh":
    _decl("sbuf", "float32", " ".join(n + _c + ":16" for n in TEMPS if n[0] == "F"))
    _decl("sbuf", "int32", " ".join(n + _c + ":16" for n in TEMPS if n[0] == "I"))
_decl("psum", "float32", "P0:512 P1:512 P2:512 P3:512 P4:512 P5:512 P6:512 P7:512")

SEMAPHORES = (["sv", "sa", "st", "sg"] + ["d%d" % i for i in range(32)] + ["ls%d" % i for i in range(6 * TR)]
              + ["ar%d" % i for i in range(4 * TR)])


def _mask(engines):
    m = 0
    for e in engines:
        m |= 1 << e
    return m


def share(engines, i, n):
    return engines[i * len(engines) // n:(i + 1) * len(engines) // n]


def calls(r):
    half = N // 2
    lo = half * (r // half)
    own = [lo + (r - lo + i) % half for i in range(1, half)]
    return [[d for d in range(N) if not lo <= d < lo + half], own[:2], own[2:]]


def arrivals(T, topo, d, part):
    n = 0
    for r in range(N):
        for i, p in enumerate(calls(r)):
            if d in p and min(i, 1) == part:
                n += len(topo.engines(T.cores[r], T.cores[d])) // len(p)
    return n


def transfer(topo, dst, engines, sem, src_ap, dst_ap):
    rid, pid, _ = topo.addr(dst)
    return RemoteDMATransfer(dst_ids=[DstId(rid=rid, pnc=pid)], dma_engine_mask=_mask(engines), remote_sem=sem, src=src_ap, dst=dst_ap)


def close_up(seq, eng, banks, kin, preds, paces, lag):
    n = len(seq)
    succ = [[] for _ in seq]
    for i in range(n):
        for j, _ in preds[i]:
            succ[j].append(i)

    def times(seq, dur):
        fin, ready, why, free, last = [0.0] * n, [0.0] * n, [None] * n, {}, {}
        for i in seq:
            e = eng[i]
            s, w = 0.0, None
            for j, gp in preds[i]:
                if fin[j] + gp >= s:
                    s, w = fin[j] + gp, j
            ready[i] = s
            if e in free and free[e][0] > s:
                s, w = free[e]
            for b in banks[i]:
                for e2, tj in last.setdefault(b, {}).items():
                    if e2 != e and tj[0] > s:
                        s, w = tj
            fin[i] = s = s + dur[i]
            why[i] = w
            if e != "x":
                free[e] = (s, i)
            for b in banks[i]:
                last[b][e] = (s + LAT, i)
        i = max(range(n), key=lambda k: fin[k] + lag[k])
        end, held = fin[i] + lag[i], []
        while why[i] is not None:
            if fin[i] - dur[i] > ready[i] + 0.02:
                held.append((i, why[i]))
            i = why[i]
        return end + TIDY * sum(fin) / n, held, fin, ready

    def worth(seq):
        r = [times(seq, dur) for dur in paces]
        return sum(x[0] / w for x, w in zip(r, PACE)), [p for x in r for p in x[1]], r[0][2], r[0][3]

    def move(seq, i, j, ahead):
        a, b = seq.index(j), seq.index(i)
        if a >= b:
            return seq
        part = seq[a:b + 1]
        took = {i if ahead else j}
        for k in (reversed(part) if ahead else part):
            if k in took:
                took.update([x for x, _ in preds[k]] if ahead else succ[k])
        if (j if ahead else i) in took:
            return seq
        one, two = [k for k in part if k in took], [k for k in part if k not in took]
        return seq[:a] + (one + two if ahead else two + one) + seq[b + 1:]

    dur = paces[0]
    best, held, fin, ready = worth(seq)
    r = 12345
    for turn in range(PASSES):
        r = (r * 6364136223846793005 + 1442695040888963407) % 2 ** 64
        i, j = held[(r >> 40) % len(held)]
        how = (r >> 33) % 5
        if how == 0:
            new = move(seq, i, j, True)
        elif how == 1:
            new = move(seq, i, j, False)
        elif how == 2:
            new = move(seq, i, [k for k in seq if eng[k] == eng[i] and fin[k] > ready[i]][0], True)
        else:
            if how == 4:
                j = (r >> 20) % n
            mine = [k for k in seq if eng[k] == eng[j] and ready[j] - 0.1 < fin[k] < fin[j] + REACH]
            idle = [(a, b) for a, b in zip(mine, mine[1:]) if j not in (a, b) and fin[b] - dur[b] - max(fin[a], ready[j]) > 0.5 * dur[j]]
            if not idle:
                continue
            a, b = idle[(r >> 12) % len(idle)]
            new = move(seq, j, b, True) if fin[b] < fin[j] else move(seq, a, j, False)
        if new is not seq:
            value, h2, f2, r2 = worth(new)
            if value <= best + EASE * (1.0 - turn / PASSES):
                best, held, fin, ready = value, h2, f2, r2
                seq = [k for _, _, k in sorted((fin[k] - dur[k], p, k) for p, k in enumerate(new))]
    return seq


def rank_program(g, core, T, topo):
    rank = T.rank_of(core)
    if rank is None:
        return

    eng = {"v": g.vector, "a": g.scalar, "t": g.tensor, "g": g, "s": g.sync}
    known = {e: {} for e in eng}
    count = {"sv": 0, "sa": 0, "st": 0, "sg": 0}
    recs = {}
    ndma = [0]
    ntag = [0]
    ctx = ["a"]

    def need(e, toks):
        best = {}
        for tk in toks:
            if tk[0] not in best or best[tk[0]][1] < tk[1]:
                best[tk[0]] = tk
        for tk in sorted(best.values(), key=lambda k: -len(k[2])):
            if known[e].get(tk[0], 0) < tk[1]:
                eng[e].wait_ge(T.sem[tk[0]], tk[1])
                known[e][tk[0]] = tk[1]
                for s, val in tk[2].items():
                    if known[e].get(s, 0) < val:
                        known[e][s] = val

    def deps(e, reads, writes, tag=None):
        toks = []
        for spans, w in ((reads, False), (writes, True)):
            for (nm, lo, hi) in spans:
                ps = SCRATCH[nm][0] == "psum"
                for (l2, h2, w2, e2, tk, tg) in recs.get(nm, []):
                    if w and tag is not None and tg == tag:
                        continue
                    if ps and e2 != e:
                        toks.append(tk)
                    elif e == "t" and e2 == "t":
                        continue
                    elif l2 < hi and lo < h2 and (w or w2):
                        toks.append(tk)
        return toks

    def note(e, reads, writes, tk, tag=None):
        for (nm, lo, hi) in writes:
            recs[nm] = [x for x in recs.get(nm, []) if not (lo <= x[0] and x[1] <= hi) or (tag is not None and x[5] == tag)] + [(lo, hi, True, e, tk, tag)]
        for (nm, lo, hi) in reads:
            recs[nm] = [x for x in recs.get(nm, []) if not (x[3] == e and not x[2] and lo <= x[0] and x[1] <= hi)] + [(lo, hi, False, e, tk, None)]

    def A(nm, lo=0, hi=None, st=1):
        nm, base, cols = PART[nm + ctx[0] if nm in TEMPS else nm]
        lo, hi = base + lo, base + (cols if hi is None else hi)
        return (T[nm][:, lo:hi:st] if st != 1 else T[nm][:, lo:hi], (nm, lo, hi), [], (hi - lo + st - 1) // st)

    def IX(win, off):
        return (win[0].indirect(off[0]), win[1], [off[1]], 16 * off[3])

    ops = []

    line = [False]
    chain = {}
    order = {}

    def later(e, reads, writes, dur, lag, fn, tag=None):
        if line[0]:
            if e in chain:
                order[len(ops)] = [chain[e]]
            chain[e] = len(ops)
        ops.append((e, reads, writes, dur, lag, fn, tag))
        k = (e, ctx[0]) + tuple(x[0] if x[0][0] != "P" else x[:2] for x in writes[:1] + reads[:1])
        seen[k] = seen.get(k, 0) + 1
        kin.append(k + (seen[k],))

    seen = {}
    kin = []
    early = {}
    marks = {}

    def name(nm):
        i = len(ops) - 1
        early[i] = SOONER.get(nm, 0.0)
        order[i] = order.get(i, []) + [marks[x] for x in AFTER.get(nm, "").split() if x in marks]
        marks[nm] = i

    def issue():
        last = {}
        preds = []
        soft = set()
        for i, (e, reads, writes, dur, lag, fn, tag) in enumerate(ops):
            p = set()
            for spans, w in ((reads, False), (writes, True)):
                for (nm, lo, hi) in spans:
                    for (l2, h2, w2, j, tg) in last.get(nm, []):
                        if l2 < hi and lo < h2 and (w or w2) and (not w or tag is None or tg != tag):
                            p.add(j)
            for (nm, lo, hi) in writes:
                last[nm] = [x for x in last.get(nm, []) if not (lo <= x[0] and x[1] <= hi) or (tag is not None and x[4] == tag)] + [(lo, hi, True, i, tag)]
            for (nm, lo, hi) in reads:
                last.setdefault(nm, []).append((lo, hi, False, i, None))
            p.discard(i)
            for j in order.get(i, []):
                if j not in p:
                    p.add(j)
                    soft.add((j, i))
            preds.append(p)
        succ = [[] for _ in ops]
        for i, p in enumerate(preds):
            for j in p:
                succ[j].append(i)
        banks = [sorted(set(nm for (nm, lo, hi) in o[1] + o[2] if SCRATCH[nm][0] == "psum")) for o in ops]

        def gap(i, j):
            return 0.0 if ops[i][0] == "t" and ops[j][0] == "t" or (i, j) in soft else ops[i][4] + LAT

        def place(key, before, after, back):
            left = [len(p) for p in before]
            at = [0.0] * len(ops)
            busy = {}
            ready = [i for i in range(len(ops)) if not left[i]]
            while ready:
                i = min(ready, key=lambda k: (key[k], k))
                ready.remove(i)
                e, dur, s = ops[i][0], ops[i][3], at[i]
                lanes = [(busy.setdefault(nm, []), LAT) for nm in banks[i]] + ([(busy.setdefault(e, []), 0.0)] if e != "x" else [])
                moved = True
                while moved:
                    moved = False
                    for taken, pad in lanes:
                        for (lo, hi, e2) in reversed(taken):
                            if hi + LONG < s:
                                break
                            if (not pad or e2 != e) and lo < s + max(dur - SQUEEZE, min(dur, 0.02)) + pad and s < hi + pad:
                                s, moved = hi + pad, True
                at[i] = s
                for taken, pad in lanes:
                    k = len(taken)
                    while k and taken[k - 1][0] > s:
                        k -= 1
                    taken.insert(k, (s, s + dur, e))
                for j in after[i]:
                    at[j] = max(at[j], s + dur + (gap(j, i) if back else gap(i, j)))
                    left[j] -= 1
                    if not left[j]:
                        ready.append(j)
            free = {}
            for i in sorted(range(len(ops)), key=lambda k: (at[k], k)):
                e = ops[i][0]
                at[i] = max([free.get(e, 0.0)] + [at[j] + ops[j][3] + gap(j, i) for j in before[i]]
                            + [s for nm in banks[i] for e2, s in free.get(nm, {}).items() if e2 != e])
                if e != "x":
                    free[e] = at[i] + ops[i][3]
                for nm in banks[i]:
                    free.setdefault(nm, {})[e] = at[i] + ops[i][3] + LAT
            return at

        key = [0.0] * len(ops)
        for i in range(len(ops) - 1, -1, -1):
            key[i] = min([key[j] - gap(i, j) for j in succ[i]] + [0.0]) - ops[i][3]
        if not KEPT:
            base, best, more = key, None, {}
            for n in range(TRIES):
                key = list(base)
                for i in range(len(ops) - 1, -1, -1):
                    key[i] = min([key[i] - early.get(i, 0.0) - max(0.0, more.get(kin[i], 0.0))] + [key[j] - gap(i, j) - ops[i][3] for j in succ[i]])
                key = [key[i] - min(0.0, more.get(kin[i], 0.0)) for i in range(len(ops))]
                at = place(key, preds, succ, False)
                i = max(range(len(ops)), key=lambda k: at[k] + ops[k][3] + ops[k][4])
                end = at[i] + ops[i][3] + ops[i][4]
                if best is None or end <= best[0]:
                    ends = {}
                    for j in range(len(ops)):
                        for nm, pad in [(ops[j][0], 0.0)] + [(b, LAT) for b in banks[j]]:
                            ends[(nm, round(at[j] + ops[j][3] + pad, 4))] = j
                    held = []
                    while at[i] > 0:
                        p = [j for j in preds[i] if at[j] + ops[j][3] + gap(j, i) > at[i] - 1e-4]
                        if not p:
                            p = [ends[(nm, round(at[i], 4))] for nm in [ops[i][0]] + banks[i] if ends.get((nm, round(at[i], 4)), i) != i]
                            held.append((i, p[0]))
                        i = p[0]
                    best = (end, at, more, held, key)
                i, j = best[3][n * 7919 // 3 % len(best[3])]
                more = dict(best[2])
                if n % 3 == 0:
                    more[kin[i]] = more.get(kin[i], 0.0) + max(0.0, best[4][i] - best[4][j]) + 0.1
                elif n % 3 == 1:
                    more[kin[j]] = more.get(kin[j], 0.0) + STEP
                else:
                    more[kin[j]] = min(0.0, more.get(kin[j], 0.0)) - max(0.0, best[4][i] - best[4][j]) - 0.1
            at = best[1]
            seq = close_up(sorted(range(len(ops)), key=lambda k: (at[k], k)), [o[0] for o in ops], banks, kin,
                           [[(j, gap(j, i)) for j in preds[i]] for i in range(len(ops))],
                           [[o[3] * (1.0 if o[0] in "xs" or o[3] == 0.3 else f) for o in ops] for f in PACE], [o[4] for o in ops])
            KEPT.update({i: n for n, i in enumerate(seq)})
        left = [len(p) for p in preds]
        ready = [i for i in range(len(ops)) if not left[i]]
        while ready:
            i = min(ready, key=lambda k: KEPT[k])
            ready.remove(i)
            ops[i][5]()
            for j in succ[i]:
                left[j] -= 1
                if not left[j]:
                    ready.append(j)

    def col(j):
        return A("COL", j, j + 1)

    def emit(e, out, ins, fn, tag=None, more=()):
        aps = [x for x in ins if isinstance(x, tuple)]
        reads = [x[1] for x in aps] + [y for x in aps for y in x[2]] + out[2]
        writes = [out[1]] + [x[1] for x in more]
        wide = [x for x in aps if x[3] > 1]
        kinds = [SCRATCH[x[1][0]] for x in [out] + wide]
        n = out[3]
        if out[2]:
            dur = 0.05 + SCA * CY * n
        elif wide and wide[0][2]:
            dur = 0.06 + GAT * CY * n
        elif e == "g":
            dur = 0.17 + 2 * CY * n
        elif e == "a":
            dur = 0.06 + max(64, n) * CY
        elif len(wide) == 2 and len(ins) == 3:
            dur = max(64, n * (1 if "psum" in [k[0] for k in kinds[1:]] else 2)) * CY
        else:
            dur = max(64, n * (0.5 if all(k[2] in ("bfloat16", "uint16") for k in kinds) else 1)) * CY

        def go():
            need(e, deps(e, reads, writes, tag))
            s = "s" + e
            count[s] += 1
            fn(*[x[0] if isinstance(x, tuple) else x for x in [out] + ins]).then_inc(T.sem[s], 1)
            note(e, reads, writes, (s, count[s], dict(known[e])), tag)
        later(e, reads, writes, dur, 0.0, go, tag)

    def cp(out, a):
        emit("v", out, [a], g.vector.tensor_copy)

    def tt(out, a, b, op):
        emit("v", out, [a, b, op], g.vector.tensor_tensor)

    def ts(out, a, s1, op0, s2=None, op1=None):
        emit("v", out, [a, s1, s2, op0] + ([op1] if op1 is not None else []), g.vector.tensor_scalar)

    def scan(out, d0, d1, init, op0, op1):
        emit("v", out, [d0, d1, init, op0, op1], g.vector.tensor_tensor_scan)

    def mset(out, c, tag=None):
        emit("v", out, [c], g.vector.memset, tag)

    def act(out, a, f=AF.Identity, scale=1.0, bias=0.0, tag=None):
        if isinstance(bias, tuple):
            emit("a", out, [a, bias], lambda o, i, b: g.scalar.activation(o, i, f, bias=b, scale=scale), tag)
        elif scale == 1.0 and bias == 0.0:
            emit("a", out, [a], lambda o, i: g.scalar.activation(o, i, f), tag)
        else:
            emit("a", out, [a], lambda o, i: g.scalar.activation(o, i, f, bias=bias, scale=scale), tag)

    def iota(out, pat, base=0, cm=0):
        if SCRATCH[out[1][0]][2] == "int32":
            emit("g", out, [], lambda o: g.iota(o, pat, base, cm))
        else:
            emit("g", out, [], lambda o: g.iota(o, pat, base, cm, allow_small_or_imprecise_dtypes=True))

    def copy(e, o, i, tag=None):
        if e == "v":
            emit(e, o, [i], g.vector.tensor_copy, tag)
        elif e == "a":
            emit(e, o, [i], lambda o, i: g.scalar.activation(o, i, AF.Copy), tag)
        else:
            n = o[3]
            emit(e, o, [i], lambda o, i: g.affine_select(o, i, [[0, n]], OP.is_ge, 0.0, 0, 0), tag)

    def mm(items, whole=False):
        whole = whole or not (items[0][3] and items[-1][4])
        dur = sum(max(64, it[2][3]) * (4 if SCRATCH[it[1][1][0]][2] == "float32" else 1) for it in items) * CY / 2
        later("t", [x[1] for it in items for x in it[1:3]], [(it[0][1][0], 0, 512) if whole else it[0][1] for it in items], dur, 0.0,
              lambda: mm_now(items))

    def mm_now(items):
        count["st"] += 1
        done = []
        for it in items:
            reads = [it[1][1], it[2][1]]
            need("t", deps("t", reads, [it[0][1]]))
            ins = g.tensor.matmul(it[0][0], it[1][0], it[2][0], it[3], it[4])
            done.append((reads, it[0][1]))
        ins.then_inc(T.sem.st, 1)
        tk = ("st", count["st"], dict(known["t"]))
        for reads, w in done:
            note("t", reads, [w], tk)

    def dma(e, out_ap, in_ap, reads, writes, lag=2.5):
        later(e, reads, writes, 0.06, lag, lambda: dma_now(e, out_ap, in_ap, reads, writes))

    def dma_now(e, out_ap, in_ap, reads, writes):
        need(e, deps("d", reads, writes))
        s = "d%d" % ndma[0]
        ndma[0] += 1
        eng[e].dma_start(out_ap, in_ap).then_inc(T.sem[s], 16)
        count[s] = 16
        note("d", reads, writes, (s, 16, dict(known[e])))

    def conv(out, lw, src, lo, n, strided=True, rot=0, first=True, last=True):
        mm([(out, A(lw, 15 - (j + rot) % 16, 143 - (j + rot) % 16),
             A(src, lo + j, lo + 16 * n, 16) if strided else A(src, lo + n * j, lo + n * j + n), first and j == 0, last and j == 15)
            for j in range(16)])

    def fill(nm, lo, hi, c, st=1, tag=None):
        while lo < hi:
            n = min(272, (hi - lo + st - 1) // st)
            act(A(nm, lo, min(hi, lo + n * st), st), A("IN", 0, n), scale=0.0, bias=c, tag=tag)
            lo += n * st

    def pieces(nm, ranks):
        return [(nm, L * d, L * d + CAP) for d in ranks]

    plan = calls(rank)

    def source(x, d):
        return ("SB", L * d, L * d + CAP) if x % 2 == 0 else ("AW", CAP * d, CAP * d + CAP)

    def landing(x, s):
        return ("RQ", L * (x // 2) + CAP * s, L * (x // 2) + CAP * s + CAP) if x % 2 == 0 else ("R2", L * s, L * s + CAP)

    def exchange(x, i):
        guard = [("R2", 0, N * L)] if x % 2 == 0 and i == 0 else []
        lands = [landing(x, s) for s in (plan[0] if i == 0 else plan[1] + plan[2] if i == 2 else [])]
        tok = ("ORD", 2 + 3 * x + i, 3 + 3 * x + i)
        line[0] = True
        later("g", [source(x, d) for d in plan[i]], guard + [tok], 0.3, 0.0, lambda: exchange_now(x, i, guard))
        line[0] = False
        ar = "ar%d" % (2 * x + min(i, 1))
        later("x", [tok], lands, 0.0, WAY[i], lambda: note("r", [], lands, (ar, count[ar], {})))

    def exchange_now(x, i, guard):
        reads = [source(x, d) for d in plan[i]]
        need("g", deps("r", reads, guard))
        ls, ar = "ls%d" % (3 * x + i), "ar%d" % (2 * x + min(i, 1))
        trs = []
        for k, d in enumerate(plan[i]):
            es = share(topo.engines(core, T.cores[d]), k, len(plan[i]))
            count[ls] = count.get(ls, 0) + len(es)
            (sn, sl, sh), (dn, dl, dh) = source(x, d), landing(x, rank)
            trs.append(transfer(topo, T.cores[d], es, T.sem[ar], T[sn][:, sl:sh], T[dn][:, dl:dh]))
        g.remote_dma_fused(trs, local_sem=T.sem[ls])
        note("r", reads, [], (ls, count[ls], dict(known["g"])))
        count[ar] = arrivals(T, topo, rank, min(i, 1))

    mset(A("WI"), 0)
    line[0] = True
    dma("s", T.XL[:], T.xl[:], [], [("XL", 0, 256)])
    dma("s", T.CO[:, 0:3], T.co[:], [], [("CO", 0, 8)])
    dma("s", T.SI[:], T.hlp[:], [], [("SI", 0, B)], LAGS[0])
    dma("s", T.WI[0:128:16, :], T.wl[:], [], [("WI", 0, 256)], LAGS[0])
    dma("s", T.GN[:, 0:Q], T.gen[:], [], [("GN", 0, Q)], LAGS[1])
    dma("s", T.VI[:], T.vst[:], [], [("VI", 0, 128)], LAGS[1])
    dma("s", T.XT[:, 0:H], T.xst[:], [], [("XT", 0, H)], LAGS[2])

    iota(A("IP", 0, 1), [[0, 1]], 0, 1)
    iota(A("IN"), [[1, 272]])
    iota(A("NM"), [[0, 17], [1, 16]])
    iota(A("BOF"), [[16, 8], [0, 16]])
    iota(A("F1"), [[0, 2], [32, 8]])
    iota(A("F2"), [[128, 2], [1, 8]])
    iota(A("NE"), [[1, 128], [0, 16]], 0, -1)
    line[0] = False
    cp(col(0), A("IP", 0, 1))
    ts(A("IP", 1, 2), A("IP", 0, 1), 112, OP.bitwise_and)
    ts(A("IP", 2, 3), A("IP", 0, 1), 15, OP.bitwise_and)
    cp(A("COL", 1, 3), A("IP", 1, 3))
    ts(col(3), col(1), 15.0, OP.add)
    ts(col(4), col(2), 256.0, OP.mult)
    ts(col(5), col(2), 2.0, OP.mult)
    mset(A("C192"), 192.0)
    ts(A("BM"), A("IN", 0, 144), col(3), OP.is_equal)
    ts(A("ID"), A("IN", 0, 128), col(0), OP.is_equal)
    ts(A("BOF"), A("BOF"), col(1), OP.is_equal)
    cp(A("BO"), A("BOF"))
    cp(A("COF", 0, 3), A("CO", 0, 3))

    def turn(out, src, f, scale, bias):
        for lo in range(0, L, HL):
            for e in range(2):
                act(A(out, lo + 64 * e, lo + 64 * e + 64), A(src, lo + e, lo + HL, 2), f, scale, bias)
    turn("X0", "XL", AF.Identity, 1.0, 0.0)
    act(A("QA"), A("X0"), scale=0.25, bias=191.625)
    ts(A("LA"), A("BM"), A("COF", 1, 2), OP.mult)
    ts(A("BA"), A("BO"), A("COF", 1, 2), OP.mult)
    ts(A("BC"), A("BO"), A("COF", 2, 3), OP.mult)
    mm([(A("P6", 0, 2), A("BA"), A("C192"), True, True), (A("P6", 2, 4), A("BC"), A("C192"), True, True)])
    ts(A("LW"), A("BM"), A("COF", 0, 1), OP.mult, 32.0, OP.mult)
    ts(A("LC"), A("BM"), A("COF", 2, 3), OP.mult)
    cp(A("COL", 6, 8), A("P6", 1, 3))
    ntag[0] += 1
    fill("AB", 1, Q, 0.0, 2, ntag[0])
    mset(A("AB", Q + 1, 2 * Q, 2), 0.0)

    def weights(out, base, spec):
        for i, (k, w) in enumerate(spec):
            ts(col(30 + min(i, 1)), col(2), float(k), OP.is_equal, float(w), OP.mult)
            if i:
                tt(col(30), col(30), col(31), OP.add)
        ts(out, base, col(30), OP.mult)

    def constants():
        ts(A("NE"), A("NE"), 0.0, OP.is_equal, -1.0, OP.mult)
        ts(A("KP", 0, 128), A("NM", 0, 128), 2.0, OP.mult)
        ts(A("KP", 128, 256), A("NM", 0, 128), 2.0, OP.mult, 1.0, OP.add)
        ts(col(21), col(5), 1.0, OP.add)
        ts(A("LK"), A("BM"), col(21), OP.mult)
        ts(A("BK", 256, 384), A("BO"), -4096.0, OP.mult)
        ts(A("BK", 384, 512), A("ID"), 4 * BIG, OP.mult)
        ts(A("BK", 512, 640), A("ID"), -1.0, OP.mult)
        mset(A("GN", Q, Q + 16), 192.0)
        ts(A("BASE"), A("F1"), col(4), OP.add)
        ts(A("RS"), A("NM", 0, 256), 0.0, OP.is_equal, 4 * BIG, OP.mult)
        ts(A("OH"), A("IN", 0, 32), col(5), OP.is_equal)
        fill("ONE", 0, 128, 1.0)
        ts(A("DM"), A("ONE"), col(2), OP.mult, -1.0, OP.mult)
        ts(col(16), col(2), 8.0, OP.is_lt)
        ts(A("LOW"), A("ONE"), col(16), OP.mult)
        ts(col(17), col(4), -2048.0, OP.add, col(16), OP.max)
        ts(A("LD"), A("BM"), col(17), OP.mult)
        mset(A("M1"), -1.0)
        ts(col(8), col(2), 8.0, OP.mult)
        ts(A("PERM"), A("F2"), col(8), OP.add)
        cp(A("EXP"), A("IN", 0, 16))
        cp(A("BMF"), A("BM"))
        cp(A("TF"), A("WI"))
        conv(A("P7", 0, 16), "BMF", "TF", 0, 16)
        cp(A("WN"), A("P7", 0, 16))
        ts(A("D0"), A("NM"), col(2), OP.is_equal)
        ts(A("ND"), A("NM"), col(2), OP.not_equal)
        ts(A("MB", 0, 256), A("ND", 0, 256), BIG, OP.mult)
        ts(A("MB", 256, 512), A("ND", 0, 256), BIG, OP.mult, 4096.0, OP.add)
        cp(A("IDF"), A("ID"))
        iota(A("RU"), [[16, 16], [0, 16]], B + 1)
        ts(A("TF"), A("NM", 0, 256), 0.0, OP.not_equal, -BIG, OP.mult)
        ts(A("RU"), A("RU"), col(2), OP.add)
        tt(A("RU"), A("RU"), A("TF"), OP.add)
        ts(A("BK", 0, 128), A("BO"), 4096.0, OP.mult)
        ts(A("NG", 0, 128), A("IN", 0, 128), col(0), OP.is_gt)
        tt(A("NG", 128, 256), A("NG", 0, 128), A("ID"), OP.subtract)
        tt(A("BK", 128, 256), A("NG", 128, 256), A("BK", 0, 128), OP.mult)
        for d in range(N):
            iota(A("SB", L * d, L * d + CAP), [[0, CAP]], -8)
            iota(A("WS", L * d, L * d + CAP), [[0, CAP]], 0)
        iota(A("IO"), [[1, 2048]], 1)
        iota(A("R2"), [[0, N * L]], -1)
        mset(A("TW"), 0.0)
        iota(A("TH"), [[1, 4], [0, 64]])
        iota(A("AQ"), [[0, 4], [1, 64]])
        ts(col(9), col(2), 4.0, OP.mult)
        ts(A("TH"), A("TH"), col(9), OP.add)
        dma("s", T.TW[0:128:16, :], T.TH[:], [("TH", 0, 256)], [("TW", 0, Q)])
        dma("s", T.TW[1:128:16, :], T.AQ[:], [("AQ", 0, 256)], [("TW", 0, Q)])
        weights(col(10), col(2), [(2, 127.5), (3, 85.0)])
        ts(A("VT", 0, H), A("NE"), 0.0, OP.mult, col(10), OP.add)
        ts(A("VJ", 0, 128), A("VI"), 6, OP.arith_shift_right)
        ts(A("VJ", 128, 256), A("VI"), 63, OP.bitwise_and)
        cp(A("VH"), A("VJ"))
        dma("s", T.VT[0:128:16, 0:H], T.VH[:, 0:128], [("VH", 0, 128)], [("VT", 0, H)])
        dma("s", T.VT[1:128:16, 0:H], T.VH[:, 128:256], [("VH", 128, 256)], [("VT", 0, H)])
        weights(A("LR"), A("BM"), [(0, 64), (1, 1)])
        ts(A("MX", 256, 384), A("BO"), col(30), OP.mult)
        weights(A("MX", 384, 512), A("BO"), [(2, 64), (3, 1)])
        weights(A("LN"), A("BM"), [(0, 4096), (1, 4096), (4, -8192)])
        weights(A("LU"), A("BM"), [(4, -1)])
        ts(col(11), col(0), 2.0, OP.add)
        ts(col(12), col(2), 2.0, OP.is_lt)
        ts(A("MX", 0, 128), A("IN", 0, 128), col(11), OP.is_equal, col(12), OP.mult)
        ts(col(13), col(0), -2.0, OP.add)
        ts(col(14), col(10), 0.0, OP.is_gt)
        ts(A("MX", 128, 256), A("IN", 0, 128), col(13), OP.is_equal, col(14), OP.mult)
        ts(col(15), col(2), 0.0, OP.is_equal, 1.0 / 8192, OP.mult)
        ts(A("XG", 0, 128), A("NM", 0, 128), 2.5, OP.subtract)
        tt(A("XG", 128, 256), A("XG", 0, 128), A("XG", 0, 128), OP.mult)
        ts(A("XG", 0, 128), A("XG", 128, 256), 1.0, OP.is_gt, 8192.0, OP.mult)
        tt(A("BN", 0, 128), A("XG", 0, 128), A("BO"), OP.mult)
        ts(A("BN", 128, 256), A("BN", 0, 128), -2.0, OP.mult)
        ts(A("THL"), A("BN", 0, 128), col(15), OP.mult, 4096.0, OP.mult)
        ts(A("XG", 0, 128), A("NM", 0, 128), 4.0, OP.is_equal, BIG, OP.mult)
        tt(A("BN", 256, 384), A("XG", 0, 128), A("BO"), OP.mult)
        ts(col(20), col(2), 1.0, OP.add)
        ts(A("KW"), A("BOF"), col(20), OP.mult)

    def index(ps, c, bits, keep, out, lo, hi):
        ts(A("I1", lo, hi), ps, c, OP.subtract)
        if bits == 0:
            ts(A(keep, lo, hi), A("I1", lo, hi), B - 1, OP.bitwise_and)
        else:
            ts(A(keep, lo, hi), A("I1", lo, hi), bits, OP.arith_shift_right, H - 1, OP.bitwise_and)
        cp(A(out, lo, hi), A(keep, lo, hi))

    tags = {}

    nsub = [0]

    def prep(h, x, q, bo, kind):
        pb, lo = "P%d" % (4 + h), HL * h
        if kind == 2 and not JOINT:
            conv(A(pb, 0, 8), "LA", q, lo, 8)
            index(A(pb, 0, 8), col(6), 0, "I6", bo, 8 * h, 8 * h + 8)
        elif kind == 2:
            if h:
                conv(A(pb, 96, 112), "LA", q, 0, 16)
                index(A(pb, 96, 112), col(6), 0, "I6", bo, 0, 16)
        elif h == 0:
            conv(A(pb, 96, 112), "LA", q, 0, 16)
            index(A(pb, 96, 112), col(6), 0, "I6", bo, 0, 16)
            name("columns")
        ntag[0] += 1
        tags[h] = ntag[0]
        if "x" in PIECES[kind][h].lower():
            for k in range(16):
                copy(REP[kind][k], A("XR", k, 16 * HL, 16), A(x, lo, lo + HL), tags[h])
        else:
            mm([(A(pb, 128, 256), A(x, lo, lo + HL), A("ID"), True, True)])
            act(A("XTR", lo, lo + HL), A(pb, 128, 256))
        own = A("P%d" % h, 272, 280)
        mm([(own, A("ID"), A("M1"), True, False)] + [(own, A("LW", 15 - j, 143 - j), A(x, lo + 8 * j, lo + 8 * j + 8), False, j == 15) for j in range(16)])
        copy(STAY, A("AB", Q * h + 31, Q * h + Q, 32), A(x, lo, lo + HL), tags[h])

    def scores(h, table, bo, kind, close):
        ps, lo, c0, c1 = "P%d" % h, HL * h, 8 * h, 8 * h + 8
        if kind == 2 and h == 0:
            cp(A("HS", lo, lo + 64), IX(A(table, 0, B), A(bo, c0, c0 + 4)))
            name("helpers")
            cp(A("HS", lo + 64, lo + HL), IX(A(table, 0, B), A(bo, c0 + 4, c1)))
        elif kind == 1:
            act(A("HO", lo, lo + HL), IX(A("SF", 0, B), A(bo, c0, c1)))
            cp(A("HS", lo, lo + HL), A("HO", lo, lo + HL) if table == "SF" and VIA else IX(A(table, 0, B), A(bo, c0, c1)))
        else:
            cp(A("HS", lo, lo + HL), IX(A(table, 0, B), A(bo, c0, c1)))
        mm([(A(ps, 0, HL), A("ID"), A("KP", 0, HL), True, False)])
        l0 = n = 0
        for e in PIECES[kind][h]:
            l0, n, e = l0 + n, 32 if e.islower() else 16, e.lower()
            off = A("HS", lo + l0, lo + l0 + n)
            line[0] = LINE[kind] and e != "a"
            if e == "x":
                src = A("DD", 16 * l0, 16 * (l0 + n))
                tt(src, IX(A("GN", 0, Q), off), A("XR", 16 * l0, 16 * (l0 + n)), OP.subtract)
                name("x%d" % kind)
            else:
                gg = A("GG", 16 * (lo + l0), 16 * (lo + l0 + n))
                (act if e == "a" else cp)(gg, IX(A("GN", 0, Q), off))
                name("%s%d" % (e, kind))
                line[0] = False
                nsub[0] += 1
                src = A(("P2", "P3")[nsub[0] % 2], 0, 16 * n)
                mm([(src, A("XTR", lo, lo + HL), A("NE", 16 * l0, 16 * (l0 + n)), True, False), (src, A("ID"), gg, False, True)])
            line[0] = LINE[kind] > 1
            act(A("AB", Q * h + 32 * l0, Q * h + 32 * (l0 + n), 2), src, AF.Abs, tag=tags[h])
            line[0] = False
            js = range(l0 // 8, (l0 + n) // 8)
            mm([(A(ps, 0, HL), A("LW", 15 - j, 143 - j), A("AB", Q * h + 256 * j, Q * h + 256 * j + 256, 2), False, close and j == 15) for j in js], True)

    def least(h, ak):
        ps, lo, c0, c1 = "P%d" % h, HL * h, 8 * h, 8 * h + 8
        scan(A("SC", lo, lo + HL), A("RS", 0, HL), A(ps, 0, HL), 0.0, OP.add, OP.min)
        tt(A("I2", c0, c1), A("SC", lo + 15, lo + HL, 16), A(ps, 272, 280), OP.min)
        ts(A(ak, c0, c1), A("I2", c0, c1), 31, OP.bitwise_and)
        tt(A("F1", c0, c1), A(ak, c0, c1), A("BASE", c0, c1), OP.add)

    def take(h, place, xn, qn):
        lo, c0, c1 = HL * h, 8 * h, 8 * h + 8
        cp(A("OFX", c0, c1), A(place, c0, c1))
        name("%s%d" % (xn, h))
        win = IX(A("AB", Q * h, Q * h + Q), A("OFX", c0, c1))
        if TAKE[qn][h] == "v":
            ts(A(qn, lo, lo + HL), win, 0.25, OP.mult, 191.625, OP.add)
        else:
            act(A(qn, lo, lo + HL), win, scale=0.25, bias=191.625)
        act(A(xn, lo, lo + HL), win)

    def mend(h):
        ps, pz, pb, lo, c0, c1 = "P%d" % h, ("P6", "P3")[h], "P%d" % (4 + h), HL * h, 8 * h, 8 * h + 8
        new = IX(A("SF", 0, B), A("BO1", c0, c1))
        mm([(A(pz, 0, HL), A("ID"), A("MB", 256, 256 + HL), True, False)])
        tt(A("CH", lo, lo + HL), new, A("HO", lo, lo + HL), OP.not_equal)
        tt(A("ZC", lo, lo + HL), new, A("CH", lo, lo + HL), OP.mult)
        mm([(A(pz, 0, HL), A("BK", 256, 384), A("CH", lo, lo + HL), False, False)])
        mm([(A(pz, 0, HL), A("BOF"), A("ZC", lo, lo + HL), False, True)])
        name("new z")
        conv(A(pb, 48, 56), "LK", "CH", lo, 8, False)
        name("new k")
        act(A("KT", c0, c1), A(pb, 48, 56))
        act(A("KU", c0, c1), A(pb, 48, 56), bias=-1.0)
        scan(A("SZ", lo, lo + HL), A("RS", 0, HL), A(pz, 0, HL), 0.0, OP.add, OP.min)
        cp(A("ZO", c0, c1), A("SZ", lo + 15, lo + HL, 16))
        tt(A("DN", lo, lo + HL), IX(A("GN"), A("ZO", c0, c1)), A("X0", lo, lo + HL), OP.subtract)
        act(A("AB", Q * h + 29, Q * h + Q, 32), A("DN", lo, lo + HL), AF.Abs, tag=tags[h])
        mm([(A(pb, 56, 64), A("LW", 15 - j, 143 - j), A("AB", Q * h + 256 * j + 29, Q * h + 256 * j + 256, 32), j == 0, j == 15) for j in range(16)])
        tt(A("EK", lo, lo + HL), IX(A("KT", c0, c1), A("EXP", 0, 8)), A("KP", HL, 2 * HL), OP.is_equal)
        mm([(A(ps, 0, HL), A("BK", 384, 512), A("EK", lo, lo + HL), False, True)])
        least(h, "AKA")
        tt(A("F2", c0, c1), A("I2", c0, c1), A("KT", c0, c1), OP.subtract)
        ts(A("F3", c0, c1), A("AKA", c0, c1), -1.0, OP.mult, 29.0, OP.add)
        tt(A("LT", c0, c1), A(pb, 56, 64), A("F2", c0, c1), OP.is_le)
        tt(A("F4", c0, c1), A("LT", c0, c1), A("F3", c0, c1), OP.mult)
        tt(A("F5", c0, c1), A("F4", c0, c1), A("F1", c0, c1), OP.add)
        take(h, "F5", "X1", "QB")

    def query(h):
        ps, lo = "P%d" % h, HL * h
        f = A(ps, 128, 256)
        mm([(f, A("ID"), A("DM"), True, False), (f, A("BC"), A("QC", lo, lo + HL), False, True)])
        ts(A("TF", lo, lo + HL), f, MAGIC, OP.add, MAGIC, OP.subtract)
        tt(A("OW", lo, lo + HL), f, A("TF", lo, lo + HL), OP.is_equal)
        scan(A("CN", lo, lo + HL), A("LOW"), A("OW", lo, lo + HL), A("CN", lo - 1, lo) if h else -1.0, OP.mult, OP.add)
        tt(A("VL", lo, lo + HL), A("OW", lo, lo + HL), A("CN", lo, lo + HL), OP.mult)
        conv(A(ps, 256, 264), "LD", "VL", lo, 8)
        cp(A("OFQ", 8 * h, 8 * h + 8), A(ps, 256, 264))
        cp(IX(A("SB"), A("OFQ", 8 * h, 8 * h + 8)), A("X2", lo, lo + HL))
        name("slots")

    def diagonal(out, ps, src):
        mm([(A(ps, 0, 256), A("ID"), A("MB", 0, 256), True, False), (A(ps, 0, 256), A("BOF"), A(src), False, True)])
        scan(out, A("RS"), A(ps, 0, 256), 0.0, OP.add, OP.min)

    def new_word(s):
        tt(A("I3"), s, A("WN"), OP.mult)
        act(A("F1"), s, scale=37.0)
        ts(A("I4"), A("I3"), 5, OP.arith_shift_right)
        tt(A("F2"), A("F1"), A("WN"), OP.add)
        tt(A("I5"), A("F2"), A("I4"), OP.add)
        ts(A("WN"), A("I5"), Q - 1, OP.bitwise_and)

    def key_columns(ps, off, cc, c16):
        act(A(cc), IX(A("IO"), A(off)))
        cp(A(c16), A(cc))
        mm([(A(ps, 0, 256), A("ID"), A("MB", 256, 512), True, False), (A(ps, 0, 256), A("IDF"), A(cc), False, False)])

    def first_of_key(ps, key, c16, ee, sk, out):
        pos = 0
        for c in range(16):
            lo = 16 * c
            ts(A(ee, pos, pos + 256 - lo), A(c16, lo, 256), A(key, c, c + 1), OP.is_equal)
            mm([(A(ps, lo, lo + 16), A("BK", 128, 256), A(ee, pos, pos + 16), False, c == 15)]
               + ([(A(ps, lo + 16, 256), A("BK", 0, 128), A(ee, pos + 16, pos + 256 - lo), False, False)] if c < 15 else []), True)
            pos += 256 - lo
        scan(A("SK", sk, sk + 256), A("RU"), A(ps, 0, 256), 0.0, OP.max, OP.min)
        ts(A(out), A("SK", sk + 15, sk + 256, 16), -1.0, OP.add)

    def sums(out, weight, table):
        for i in range(4):
            p = A("P2" if i % 2 else "P0")
            mm([(p, weight, A(table, 512 * i, 512 * i + 512), True, True)])
            name("sum")
            act(A(out, 512 * i, 512 * i + 512), p)
            name("summed")

    def owner(t, u):
        hu = plan[0][0] // (N // 2) if u == 0 else rank // (N // 2)
        lo, c0, c1 = HL * hu, 8 * hu, 8 * hu + 8
        rq, pk, pi = A("RQ", L * t + lo, L * t + lo + HL), "P%d" % (6 + u), A("P%d" % (4 + u), 32, 40)
        mm([(A(pk, 0, HL), A("THL"), A("ONE"), True, False)])
        ts(A("QQ", lo, lo + HL), rq, 0.25, OP.mult, 191.625, OP.add)
        name("arrived%d" % u)
        conv(pi, "LC", "QQ", lo, 8)
        act(A("NG", lo, lo + HL), rq, AF.Relu, scale=-1.0)
        mm([(A(pk, 0, HL), A("BN", 0, 128), rq, False, False), (A(pk, 0, HL), A("BN", 256, 384), A("NG", lo, lo + HL), False, False)])
        mm([(A(pk, CAP * i, CAP * i + CAP), A("MX", 0, 128), A("WS", L * (4 * hu + i), L * (4 * hu + i) + CAP), False, False) for i in range(4)])
        index(pi, col(7), 3, "HI", "HOF", c0, c1)
        off = A("HOF", c0, c1)
        tt(A("MQ", lo, lo + HL), IX(A("XT", 0, H), off), rq, OP.max)
        act(A("XG", lo, lo + HL), IX(A("XT", 0, H), off))
        act(A("VG", lo, lo + HL), IX(A("VT", 0, H), off))
        mm([(A(pk, 0, HL), A("BN", 128, 256), A("MQ", lo, lo + HL), False, False), (A(pk, 0, HL), A("BN", 0, 128), A("XG", lo, lo + HL), False, True)])
        tt(A("AW", lo, lo + HL), A(pk, 0, HL), A("VG", lo, lo + HL), OP.min)

    constants()
    ctx[0] = "a"
    for h in range(2):
        prep(h, "X0", "QA", "BO1", 0)

    for t in range(TR):
        last = t == TR - 1
        table = "SF" if t else "SI"
        seen.clear()
        ctx[0] = "a"
        for h in range(2):
            if t:
                mend(h)
                name("mended%d" % h)
                if h:
                    cp(IX(A("XT"), A("OFS")), A("RQ", L * t - L, L * t))
                    name("items")
            else:
                scores(h, table, "BO1", 0, True)
                least(h, "AK1")
                take(h, "F1", "X1", "QB")
            prep(h, "X1", "QB", "BO2", 2)
        if t:
            tt(A("F2"), A("KU"), A("AKA"), OP.subtract)
            tt(A("F3"), A("F2"), A("LT"), OP.mult)
            tt(A("AK1"), A("F3"), A("AKA"), OP.add)
        (act if t else cp)(A("HF"), IX(A(table, 0, B), A("BO1")))
        ctx[0] = "d"
        for h in range(2):
            scores(h, table, "BO2", 2, True)
            least(h, "AK2")
            take(h, "F1", "X2", "QC")
            query(h)
        for i in range(3):
            exchange(2 * t, i)
        act(A("RQ", L * t + CAP * rank, L * t + CAP * rank + CAP), A("SB", L * rank, L * rank + CAP))
        ctx[0] = "b"
        cp(A("A1"), A("AK1"))
        act(A("HG"), IX(A("HF"), A("PERM")))
        tt(A("SEL1"), IX(A("OH"), A("A1")), A("HG"), OP.mult)
        name("select")
        act(A("SELP"), IX(A("SEL1"), A("PERM")))
        diagonal(A("SD", 0, 256), "P6" if WB else "P2", "SELP")
        new_word(A("SD", 15, 256, 16))
        name("word")
        ctx[0] = "c"
        for h in range(2):
            conv(A("P4", 16 + 8 * h, 24 + 8 * h), "LA", "QB", HL * h, 8, False)
        index(A("P4", 16, 32), col(6), 0, "BI", "BP2", 0, 16)
        cp(A("A2"), A("AK2"))
        (act if t else cp)(A("H2"), IX(A(table, 0, B), A("BP2")))
        tt(A("SEL2"), IX(A("OH"), A("A2")), A("H2"), OP.mult)
        diagonal(A("SD", 256, 512), "P3", "SEL2")
        new_word(A("SD", 256 + 15, 512, 16))
        cp(A("WU"), A("WN"))
        act(A("WP"), IX(A("TW"), A("WU")))
        if JUMP == "v":
            jd = "JD"
            tt(A("JD"), IX(A("GN", 0, Q), A("WU")), A("X2"), OP.subtract)
            name("jump")
        else:
            jd = "P2"
            act(A("JD"), IX(A("GN", 0, Q), A("WU")))
            mm([(A("P2", 0, L), A("BK", 512, 640), A("X2"), True, False), (A("P2", 0, L), A("ID"), A("JD"), False, True)])
        cp(IX(A("WS"), A("OFQ")), A("WP"))
        name("words")
        if t:
            cp(IX(A("VT"), A("OFS")), A("RW"))
            name("stored")
        ts(A("B1"), A("BI"), 1.0, OP.add)
        if t == 0:
            cp(A("SF", 0, B), A("SI"))
        tt(A("HM"), IX(A("SF", 0, B), A("BP2")), A("ND", t, t + 256), OP.mult)
        if t:
            conv(A("P4", 64, 80), "LR", "WP", 0, 16, rot=t)
            act(A("WT"), A("P4", 64, 80))
        if last:
            act(A("JA"), A(jd, 0, L), AF.Abs)
            act(A("X0"), A("JA"), scale=-1.0, bias=63.0)
            dma("s", T.yx[:], T.X0[:], [("X0", 0, 256)], [])
            mm([(A("P1", 0, 256), A("MX", 256, 384), A("WP"), True, True)])
            act(A("WC"), A("P1", 0, 256))
            dma("s", T.yw[:], T.WC[0:128:16, :], [("WC", 0, 256)], [])
        else:
            turn("JA", jd, AF.Abs, 1.0, 0.0)
            act(A("QA"), A("JA"), scale=-0.25, bias=207.375)
            act(A("X0"), A("JA"), scale=-1.0, bias=63.0)
            ctx[0] = "g"
            for h in range(2):
                prep(h, "X0", "QA", "BO1", 1)
        ctx[0] = "e"
        owner(t, 0)
        exchange(2 * t + 1, 0)
        owner(t, 1)
        name("answered")
        exchange(2 * t + 1, 1)
        exchange(2 * t + 1, 2)
        if not last:
            for h in range(2):
                scores(h, table, "BO1", 1, False)
        act(A("R2", L * rank, L * rank + CAP), A("AW", CAP * rank, CAP * rank + CAP))
        ctx[0] = "f"
        rq = A("RQ", L * t, L * t + L)
        key_columns("P6", "BP2", "CC", "C16S")
        conv(A("P7", 256, 272), "LU", "AW", 0, 16)
        ts(A("F1"), A("HI"), 1.0, OP.add)
        tt(A("KO"), A("F1"), A("P7", 256, 272), OP.min)
        key_columns("P7", "HOF", "CC2", "C16O")
        first_of_key("P7", "KO", "C16O", "EF", 256, "OFS")
        name("kept")
        if last:
            cp(IX(A("XT"), A("OFS")), rq)
            name("last items")
            dma("s", T.ys[:], T.XT[:, 0:H], [("XT", 0, H)], [])
            sums("YH", A("KW"), "SF")
            sums("YV", A("MX", 256, 384), "VT")
            mm([(A("P3", 0, 256), A("KW"), A("HM"), True, False)])
        else:
            emit("a", A("AQ"), [A("AW"), col(18)], lambda o, i, s: g.scalar.activation(o, i, AF.Sign, bias=0.5, accum_out=s), None, [col(18)])
            ts(A("IP", 3, 4), col(18), 0.5, OP.mult, 128.0, OP.add)
            ts(A("IP", 4, 5), A("IP", 3, 4), 7, OP.bitwise_and)
            ts(col(19), A("IP", 4, 5), 8192.0, OP.mult, 4096.0, OP.add)
            ts(A("THL"), A("BN", 0, 128), col(19), OP.mult, col(15), OP.mult)
            for d in range(N):
                iota(A("SB", L * d, L * d + CAP), [[0, CAP]], -8)
        ctx[0] = "h"
        tt(A("NQ"), IX(A("R2"), A("OFQ")), A("WP"), OP.not_equal)
        name("differs")
        act(A("RG"), IX(A("R2"), A("OFQ")), AF.Relu)
        conv(A("P4", 80, 96), "LN", "NQ", 0, 16)
        conv(A("P5", 80, 96), "LR", "RG", 0, 16, rot=t)
        tt(A("KY"), A("B1"), A("P4", 80, 96), OP.min)
        W = A("WT" if t else "WN")
        tt(A("I3"), A("P5", 80, 96), W, OP.mult)
        tt(A("F2"), A("P5", 80, 96), W, OP.add)
        ts(A("I4"), A("I3"), 5, OP.arith_shift_right)
        tt(A("I5"), A("F2"), A("I4"), OP.add)
        ts(A("ZI"), A("I5"), Q - 1, OP.bitwise_and)
        tt(A("ZD"), IX(A("ZI"), A("EXP")), A("D0", t, t + 256), OP.mult)
        name("z")
        first_of_key("P6", "KY", "C16S", "EE", 0, "OFH")
        mm([(A("P7", L + CAP * s, L + CAP * s + CAP), A("MX", 384, 512) if last else A("MX", 128, 256), A("R2", L * s, L * s + CAP), True, True) for s in range(N)])
        if last:
            mm([(A("P3", 0, 256), A("KW"), A("ZD"), False, True)])
            act(A("YC"), A("P3", 0, 256))
            act(A("WC"), A("P7", L, 2 * L))
            cp(IX(A("YH"), A("OFH")), A("YC"))
            name("yh")
            dma("s", T.yh[:], T.YH[0:128:16, 0:B], [("YH", 0, B)], [])
            cp(IX(A("YV"), A("OFS")), A("WC"))
            name("yv")
            dma("a", T.yv[:], T.YV[0:128:16, 0:H], [("YV", 0, H)], [])
        else:
            tt(IX(A("SF"), A("OFH")), A("ZD"), A("HM"), OP.add)
            act(A("RW"), A("P7", L, 2 * L), bias=col(10))
    issue()
    for s, n in count.items():
        if n:
            g.wait_ge(T.sem[s], n)
